import numpy as np, ml_dtypes
CORES = [40,64,80,88,96,104,120,144]
N = 8
BF = ml_dtypes.bfloat16
def gentries(a):
    return np.ascontiguousarray(a.reshape(8, 16, -1).transpose(0, 2, 1)).reshape(8, -1)
def gtable(e):
    e = np.asarray(e); return np.ascontiguousarray(e.reshape(8, -1, 16).transpose(0, 2, 1)).reshape(128, -1).astype(np.int32)
V, R, L, ST, MF, SL, Q, TH = 2304, 1024, 224, 4, 7, 48, 3, 1295
def pairs(rng):
    a = rng.integers(0, R, (N, 8, L)); b = rng.integers(0, R, (N, 8, L))
    K = np.where(rng.random((N, 8, 1, L)) < 0.5, np.argsort(rng.random((N, 8, 16, L)), axis=2), rng.integers(0, 16, (N, 8, 16, L)))
    return a, b, K, rng.integers(0, 256, (N, 8, 16, L))
def pack(X, P, a, b, K, z, th):
    return {"ph": X.reshape(N, 128, V).astype(np.float32).astype(BF), "rp": np.ascontiguousarray(P.reshape(N, 128, R)).astype(np.int32),
            "av": np.stack([gtable(v) for v in a]), "bv": np.stack([gtable(v) for v in b]), "kc": np.ascontiguousarray(K.reshape(N, 128, L)).astype(np.int32),
            "zs": z.reshape(N, 128, L).astype(np.float32).astype(BF), "th": np.ascontiguousarray(th.reshape(N, 128, 1)).astype(np.int32)}
def camps(rng, M):
    h = V // 2; o = np.argsort(rng.random((N, 8, V)), axis=-1); side = np.zeros((N, 8, V), bool); np.put_along_axis(side, o[..., h:], True, 2)
    X = np.where(side[:, :, None], rng.integers(200, 256, (N, 8, 16, V)), rng.integers(0, 41, (N, 8, 16, V)))
    cl = np.broadcast_to(np.argsort(rng.random((M, 8, R)), axis=-1) & 3, (N, 8, R))
    up = np.argsort(rng.random((N, 8, 16, R)), axis=2) < np.array([0, 16, MF, MF + 1])[cl][:, :, None]
    pk = rng.integers(0, h, (N, 8, 16 * R))
    P = np.where(up, np.take_along_axis(o[..., h:2 * h], pk, 2).reshape(N, 8, 16, R), np.take_along_axis(o[..., :h], pk, 2).reshape(N, 8, 16, R))
    return X, P, np.argsort(cl, axis=-1, kind="stable")
def of(rng, birds, c):
    return np.take_along_axis(birds, c * (R // 4) + rng.integers(0, R // 4, c.shape), 2)
def setup_inputs(rng):
    a, b, K, z = pairs(rng)
    th = TH + 20 * rng.permutation(8)[None, :, None, None] + rng.integers(0, 40, (N, 8, 16, 1))
    return pack(rng.integers(0, 256, (N, 8, 16, V)), rng.integers(0, V, (N, 8, 16, R)), a, b, K, z, th)
def setup_inputs_spread(rng):
    a, b, K, z = pairs(rng)
    X = (np.exp2(8 * rng.random((N, 8, 1, V))) * rng.random((N, 8, 16, V))).astype(np.int64)
    z = (np.exp2(8 * rng.random((N, 8, 1, L))) * rng.random((N, 8, 16, L))).astype(np.int64)
    P = (V * rng.random((N, 8, 16, R)) ** 3).astype(np.int64); P[:, 1::2] = V - 1 - P[:, 1::2]
    a = (R * rng.random((N, 8, L)) ** 2).astype(np.int64); b = R - 1 - (R * rng.random((N, 8, L)) ** 3).astype(np.int64)
    K[:, ::2] = (16 * rng.random((N, 4, 16, L)) ** 2).astype(np.int64)
    th = np.minimum(4064, np.exp2(6 + 5 * rng.random((1, 8, 1, 1)) + rng.random((N, 8, 16, 1))).astype(np.int64))
    return pack(X, P, a, b, K, z, th)
def setup_inputs_ends(rng):
    s = 255 * rng.integers(0, 2, (N, 8, 1))
    kx = rng.integers(0, 3, (N, 8, 1, V)); X = np.where(kx < 2, 255 * kx, 255 * rng.integers(0, 2, (N, 8, 16, V))); X[..., 0] = s; X[..., V - 1] = 255 - s
    kz = rng.integers(0, 3, (N, 8, 1, L)); z = np.where(kz < 2, 255 * kz, 255 * rng.integers(0, 2, (N, 8, 16, L)))
    kp = rng.integers(0, 4, (N, 8, 1, R))
    P = np.where(kp < 2, (V - 1) * kp, np.where(kp == 2, (V - 1) * rng.integers(0, 2, (N, 8, 16, R)), rng.integers(0, V, (N, 8, 16, R))))
    P[..., 0] = (V - 1) * (np.argsort(rng.random((N, 8, 16)), axis=2) < rng.choice(np.array([MF, MF + 1, 3, 9]), (N, 8, 1)))
    P[..., 1] = V - 1; P[..., R - 1] = 0
    a, b = [np.where(rng.random((N, 8, L)) < 0.75, (R - 1) * rng.integers(0, 2, (N, 8, L)), rng.integers(0, R, (N, 8, L))) for i in range(2)]
    K = 15 * rng.integers(0, 2, (N, 8, 16, L)); th = 4064 * rng.integers(0, 2, (N, 8, 16, 1))
    e = np.array([0, 7, L - 1]); a[:, :, e] = R - 1; b[:, :, e] = R - 1; z[:, :, :, e] = (255 - s)[..., None]
    a[:, :, L - 2] = R - 1; b[:, :, L - 2] = 1
    return pack(X, P, a, b, K, z, th)
def setup_inputs_corners(rng):
    X, P, birds = camps(rng, N); a, b, K, z = pairs(rng); sh = int(rng.integers(0, 8))
    least = np.roll(np.array([SL, SL - 1, SL + 1, 0, L, 1, SL, L - 1]), sh); even = np.roll(np.arange(8) == 6, sh)
    C = least + ((L - least + 1) * rng.random((N, 8))).astype(np.int64); C[rng.integers(0, N, 8), np.arange(8)] = least; C = np.where(even, SL, C)
    kd = rng.integers(0, 3, (N, 8, 1)); ln = np.arange(L)
    div = np.argsort(np.argsort(np.where(kd == 0, rng.random((N, 8, L)), np.where(kd == 1, ln, -ln)), axis=-1), axis=-1) < C[..., None]
    s = rng.integers(0, 3, (N, 8, L))
    a = of(rng, birds, np.where(div, np.array([3, 1, 0])[s], np.array([0, 1, 2])[s])); b = of(rng, birds, np.where(div, np.array([0, 0, 1])[s], np.array([0, 1, 0])[s]))
    m = rng.integers(0, 6, (N, 8, 1, L)); row = np.arange(16)[:, None]
    K = np.where(m == 0, row, np.where(m == 1, 0, np.where(m == 2, 15, np.where(m == 3, 15 - row, K))))
    return pack(X, P, a, b, K, z, rng.integers(900, 2501, (N, 8, 16, 1)))
def setup_inputs_crowd(rng):
    X, P, birds = camps(rng, 1); a, b, K, z = pairs(rng); ln = np.arange(L)
    o = rng.permutation(np.array([0, 1, 2, 3, 6, 7])); p = int(rng.choice(np.array([0, 4, 6])))
    md = np.concatenate([o[:p], np.array([5, 4]), o[p:]])[None, :, None]
    two = np.take_along_axis(birds, (rng.integers(0, R // 4, (N, 8, 1)) + np.arange(2)) & (R // 4 - 1), 2)
    other = ((md == 1) & (ln == 0)) | ((md == 2) & (ln == L - 1)); same = (md < 3) | (md == 6)
    b = np.where(same, np.where(other, two[..., 1:], two[..., :1]), np.where(md == 3, np.take_along_axis(two, rng.integers(0, 2, (N, 8, L)), 2), np.where(md == 7, b, of(rng, birds, np.zeros((N, 8, L), np.int64)))))
    lone = ln == rng.integers(0, L, (N, 8, 1))
    high = (md == 4) | ((md == 5) & ~lone) | ((md == 6) & (ln < L // 2)) | ((md == 3) & (rng.random((N, 8, L)) < 0.5))
    a = np.where(md == 7, a, of(rng, birds, high.astype(np.int64)))
    K = np.where(same[:, :, None], rng.integers(0, 16, (N, 8, 1, 1)), K)
    th = np.where(md[:, :, None] < 3, 4064, rng.integers(900, 2501, (N, 8, 16, 1)))
    odd = (np.arange(N) & 1)[:, None, None] == 1; sure = (np.argsort(rng.random((N, 8, 16)), axis=2) < MF + 1)[..., None]
    near = ((md == 4) | ((md == 5) & odd))[:, :, None] & ~sure
    th = np.where(near, 4 * rng.integers(810, 851, (N, 8, 16, 1)) - rng.integers(0, 2, (N, 8, 16, 1)), th)
    return pack(X, P, a, b, K, z, th)
def setup_inputs_ties(rng):
    a, b, K, z = pairs(rng); pal = np.array([0, 60, 120, 120, 120, 120, 180, 180]); row = np.arange(16)[:, None]
    X = rng.choice(pal, (N, 8, 1, V)) + ((rng.random((N, 8, 1, V)) < 0.3) & (row == rng.integers(0, 16, (N, 8, 1, V))))
    z = rng.choice(pal, (N, 8, 1, L)) + ((rng.random((N, 8, 1, L)) < 0.3) & (row == rng.integers(0, 16, (N, 8, 1, L))))
    P = rng.integers(0, V, (N, 8, 16, R)); P[:, 1::2, 8:] = P[:, 1::2, :8]
    b = np.where(rng.random((N, 8, L)) < 0.3, a, b); a[:, :, 0] = 0; b[:, :, 0] = R - 1; a[:, :, L - 1] = R - 1; b[:, :, L - 1] = R - 1
    K = np.where(rng.random((N, 8, 1, L)) < 0.2, row, K); h = L // 2
    for v in (a, b, K, z): v[:, 2::3, ..., h:] = v[:, 2::3, ..., :h]
    th = 960 - rng.integers(-1, 33, (N, 8, 16, 1))
    Y, W, birds = camps(rng, 1); s = np.array([3, 4, 6]); lo = rng.integers(0, 156, (N, 8, 16, 1)); up = rng.integers(40, 100, (N, 8, 16, 1))
    rest = birds[0, 6, R // 4 + R // 128:]; W[:, 6][:, :, rest] = W[:, 6][:, :, birds[0, 6, rng.integers(0, R // 4, len(rest))]]
    cnt = (np.arange(N)[:, None] + rng.integers(0, 4, 3)) & 3; cnt[:, 1] = 1 + (np.arange(N) + int(rng.integers(0, 3))) % 3
    e = np.ones((N, 3), np.int64); e[:, 1] = cnt[:, 1] + rng.integers(0, 2, N); e[:, 2] = rng.integers(1, 4, N)
    hot = np.argsort(rng.random((N, 3, L)), axis=-1) < cnt[..., None]
    warm = np.take_along_axis(birds, R // 4 + rng.integers(0, R // 128, (N, 8, L)), 2); calm = of(rng, birds, np.zeros((N, 8, L), np.int64))
    X[:, s] = (lo + up * (Y[:, :, :1] >= 200))[:, s]; P[:, s] = W[:, s]; z[:, s] = rng.integers(0, 256, (N, 3, 16, L))
    a[:, s] = np.where(hot, warm[:, s], calm[:, s]); b[:, s] = of(rng, birds, np.zeros((N, 8, L), np.int64))[:, s]
    th[:, s] = np.add.reduce(up, axis=2, keepdims=True)[:, s] - e[:, :, None, None]
    return pack(X, P, a, b, K, z, th)
def check_inputs(d):
    bad = []
    for k, lo, hi in (("ph", 0, 255), ("rp", 0, V - 1), ("av", 0, R - 1), ("bv", 0, R - 1), ("kc", 0, 15), ("zs", 0, 255), ("th", 0, 4064)):
        v = np.asarray(d[k]).astype(np.float64)
        if not (np.min(v) >= lo and np.max(v) <= hi): bad.append("range of " + k)
        elif np.any(v != np.floor(v)): bad.append("whole numbers in " + k)
    return bad
def reference(ph, rp, av, bv, kc, zs, th):
    X = ph.astype(np.int32).reshape(N, 8, 16, V); P = rp.astype(np.int64).reshape(N, 8, 16, R); lim = th.astype(np.int64).reshape(N, 8, 16, 1)
    a = np.stack([gentries(v) for v in av]).astype(np.int64); b = np.stack([gentries(v) for v in bv]).astype(np.int64)
    K = kc.astype(np.int64).reshape(N, 8, 16, L); z = zs.astype(np.int32).reshape(N, 8, 16, L); A = np.zeros((N, 8), np.int64)
    wt = (2 * np.arange(16) + 1)[:, None]
    for t in range(ST):
        if t > 0: a, b, K, z = [np.roll(v, 1, axis=0) for v in (a, b, K, z)]
        ra = np.take_along_axis(P, a[:, :, None], 3); rb = np.take_along_axis(P, b[:, :, None], 3)
        x = np.take_along_axis(X, ra.reshape(N, 8, 1, 16 * L), 3).reshape(N, 8, 16, 16, L)
        y = np.take_along_axis(X, rb.reshape(N, 8, 1, 16 * L), 3).reshape(N, 8, 16, 16, L)
        w = np.take_along_axis(y, K[:, :, None], 3)
        d = np.add.reduce(np.abs(x - w), axis=2)
        mis = d > lim + (A & 31)[:, :, None, None]
        div = np.add.reduce(mis.astype(np.int64), axis=2) > MF
        k = np.argmin(np.add.reduce(np.abs(x - z[:, :, :, None]), axis=2), axis=2)
        xk = np.take_along_axis(x, k[:, :, None, None], 3)[:, :, :, 0]; wk = np.take_along_axis(w, k[:, :, None, None], 3)[:, :, :, 0]
        c = np.take_along_axis(rb, np.take_along_axis(K, k[:, :, None], 2), 2)[:, :, 0]
        half = (xk + wk) >> 1
        for h in range(N):
            for g in range(8):
                m = np.flatnonzero(~div[h, g]); col, first = np.unique(c[h, g, m], return_index=True)
                X[h, g][:, col] = half[h, g][:, m[first]]
        zn = np.where(div[:, :, None], (z + x[:, :, :, 0]) >> 1, np.abs(z - wk))
        an = np.where(div, a, (5 * a + np.add.reduce(zn * wt, axis=2)) & (R - 1))
        A = np.add.reduce(div.astype(np.int64), axis=2); n = np.minimum(SL, np.minimum.reduce(A, axis=0))
        bn = np.array(b); Kn = np.array(K)
        for h in range(N):
            q = (h + Q) % N
            for g in range(8):
                me = np.flatnonzero(div[h, g])[:n[g]]; mate = np.flatnonzero(div[q, g])[:n[g]]
                bn[h, g, me] = b[q, g, mate]; own = K[h, g][:, me]
                Kn[h, g][:, me] = np.where(mis[h, g][:, me], np.take_along_axis(K[q, g][:, mate], own, 0), own)
        a, b, K, z = an, bn, Kn, zn
    return {"yx": X.reshape(N, 128, V).astype(np.float32).astype(BF), "yk": K.reshape(N, 128, L).astype(np.float32).astype(BF),
            "ya": np.stack([gtable(v) for v in a]).astype(np.float32), "yb": np.stack([gtable(v) for v in b]).astype(np.float32), "yz": z.reshape(N, 128, L).astype(np.float32).astype(BF)}

@@ -1,0 +1,704 @@
+from concourse.bass import DstId, RemoteDMATransfer
+from concourse.mybir import AluOpType as AL, AxisListType as AX, ActivationFunctionType as AF
+
+N, V, R, L, ST, Q = 8, 2304, 1024, 224, 4, 3
+W = 16 * L
+CH = 4
+CUT = [0, 64, 128, 176, L]
+RELU = []
+WACT = []
+SPLIT = []
+SOFT = [False]
+KW = 320
+MW = 160
+BF, F32, I32, U16, F16 = "bfloat16", "float32", "int32", "uint16", "float16"
+
+_S = {
+    "X": (V + 64, BF), "rpt": (R, I32), "xg": (W, BF), "yg": (W + 768, BF), "dg": (W, BF), "a2": (W, BF),
+    "avi": (16, I32), "bvi": (16, I32), "kci": (L, I32), "thi": (8, I32),
+    "KB": (ST * 2 * KW, BF), "M": (ST * MW, BF), "MP": (ST * 112, BF), "MQ": (ST * 112, BF), "At": (ST * 32, F32),
+    "zs_": (ST * L, BF), "zl": (ST * L, BF), "as_": (ST * L, U16), "al": (ST * L, U16),
+    "ra": (L, U16), "rb": (L, U16), "rbf": (KW, F32), "offf": (KW, F32), "off": (L, U16), "bl": (16, U16),
+    "bl2": (4, U16), "rb2": (48, U16), "rb2f": (48, F32), "kpc": (48, F32), "dlf": (48, F32),
+    "negn": (4, F32), "tL": (4, F32), "Lx": (4, U16), "ko": (48, BF), "gm": (768, BF), "sc": (768, F32), "tk": (48, F32),
+    "dl": (48, F32), "dl2": (48, BF),
+    "ks": (256, F32), "ki": (16, I32), "kt": (32, I32), "ek": (256, BF), "eK": (256, BF), "l1": (16, U16),
+    "prod": (L, F16), "cl": (16, U16), "cf": (16, F32), "kb": (16, F32), "xk": (L, BF), "zz": (2 * L, BF),
+    "hz": (2 * L, I32), "zo": (16, F32), "zp": (16, F32), "zq": (16, U16), "dr": (W, BF), "Zn": (144, BF), "Z2": (144, BF), "af": (16, F32), "a5": (16, F32), "ui": (16, I32), "am": (16, I32), "dm": (16, F32),
+    "mis": (240, BF), "div": (L, BF), "cum": (L, BF), "sg": (3 * L, BF), "S": (4, F32), "Du": (4, U16),
+    "dvl": (16, F32), "t1": (16, F32), "an": (16, F32), "tz": (L, BF), "thf": (4, F32), "thr": (4, F32), "Ai": (4, I32), "Aj": (4, I32),
+    "ab": (896, BF), "ms": (896, BF), "b1": (16, F32), "b2": (16, F32), "b3": (16, F32), "b4": (16, F32), "so": (16, U16), "ybf": (16, F32),
+    "pi": (4, I32), "pj": (8, I32), "col": (8, F32), "ci": (L, F32), "cb": (128, F32), "mc": (768, BF), "r64": (896, BF),
+    "Z": (144, BF), "Zw": (144, BF), "Zh": (144, F16), "BO": (128, BF), "BOh": (128, F16), "B8": (8, BF),
+    "I": (128, BF), "In": (128, BF), "Ih": (128, BF), "Ib": (128, BF), "RM": (16, F32), "E": (16 * 128, BF), "kr": (128, BF),
+    "l16": (L, BF), "lq": (L, BF), "ex": (48, U16), "mT": (256, BF), "r16": (128, BF), "one": (L, BF), "cj": (48, F32),
+    "lc": (16, F32), "l16l": (16, BF), "sb": (4, F32), "jc": (4, F32), "jd": (4, BF), "dmp": (16, F32), "kc0": (16, F32),
+    "bh": (32, I32), "bhb": (32, BF), "bt": (2 * L, BF),
+}
+SCRATCH = {k: ("sbuf", [128, w], d) for k, (w, d) in _S.items()
+           if (RELU or k not in ("Zn", "Z2")) and (RELU or WACT or k != "dr")}
+_P = ["XA", "XB", "T0", "T1", "DD", "M0", "M1", "M2"]
+for _b in _P:
+    SCRATCH[_b] = ("psum", [128, 512], F32)
+_MSG = ["A", "MP", "MQ", "a", "z", "KB"]
+SEMAPHORES = (["cv", "ca", "cp", "cg", "ls"] + ["%s%d" % (m, t) for m in _MSG for t in range(ST)]
+              + ["ld%d" % i for i in range(8)] + ["st%d" % i for i in range(6)])
+
+COST = {"cy": 0.83e-3, "phi": 1.25, "gam": 1.56, "sca": 3.5, "pe": 0.6e-3, "fix": 0.06, "lat": 0.23, "issue": 0.6, "far": 5.5, "dma": 2.0}
+LETTERS = "abcdefghijklmnopqrstuvwxyzABCDEFGHIJKLMNOPQRSTUVWXYZ"
+SHIFT = "HAGwyvLyEEOEGPNACwDHPCHvxFMIDTPLBFBKADDIuDECBBzEAxAArqoMDwCDzAABABBEACODDACEBLCIDDEGFACAOzzGACAABIzKAAIHEGAPAAJDzJGJECrFzAEEBJACGwxxoIuOzyuGLDFGAFSvsTRszGBAvuHFYYYxzGpvDHFJKyovwZZvBCZFuzECPXIvwYEQzFZZCDCzCzKADwrZxHwvyzsEzzMSDBxKEJwxxJDCBEznpxEwItwMwDFFQryvxvGwyCvuAsyykFSBKGFwxDvxAtEBBMLTGCOmXGSyTYvAsLytrvCYKwKCBwsFyGPJQjCLFFQDvtGCFYFFYuQAACIGNzAyFwCLxAIGxABoxJtxCuAyPGCAKZkMXAAvBsCCADEzIEvYJEvzADACCyAEAzADFsAAAALzJICFLBzBAnBzACVAyF"
+ENGINE = "axxaxaaxavxvxaxx"
+ORDER = "acaaaeagaiakaoaqamasaucnaBaHchazaTaRbZaFbTbfcjcrdlbbawdndjclbddpcddVaZeodIbEbAbwbobudZdKdFefdNebdtdPdWeSeqewecesbseyeCeIeUeEbqfaeKeWfcbybKbgfxfDeufgfifmfoeAeYeGeMfefkfqeOfseRfvaDdrfVdHfZfXcLgbfybidQfAfEdSbIbkbCbmbGgefGfJgjbNaJglgqaPendvfPaLcbgtcRdbfKdwfQfMgdggdAdyfSgzcPaVbRgAgngodDgVgGegeigYcZelaXgLbVgPhvhpgTgCgWgEluhxhbbPhrgJhdhzhegNgxhtcthghAhChHhIhKhMdfddcfcxgvcTiIiEiKiOiQiGiAiwikiyiCiWiMiUiSdhiZcpgRiskQhEhihkhmhQjbhPcvjdaNjfinjhhUhWhSiuipjjjljnhYiaicjpbXcVifjqjzjZjDjAjukSkYkUjIjtkbjHknjUjWjElajwkijLcXkpkkjNkrlkkhkdktjTkfkBjOlenelwirkDczkvkHlmlgkxkNmflZlIlCkWlclylOlAlilolqlKlEmglGlQlMlSlUmamcmimlltmmlXmrmxmsmojRcBmBmzcNmDkFmFmGmLmumIkzmNihijmPnxmSmVmQkIkKkPnbnynDnAngncmZnFninKnMnInOnGpupapypepipopkpcmXnlnXnnnZnrnRrWnvnpnTobornVodpgoYpwpqpmpsojntozoeokomoopBrsowosouogcDoMpDoHpFoAoCoEcFpHoPoUoJpJoRpLpNoWoLpPpRpWoTpVqBpSqbqDrrqfqkqPqnqvqwqyqcqMqKrurAqpqgqqrwqTqRqjrGrCrMryqVqtqHqFrdqJrpqXrfrhqZrjrbsBsHrYrEtGrIpYserOsksasqrKrkrmrQrSscsgsmsisssosusCswsIsEsNszrVsOsKcJsZsTtdsUtbtfthsQtitnsWtktptrtstZcHtuuavwvyuctxuftDtItEtBuhuzuttNtKuoukuqumuitPuBtTuTtXyuvWvUvCvEvIvSvMvGvAtRuvuDvKuWwavOuxuFvQvYvauLtzuZuUvjuGuMuOuQwdvouItVxQwfvlwhvrvcvevgwjvtwlvnwnwpwrwtvvwxxdwuwywDwMwEwIwYxPxfwHxSxYxmxowLwPxrxaxUwAyaxlxhxtwRwSyeykxvxjwXxxxDxFwVxzywygyCxWxHymxByIyyyOycxLxJyZyEyKyAAeyGyQzayMzfySyiyoyqzlzcyUzgzmzizryXytzszoxNzxzzzBzFzDzuzGAxzIzLAyzPADAAzQAFzNARAXAOAMAKzSAZAIBbAGBnBoBeBgzZBsBqzVBvzXBwByBSBWBEBIBABKBUBYBMCaBOBQBGAbBCCRAgAlAtAcCdApCAAiCfAnChArBcCjAvBkClATCnCpCrAVCtCDCyCFBiCLCJCHCMCODdCTCVCXCwCuDeCZDbDhDkDi"
+
+
+CHAIN = {
+    "f": {"a": "xg.1 xg.3 a2.1 a2.2 a2.3 a2.4 a2.5 a2.6 a2.7 a2.8 yg.4 dg.2 dg.4 dg.6 dg.8",
+          "v": "ra.1 xg.2 xg.4 yg.1 yg.2 yg.3 dg.1 dg.3 dg.5 dg.7"},
+    "m": {"a": "yg.1 xg.1 a2.1 a2.2 a2.3 a2.4 a2.5 a2.6 a2.7 a2.8 dg.2 dg.4 dg.6 dg.8",
+          "v": "ra.1 xg.2 gm.1 sc.1 sc.2 dg.1 dg.3 dg.5 dg.7"},
+}
+
+
+def _tune(nodes):
+    keys = sorted({n["key"] for n in nodes})
+    flex = dict(zip(sorted({n["key"] for n in nodes if len(n["alt"]) > 1}), ENGINE.replace("x", " ")))
+    return {k: ((LETTERS.index(s) - 26) / 2, flex.get(k, "").strip()) for k, s in zip(keys, SHIFT)}
+
+
+_ORDER = {}
+
+
+def _mask(es):
+    m = 0
+    for e in es:
+        m |= 1 << e
+    return m
+
+
+def _pow2(n):
+    k = 1
+    while 2 * k <= n:
+        k *= 2
+    return k
+
+
+def _deal(topo, src, dsts):
+    on = [d for d in dsts if d in topo.cores_of(src)]
+    out_ = [d for d in dsts if d not in on]
+    used = topo.engines(src, out_[0]) if out_ else []
+    free = [e for e in topo.engines(src, on[0]) if e not in used] if on else []
+    res, i, j = [], 0, 0
+    for d in dsts:
+        if d in on:
+            k = _pow2(len(free) // len(on))
+            res.append(free[i:i + k])
+            i += k
+        else:
+            k = _pow2(len(used) // len(out_))
+            res.append(used[j:j + k])
+            j += k
+    return res
+
+
+def _traffic(T, topo):
+    calls, arrive = {}, {}
+
+    def call(src, msg, t, items):
+        es = _deal(topo, src, [i[2] for i in items])
+        items = [i + (e,) for i, e in zip(items, es)]
+        calls.setdefault(src, []).append((msg, t, items))
+        for i in items:
+            arrive[(i[2], i[3])] = arrive.get((i[2], i[3]), 0) + len(i[4])
+
+    def pair(c, msg, t, items):
+        call(c, msg, t, [(s, d, to if topo.may_write(c, to) else port, sem) for s, d, to, sem, port in items])
+        for s, d, to, sem, port in items:
+            if not topo.may_write(c, to):
+                call(port, msg, t, [(d, d, to, sem)])
+
+    for r, c in enumerate(T.cores):
+        far = [d for d in T.cores if not topo.may_write(c, d)]
+        ports = [x for x in topo.cores_of(c) if x != c and all(topo.may_write(x, d) for d in far)]
+        ports.sort(key=lambda x: topo.die(x) != topo.die(c))
+        near = [d for d in T.cores if d != c and d not in far]
+        fan = {x: [] for x in ports}
+        for i, d in enumerate(far):
+            fan[ports[i % len(ports)]].append(d)
+        for i, d in enumerate(near):
+            fan[ports[-1 - i % len(ports)]].append(d)
+        nx = T.cores[(r + 1) % N]
+        for t in range(ST):
+            last = t == ST - 1
+            if not last:
+                o, p = 2 * KW * t, 2 * KW * (t + 1)
+                pair(c, "KB", t, [(("KB", o, o + L), ("KB", p, p + L), nx, "KB%d" % t, ports[2]),
+                                  (("KB", o + KW, o + KW + L), ("KB", p + KW, p + KW + L), nx, "KB%d" % t, ports[3])])
+            av = ("At", 32 * t + 4 * r, 32 * t + 4 * r + 1)
+            call(c, "A", t, [(av, av, x, "A%d" % t) for x in ports])
+            for x in ports:
+                call(x, "A", t, [(av, av, d, "A%d" % t) for d in fan[x]])
+            if not last:
+                pair(c, "a", t, [(("as_", L * t, L * t + L), ("al", L * t + L, L * t + 2 * L), nx, "a%d" % t, ports[2]),
+                                 (("zs_", L * t, L * t + L), ("zl", L * t + L, L * t + 2 * L), nx, "z%d" % t, ports[3])])
+            mate = T.cores[(r - Q + (0 if last else 1)) % N]
+            items = [(("M", MW * t + 48, MW * t + 160), ("MQ", 112 * t, 112 * t + 112), mate, "MQ%d" % t, ports[1])]
+            if not last:
+                items.append((("M", MW * t, MW * t + 112), ("MP", 112 * t, 112 * t + 112), nx, "MP%d" % t, ports[0]))
+            pair(c, "M", t, items)
+    return calls, arrive
+
+
+def _cost(kind, out, ins, c):
+    def n(v):
+        if v[0] == "ind":
+            return 16 * (v[2][2] - v[2][1])
+        return len(range(v[1], v[2], v[3] if len(v) > 3 else 1))
+
+    def two(v):
+        return v[0] in _S and _S[v[0]][1] in (BF, U16, F16)
+    if kind == "pe":
+        return max(64, n(ins[1])) * c["pe"]
+    if kind == "iota":
+        return 0.13 + 2 * n(out) * c["cy"] * c["phi"]
+    m = max([n(v) for v in ins] + [n(out) if not ins else 0])
+    if out[0] == "ind":
+        return c["fix"] + n(out) * c["sca"] * c["cy"]
+    if any(v[0] == "ind" for v in ins):
+        return c["fix"] + m * c["gam"] * c["cy"]
+    k = 1.0
+    if kind == "half" and all(two(v) for v in [out] + ins):
+        k = 0.5
+    if kind == "tt" and all(v[0] in _S for v in ins):
+        k = 2.0
+    return c["fix"] + max(64, m * k) * c["cy"] * c["phi"]
+
+
+def _times(nd, e, c):
+    k = nd["kind"]
+    if k == "land":
+        return 0.0, c["far"] + {"A": 1.0, "M": 0.8, "K": 1.0}.get(nd["sem"][0], 0.0)
+    if k == "send":
+        return c["issue"], 0.0
+    if k == "dma":
+        return 0.1, c["dma"] + nd["bytes"] / 2.5e3
+    d = sum(_cost(x[1], x[2], x[3], c) for x in nd["alt"][e])
+    return d, d + c["lat"]
+
+
+def _schedule(nodes, c, tune):
+    n = len(nodes)
+    tm = c.get("tm") or [{e: _times(nd, e, c) for e in nd["alt"]} for nd in nodes]
+    kids = [[] for i in range(n)]
+    for i, nd in enumerate(nodes):
+        for d in nd["deps"]:
+            kids[d].append(i)
+    pr = [0.0] * n
+    left = [len(nd["deps"]) for nd in nodes]
+    topo_ = [i for i in range(n) if left[i] == 0]
+    for i in topo_:
+        for k in kids[i]:
+            left[k] -= 1
+            if left[k] == 0:
+                topo_.append(k)
+    for i in topo_[::-1]:
+        pr[i] = min(x[1] for x in tm[i].values()) + max([pr[k] for k in kids[i]] + [0.0])
+    pr = [p + tune.get(nd["key"], (0.0, ""))[0] for p, nd in zip(pr, nodes)]
+    left = [len(nd["deps"]) for nd in nodes]
+    ready = [i for i in range(n) if left[i] == 0]
+    at = [0.0] * n
+    busy, order, end = {}, [], 0.0
+    while ready:
+        i = max(ready, key=lambda j: pr[j])
+        ready.remove(i)
+        best = None
+        for e in (len(tm[i]) > 1 and tune.get(nodes[i]["key"], (0.0, ""))[1] or tm[i]):
+            s, d, b = at[i], tm[i][e][0], busy.setdefault(e, [])
+            k = len(b)
+            while k > 0 and b[k - 1][1] > s:
+                k -= 1
+            while k < len(b) and b[k][0] < s + d:
+                s = max(s, b[k][1])
+                k += 1
+            if best is None or s < best[0]:
+                best = (s, e, k)
+        s, e, k = best
+        if e != "r":
+            busy[e].insert(k, (s, s + tm[i][e][0]))
+        order.append((s, len(order), i, e))
+        end = max(end, s + tm[i][e][1])
+        for k in kids[i]:
+            both = list(tm[k]) == [e] and (e == "p" or i not in nodes[k]["hard"])
+            at[k] = max(at[k], s + (tm[i][e][0] if both else tm[i][e][1]))
+            left[k] -= 1
+            if left[k] == 0:
+                ready.append(k)
+    return [x[2:] for x in sorted(order)], end
+
+
+def rank_program(g, core, T, topo):
+    if "traffic" not in _ORDER:
+        _ORDER["traffic"] = _traffic(T, topo)
+    calls, arrive = _ORDER["traffic"]
+    if core not in calls:
+        return
+    mine = calls[core]
+    rank = T.rank_of(core)
+
+    def ap(v):
+        if v[0] == "ind":
+            return ap(v[1]).indirect(ap(v[2]))
+        if len(v) == 5:
+            return T[v[0]][0:v[4], v[1]:v[2]:v[3]]
+        if len(v) == 4:
+            return T[v[0]][:, v[1]:v[2]:v[3]]
+        return T[v[0]][:, v[1]:v[2]]
+
+    sent = [0]
+
+    def fused(items):
+        trs = []
+        for s, d, to, sem, es in items:
+            rid, pid = topo.addr(to, core)
+            trs.append(RemoteDMATransfer(dst_ids=[DstId(rid=rid, pnc=pid)], dma_engine_mask=_mask(es), remote_sem=T.sem[sem],
+                                         src=ap(s), dst=ap(d)))
+            sent[0] += len(es)
+        g.remote_dma_fused(trs, local_sem=T.sem.ls)
+
+    if rank is None:
+        for msg, t, items in mine:
+            g.wait_ge(T.sem[items[0][3]], arrive[(core, items[0][3])])
+            fused(items)
+        g.wait_ge(T.sem.ls, sent[0])
+        return
+
+    Qs = {"v": g.vector, "a": g.scalar, "p": g.tensor, "g": g, "s": g.sync}
+    nodes, acc, lastsend, seen = [], {}, [], {}
+
+    def node(kind, alt, outs, ins, more=(), **kw):
+        rd, wr = [], []
+        for v in ins:
+            rd += [v[1], v[2]] if v[0] == "ind" else [v]
+        for v in outs:
+            if v[0] == "ind":
+                wr.append(v[1])
+                rd.append(v[2])
+            else:
+                wr.append(v)
+        e = sorted(alt)[0]
+        deps, hard = set(more), set(more)
+        for vs, w in ((rd, False), (wr, True)):
+            for v in vs:
+                for lo, hi, w0, e0, j in acc.get(v[0], []):
+                    if ((w or w0) and lo < v[2] and v[1] < hi) or (v[0] in _P and (e0 != e or e == "p")):
+                        deps.add(j)
+                        if not SOFT[0] or (w0 and not w) or kind != "c" or nodes[j]["kind"] != "c":
+                            hard.add(j)
+        i = len(nodes)
+        for v in wr:
+            acc[v[0]] = [] if v[0] in _P and e == "p" else [a for a in acc.get(v[0], []) if not (len(v) == 3 and v[1] <= a[0] and a[1] <= v[2])]
+        for vs, w in ((rd, False), (wr, True)):
+            for v in vs:
+                acc.setdefault(v[0], []).append((v[1], v[2], w, e, i))
+        name = (wr[0][0] if wr else kind) + "."
+        seen[name] = seen.get(name, 0) + 1
+        nodes.append(dict(kind=kind, alt=alt, deps=sorted(deps), hard=hard, step=seen.get("t", -1), key=seen.get("", "s") + name + str(seen[name]), **kw))
+        return i
+
+    def aps(*xs):
+        return [x for x in xs if isinstance(x, tuple)]
+
+    def val(x):
+        return ap(x) if isinstance(x, tuple) else x
+
+    def vec(fn, kind, out, big, small=()):
+        node("c", {"v": [(fn, kind, out, big)]}, [out], big + aps(*small))
+
+    def cp(out, in_):
+        vec(lambda: g.vector.tensor_copy(ap(out), ap(in_)), "half", out, [in_])
+
+    def tt(out, a, b, o):
+        vec(lambda: g.vector.tensor_tensor(ap(out), ap(a), ap(b), o), "tt", out, [a, b])
+
+    def ts(out, a, s1, o0, s2=None, o1=None):
+        if o1 is None:
+            vec(lambda: g.vector.tensor_scalar(ap(out), ap(a), val(s1), None, o0), "half", out, [a], [s1])
+        else:
+            vec(lambda: g.vector.tensor_scalar(ap(out), ap(a), val(s1), val(s2), o0, o1), "half", out, [a], [s1, s2])
+
+    def scan(out, d0, d1, o0, o1):
+        vec(lambda: g.vector.tensor_tensor_scan(ap(out), ap(d0), ap(d1), 0.0, o0, o1), "half", out, [d0, d1])
+
+    def mset(out, c):
+        vec(lambda: g.vector.memset(ap(out), c), "half", out, [])
+
+    def act(out, in_, f, bias=0.0, scale=1.0, accum=None):
+        if accum is None:
+            fn = lambda: g.scalar.activation(ap(out), ap(in_), f, bias=val(bias), scale=val(scale))
+        else:
+            fn = lambda: g.scalar.activation(ap(out), ap(in_), f, bias=val(bias), scale=val(scale), accum_out=ap(accum))
+        node("c", {"a": [(fn, "one", out, [in_])]}, [out] + aps(accum), [in_] + aps(bias, scale))
+
+    def mov(out, in_):
+        node("c", {"a": [(lambda: g.scalar.activation(ap(out), ap(in_), AF.Copy), "one", out, [in_])],
+                   "v": [(lambda: g.vector.tensor_copy(ap(out), ap(in_)), "half", out, [in_])]}, [out], [in_])
+
+    def mms(ms):
+        def one(m):
+            return (lambda: g.tensor.matmul(ap(m[0]), ap(m[1]), ap(m[2]), m[3], m[4]), "pe", m[0], [m[1], m[2]])
+        node("c", {"p": [one(m) for m in ms]}, [m[0] for m in ms], [m[1] for m in ms] + [m[2] for m in ms])
+
+    def total(out, terms):
+        mms([(out, a, b, i == 0, i == len(terms) - 1) for i, (a, b) in enumerate(terms)])
+
+    def iota(out, pattern, base, cm):
+        if _S[out[0]][1] == I32:
+            fn = lambda: g.iota(ap(out), pattern, base, cm)
+        else:
+            fn = lambda: g.iota(ap(out), pattern, base, cm, allow_small_or_imprecise_dtypes=True)
+        node("c", {"g": [(fn, "iota", out, [])]}, [out], [])
+
+    def size(v):
+        return (v[2] - v[1]) * (4 if _S[v[0]][1] in (F32, I32) else 2)
+
+    def load(e, sem, dst, src, slow=False):
+        if slow:
+            fn = lambda: Qs[e].dma_start(ap(dst), src, allow_slow_non_contiguous=True)
+        else:
+            fn = lambda: Qs[e].dma_start(ap(dst), src)
+        node("dma", {e: fn}, [dst], [], sem=sem, bytes=size(dst))
+
+    def store(e, sem, dst, src):
+        node("dma", {e: lambda: Qs[e].dma_start(dst, ap(src))}, [], [src], sem=sem, bytes=size(src))
+
+    def send(msg, t, lands):
+        items = [i for m, u, i in mine if m == msg and u == t][0]
+        i = node("send", {"g": lambda: fused(items)}, [], [x[0] for x in items], more=lastsend[-1:])
+        lastsend.append(i)
+        for sem, views in lands:
+            node("land", {"r": None}, views, [], more=[i], sem=sem)
+
+    def ind(win, offs):
+        return ("ind", win, offs)
+
+    def to_list(out, zmat, src, o, n=L):
+        total(out, [((zmat, 15 - r, 143 - r), (src, o + r, o + n, 16)) for r in range(16)])
+
+    C = lambda name, i: (name, i, i + 1)
+    I_, In, Ih, Ib, BO = ("I", 0, 128), ("In", 0, 128), ("Ih", 0, 128), ("Ib", 0, 128), ("BO", 0, 128)
+    GP, RR, O15, PP, EV, OD, WT = [C("col", i) for i in range(7)]
+    Xw, RP = ("X", 0, V), ("rpt", 0, R)
+    Em = lambda m: ("E", 128 * m, 128 * m + 128)
+
+    load("s", "ld0", ("avi", 0, 14), T.av[:])
+    load("s", "ld1", RP, T.rp[:])
+    load("s", "ld2", Xw, T.ph[:])
+    load("a", "ld3", ("bvi", 0, 14), T.bv[:])
+    load("a", "ld4", ("kci", 0, L), T.kc[:])
+    load("a", "ld5", ("zl", 0, L), T.zs[:])
+    load("g", "ld6", ("thi", 0, 1), T.th[:], True)
+    iota(("pi", 0, 1), [[0, 1]], 0, 1)
+    iota(("ci", 0, L), [[1, L]], 0, 0)
+    iota(("cb", 0, 128), [[16, 8], [0, 16]], 0, 0)
+    iota(("mc", 0, 768), [[0, 48], [1, 16]], 0, 0)
+    iota(("r64", 0, 896), [[0, 14], [1, 64]], 0, 0)
+    ts(C("pj", 0), C("pi", 0), 112, AL.bitwise_and)
+    ts(C("pj", 1), C("pi", 0), 15, AL.bitwise_and)
+    ts(C("pj", 2), C("pi", 0), 1, AL.bitwise_and)
+    cp(("col", 0, 2), ("pj", 0, 2))
+    cp(PP, C("pi", 0))
+    cp(OD, C("pj", 2))
+    ts(EV, C("pj", 2), -1.0, AL.mult, 1.0, AL.add)
+    ts(O15, C("pj", 1), -16.0, AL.mult, 240.0, AL.add)
+    ts(WT, C("pj", 1), 2.0, AL.mult, 1.0, AL.add)
+    ts(I_, ("ci", 0, 128), PP, AL.is_equal)
+    ts(In, ("ci", 0, 128), PP, AL.is_equal, -1.0, AL.mult)
+    ts(Ih, ("ci", 0, 128), PP, AL.is_equal, 0.5, AL.mult)
+    ts(Ib, ("ci", 0, 128), PP, AL.is_equal, 8192.0, AL.mult)
+    ts(("Z", 0, 144), ("ci", 0, 144), GP, AL.subtract, 15.0, AL.is_equal)
+    ts(BO, ("cb", 0, 128), GP, AL.is_equal)
+    ts(("B8", 0, 8), ("cb", 0, 128, 16), GP, AL.is_equal, 256.0, AL.mult)
+    ts(("RM", 0, 16), ("ci", 0, 16), RR, AL.is_equal)
+    for m in range(16):
+        act(Em(m), BO, AF.Identity, scale=C("RM", m))
+    cp(("Zh", 0, 144), ("Z", 0, 144))
+    cp(("BOh", 0, 128), BO)
+    ts(("Zw", 0, 144), ("Z", 0, 144), WT, AL.mult)
+    ts(("l16", 0, L), ("ci", 0, L), 16.0, AL.mult)
+    ts(("lq", 0, L), ("ci", 0, L), 1.0 / 512, AL.mult)
+    ts(("cj", 0, 48), ("ci", 0, 48), 16.0, AL.mult)
+    cp(("ex", 0, 48), ("ci", 0, 48))
+    ts(("mT", 0, 256), ("mc", 0, 256), RR, AL.is_equal)
+    ts(("r16", 0, 128), ("mc", 0, 128), 0.0, AL.is_equal, float(2 ** 24), AL.mult)
+    ts(("r64", 0, 896), ("r64", 0, 896), 0.0, AL.is_equal, 65536.0, AL.mult)
+    mset(("one", 0, L), 1.0)
+    ts(("kr", 0, 128), ("one", 0, 128), RR, AL.mult, 16.0, AL.mult)
+    mset(("X", V, V + 64), 0.0)
+    mset(("yg", 0, 768), 0.0)
+    mset(("mis", L, 240), 0.0)
+    mset(("M", 0, ST * MW), 0.0)
+    mset(("as_", 0, (ST - 1) * L), 0)
+    for t in range(ST):
+        mset(("KB", 2 * KW * t + L, 2 * KW * t + L + 16), 0.0)
+        mset(("KB", 2 * KW * t + KW + L, 2 * KW * t + KW + L + 16), 0.0)
+    ts(("lc", 0, 14), ("ci", 0, 14), 16.0, AL.mult, RR, AL.add)
+    cp(C("thf", 0), C("thi", 0))
+    cp(C("thr", 0), C("thi", 0))
+    ts(("l16l", 0, 14), ("lc", 0, 14), 16.0, AL.mult)
+    ts(("sb", 0, 3), ("lc", 0, 3), 0.5, AL.add)
+    ts(("jc", 0, 3), ("lc", 0, 3), 1.0, AL.add, 1000.0, AL.mult)
+    ts(("jd", 0, 3), ("lc", 0, 3), 2.0, AL.mult, float(L), AL.add)
+    ts(("kc0", 0, 14), ("lc", 0, 14), -1.0 / 512, AL.mult, 0.25, AL.add)
+    for s in range(0, 14, 4):
+        e = min(s + 4, 14)
+        ts(("dmp", s, e), ("lc", 0, e - s), float(V), AL.add)
+    cp(("al", 0, 14), ("avi", 0, 14))
+    cp(("bl", 0, 14), ("bvi", 0, 14))
+    cp(("KB", 0, L), ("kci", 0, L))
+    ts(("bh", 0, 14), ("bvi", 0, 14), 992, AL.bitwise_and)
+    ts(("bh", 16, 30), ("bvi", 0, 14), 31, AL.bitwise_and)
+    cp(("bhb", 0, 14), ("bh", 0, 14))
+    cp(("bhb", 16, 30), ("bh", 16, 30))
+    mms([(("M0", h * L + r, h * L + L, 16), Em(r), ("bhb", 16 * h, 16 * h + 14), True, True) for h in range(2) for r in range(16)])
+    act(("bt", 0, L), ("M0", 0, L), AF.Identity, scale=EV)
+    act(("bt", L, 2 * L), ("M0", L, 2 * L), AF.Identity, scale=OD)
+    tt(("KB", KW, KW + L), ("bt", 0, L), ("bt", L, 2 * L), AL.add)
+
+    ch = lambda name, c: (name, 16 * CUT[c], 16 * CUT[c + 1])
+    lc = lambda name, c: (name, CUT[c], CUT[c + 1])
+    if RELU:
+        ts(("Zn", 0, 144), ("Z", 0, 144), -1.0, AL.mult)
+        ts(("Z2", 0, 144), ("Z", 0, 144), 2.0, AL.mult)
+    Lx = ("Lx", 0, 3)
+
+    def early(t):
+        ko = 2 * KW * t
+        if t > 0:
+            to_list(("M2", 0, 14), "Z", "KB", ko + KW)
+            ts(("bl", 0, 14), ("M2", 0, 14), 0.125, AL.mult)
+        cp(("rb", 0, L), ind(RP, ("bl", 0, 14)))
+        ts(("rbf", 0, L), ("rb", 0, L), -1152.0, AL.add)
+        total(("M1", 0, L), [(I_, ("l16", 0, L)), (I_, ("KB", ko, ko + L))])
+        act(("offf", 0, L), ("M1", 0, L), AF.Identity, bias=768.0)
+
+    def merge(t, ko, mp, mo, final):
+        qo = 112 * t
+        Kp, mis_ = (mp, mo + 64, mo + 112), (mp, mo + 16, mo + 64)
+        if not final:
+            to_list(("M2", 0, 3), "Z", "MQ", qo + 64, 48)
+            ts(("bl2", 0, 3), ("M2", 0, 3), 0.125, AL.mult)
+            cp(("rb2", 0, 48), ind(RP, ("bl2", 0, 3)))
+            mov(("yg", 0, 768), ind(Xw, ("rb2", 0, 48)))
+            ts(("rb2f", 0, 48), ("rb2", 0, 48), -1152.0, AL.add)
+            tt(("kpc", 0, 48), Kp, ("cj", 0, 48), AL.add)
+        act(("ko", 0, 48), ("MQ", qo + 16, qo + 64), AF.Identity, bias=O15)
+        act(("tk", 0, 48), Kp, AF.Identity, bias=-240.0, scale=15.0)
+        node("c", {"v": [(lambda: g.vector.tensor_reduce(ap(C("negn", 0)), ap(("At", 32 * t, 32 * t + 32, 4)), AX.X, AL.min, negate=True),
+                          "one", C("negn", 0), [C("negn", 0)])]}, [C("negn", 0)], [("At", 32 * t, 32 * t + 32)])
+        ts(("tL", 0, 3), ("jc", 0, 3), C("negn", 0), AL.add)
+        for s in range(3):
+            ts(C("Lx", s), C("tL", s), C("jd", s), AL.min, C(mp, mo + s), AL.max)
+        mms([(("DD", m, 512, 16), Em(m), ("ko", 0, 32), True, True) for m in range(16)])
+        mms([(("M0", m, 256, 16), Em(m), ("ko", 32, 48), True, True) for m in range(16)])
+        tt(("gm", 0, 768), ind(Kp, ("ex", 0, 48)), ("mc", 0, 768), AL.is_lt)
+        scan(("sc", 0, 512), ("gm", 0, 512), ("DD", 0, 512), AL.mult, AL.max)
+        scan(("sc", 512, 768), ("gm", 512, 768), ("M0", 0, 256), AL.mult, AL.max)
+        tt(("dl", 0, 48), ("sc", 15, 768, 16), ("tk", 0, 48), AL.add)
+        tt(("dl2", 0, 48), ("dl", 0, 48), mis_, AL.mult)
+        tt(ind(("KB", ko, ko + KW), Lx), Kp, ("dl2", 0, 48), AL.add)
+        cp(ind(("KB", ko + KW, ko + 2 * KW), Lx), ("MQ", qo + 64, qo + 112))
+        if final:
+            to_list(("M2", 0, 14), "Z", "KB", ko + KW)
+            ts(("ybf", 0, 14), ("M2", 0, 14), 0.125, AL.mult)
+            store("s", "st0", T.yb[:], ("ybf", 0, 14))
+            store("a", "st5", T.yk[:], ("KB", ko, ko + L))
+        else:
+            tt(("dlf", 0, 48), ("dl", 0, 48), mis_, AL.mult)
+            tt(ind(("offf", 0, KW), Lx), ("dlf", 0, 48), ("kpc", 0, 48), AL.add)
+            cp(ind(("rbf", 0, KW), Lx), ("rb2f", 0, 48))
+
+    early(0)
+    for t in range(ST):
+        last = t == ST - 1
+        seen.clear()
+        seen[""], seen["t"] = "f" if t == 0 else "m", t
+        ko, mo, p = 2 * KW * t, MW * t, 2 * KW * (t + 1)
+        K_, z_, a_ = ("KB", ko, ko + L), ("zl", L * t, L * t + L), ("al", L * t, L * t + 14)
+        for c in range(CH):
+            mov(("yg", 768 + 16 * CUT[c], 768 + 16 * CUT[c + 1]), ind(Xw, lc("rb", c)))
+        cp(("ra", 0, L), ind(RP, a_))
+        for c in range(CH):
+            mov(ch("xg", c), ind(Xw, lc("ra", c)))
+        if t > 0:
+            merge(t - 1, ko, "MP", 112 * (t - 1), False)
+        cp(("off", 0, L), ("offf", 0, L))
+        if not last:
+            send("KB", t, [("KB%d" % t, [("KB", p, p + L), ("KB", p + KW, p + KW + L)])])
+        cp(("af", 0, 14), a_)
+        ts(("a5", 0, 14), a_, 5.0, AL.mult)
+
+        for h, (l0, n) in enumerate(((0, 128), (128, L - 128))):
+            Th = "T%d" % h
+            mms([((Th, 0, 128), ("kr", 0, 128), I_, True, False)])
+            for i in range(4):
+                bank, o = ("XA", "XB", "M1")[(4 * h + i) % 3], 16 * l0 + 4 * n * i
+                mms([((bank, n * j, n * j + n), a, b, s, not s) for j in range(4)
+                     for a, b, s in ((I_, ("xg", 16 * l0 + 4 * i + j, 16 * (l0 + n), 16), True), (In, ("zl", L * t + l0, L * t + l0 + n), False))])
+                act(("a2", o, o + 4 * n), (bank, 0, 4 * n), AF.Abs)
+                if i == 3:
+                    mms([((Th, 0, 128, 1, n), ("KB", ko + l0, ko + l0 + n), I_, False, False)])
+                mms([((Th, 4 * i + j, 128, 16, n), ("a2", o + n * j, o + n * j + n), ("B8", 0, 8), False, i == 3 and j == 3 and n == 128)
+                     for j in range(4)] + ([((Th, 0, 128, 16), I_, ("M", 4, 12), False, True)] if i == 3 and n < 128 else []))
+            scan(("ks", 128 * h, 128 * h + 128), ("r16", 0, 128), (Th, 0, 128), AL.max, AL.min)
+        for c in range(CH):
+            rows = lambda z, b: [((z, 15 - k, 143 - k), (b, 16 * CUT[c] + k, 16 * CUT[c + 1], 16)) for k in range(16)]
+            yw, mid = ("yg", 0, 768 + 16 * CUT[c + 1]), (CUT[c] + CUT[c + 1]) // 2
+            if c in WACT:
+                act(ch("dr", c), ind(yw, lc("off", c)), AF.Copy)
+                for bank, p0, p1 in (("XA", CUT[c], mid), ("XB", mid, CUT[c + 1])):
+                    total((bank, 0, 16 * (p1 - p0)), [(I_, ("dr", 16 * p0, 16 * p1)), (In, ("xg", 16 * p0, 16 * p1))])
+                    act(("dg", 16 * p0, 16 * p1), (bank, 0, 16 * (p1 - p0)), AF.Abs)
+                total(lc("DD", c), rows("Z", "dg"))
+                continue
+            for p0, p1 in ((CUT[c], mid), (mid, CUT[c + 1])) if c in SPLIT else ((CUT[c], CUT[c + 1]),):
+                tt(("dg", 16 * p0, 16 * p1), ind(yw, ("off", p0, p1)), ("xg", 16 * p0, 16 * p1), AL.subtract)
+            if c in RELU:
+                ts(ch("dr", c), ch("dg", c), 0.0, AL.max)
+                total(lc("DD", c), rows("Zn", "dg") + rows("Z2", "dr"))
+            else:
+                act(ch("dg", c), ch("dg", c), AF.Abs)
+                total(lc("DD", c), rows("Z", "dg"))
+        cp(("ki", 0, 16), ("ks", 15, 256, 16))
+        ts(("kt", 0, 16), ("ki", 0, 16), 4, AL.logical_shift_right, 15, AL.bitwise_and)
+        ts(("kt", 16, 32), ("ki", 0, 16), 15, AL.bitwise_and)
+        cp(("eK", 0, 256), ind(("kt", 16, 32), ("ex", 0, 16)))
+        tt(("ek", 0, 256), ind(("kt", 0, 16), ("ex", 0, 16)), ("mT", 0, 256), AL.mult)
+        mms([(("T0", 0, 128), ("eK", 0, 128), I_, True, True), (("T0", 128, L), ("eK", 128, 256), ("I", 0, 96), True, True)])
+        mms([(("T1", 0, 14), I_, ("l16l", 0, 14), True, False), (("T1", 0, 8), ("ek", 0, 128), ("BO", 0, 128, 16), False, False),
+             (("T1", 8, 14), ("ek", 128, 256), ("BO", 0, 96, 16), False, True)])
+        ts(("T0", 256, 256 + L), ("T0", 0, L), RR, AL.is_equal)
+        tt(("prod", 0, L), ("T0", 256, 256 + L), ("rbf", 0, L), AL.mult)
+        cp(("l1", 0, 14), ("T1", 0, 14))
+        mov(("xk", 0, L), ind(("xg", 0, W), ("l1", 0, 14)))
+        to_list(("M2", 0, 14), "Zh", "prod", 0)
+        ts(("cl", 0, 14), ("M2", 0, 14), 1152.0, AL.add)
+        ts(("cf", 0, 14), ("M2", 0, 14), 1152.0, AL.add)
+        tt(("kb", 0, 14), ("kc0", 0, 14), ("M2", 0, 14), AL.subtract)
+        tt(("tz", 0, L), ind(Xw, ("cl", 0, 14)), z_, AL.subtract)
+        act(("zz", 0, L), ("tz", 0, L), AF.Abs)
+        total(("M0", L, 2 * L), [(Ih, z_), (Ih, ("xg", 0, W, 16))])
+        total(("M0", 0, L), [(Ih, ("xk", 0, L)), (Ih, ("tz", 0, L)), (Ih, z_)])
+        to_list(("T1", 0, 14), "Zw", "zz", 0)
+        ts(("hz", 0, 2 * L), ("M0", 0, 2 * L), -0.25, AL.add)
+        tt(("ui", 0, 14), ("T1", 0, 14), ("a5", 0, 14), AL.add)
+        cp(("zz", L, 2 * L), ("hz", L, 2 * L))
+        ts(("am", 0, 14), ("ui", 0, 14), R - 1, AL.bitwise_and)
+        tt(("b2", 0, 14), ("dmp", 0, 14), ("cf", 0, 14), AL.subtract)
+        tt(("dm", 0, 14), ("af", 0, 14), ("am", 0, 14), AL.subtract)
+
+        ts(("mis", 0, L), ("DD", 0, L), C("thr", 0), AL.is_gt)
+        total(("XA", 0, L), [(BO, ("mis", 0, L))])
+        to_list(("XB", 0, 14), "Z", "mis", 0)
+        ts(("div", 0, L), ("XA", 0, L), 7.5, AL.is_gt)
+        scan(("cum", 0, L), ("one", 0, L), ("div", 0, L), AL.mult, AL.add)
+        total(("T0", 0, L), [(("BOh", 0, 128), ("prod", 0, L)), (I_, ("lq", 0, L)), (Ib, ("div", 0, L))])
+        act(C("At", 32 * t + 4 * rank), C("cum", L - 1), AF.Identity, scale=1000.0)
+        for s in range(3):
+            act(("sg", L * s, L * s + L), ("cum", 0, L), AF.Sign, bias=C("sb", s), scale=-1.0, accum=C("S", s))
+        ts(("dvl", 0, 14), ("XB", 0, 14), 7.5, AL.is_gt)
+        tt(("t1", 0, 14), ("dvl", 0, 14), ("dm", 0, 14), AL.mult)
+        tt(("an", 0, 14), ("t1", 0, 14), ("am", 0, 14), AL.add)
+        ts(("zo", 0, 14), ("XB", 0, 14), 7.5, AL.is_gt, float(L), AL.mult)
+        tt(("zp", 0, 14), ("zo", 0, 14), ("lc", 0, 14), AL.add)
+        cp(("zq", 0, 14), ("zp", 0, 14))
+        mov(("zs_", L * t, L * t + L), ind(("zz", 0, 2 * L), ("zq", 0, 14)))
+        send("A", t, [("A%d" % t, [C("At", 32 * t + 4 * r) for r in range(N) if r != rank])])
+        if last:
+            store("s", "st1", T.ya[:], ("an", 0, 14))
+            store("s", "st2", T.yz[:], ("zs_", L * t, L * t + L))
+        else:
+            cp(("as_", L * t, L * t + 14), ("an", 0, 14))
+            send("a", t, [("a%d" % t, [("al", L * t + L, L * t + 2 * L)]), ("z%d" % t, [("zl", L * t + L, L * t + 2 * L)])])
+        ts(("Du", 0, 3), ("S", 0, 3), 0.5, AL.mult, 112.0, AL.add)
+        act(("M", mo, mo + 3), ("S", 0, 3), AF.Identity, bias=112.0, scale=0.5)
+        mov(("M", mo + 64, mo + 112), ind(("KB", ko, ko + 240), ("Du", 0, 3)))
+        mov(("M", mo + 16, mo + 64), ind(("mis", 0, 240), ("Du", 0, 3)))
+        mov(("M", mo + 112, mo + 160), ind(("KB", ko + KW, ko + KW + 240), ("Du", 0, 3)))
+        send("M", t, [("MQ%d" % t, [("MQ", 112 * t, 112 * t + 112)])] + ([] if last else [("MP%d" % t, [("MP", 112 * t, 112 * t + 112)])]))
+        if not last:
+            cp(C("Ai", 0), C("cum", L - 1))
+            ts(C("Aj", 0), C("Ai", 0), 31, AL.bitwise_and)
+            tt(C("thr", 0), C("Aj", 0), C("thf", 0), AL.add)
+            early(t + 1)
+
+        for s in range(14):
+            w0 = min(64 * (s // 4), L - 64)
+            act(("ab", 64 * s, 64 * s + 64), ("T0", w0, w0 + 64), AF.Abs, bias=C("kb", s))
+        scan(("ms", 0, 896), ("r64", 0, 896), ("ab", 0, 896), AL.max, AL.min)
+        ts(("b1", 0, 14), ("ms", 63, 896, 64), 0.25, AL.not_equal)
+        tt(("b3", 0, 14), ("b1", 0, 14), ("b2", 0, 14), AL.mult)
+        tt(("b4", 0, 14), ("b3", 0, 14), ("cf", 0, 14), AL.add)
+        cp(("so", 0, 14), ("b4", 0, 14))
+        for s in (12, 8, 4, 0):
+            e = min(s + 4, 14)
+            cp(ind(("X", 0, V + 64), ("so", s, e)), ("hz", 16 * s, 16 * e))
+        if last:
+            store("s", "st3", T.yx[:, 0:V // 2], ("X", 0, V // 2))
+            store("a", "st4", T.yx[:, V // 2:V], ("X", V // 2, V))
+            merge(t, ko, "M", mo, True)
+
+    for t in range(0 if ORDER else ST):
+        byk = {nd["key"][1:]: i for i, nd in enumerate(nodes) if nd["step"] == t}
+        for e, names in CHAIN["f" if t == 0 else "m"].items():
+            row = [byk[x] for x in names.split()]
+            for i, j in zip([None] + row, row):
+                nodes[j]["alt"] = {e: nodes[j]["alt"][e]}
+                if i is not None:
+                    nodes[j]["deps"] = sorted(set(nodes[j]["deps"]) | {i})
+    if ORDER and "order" not in _ORDER:
+        code_ = [52 * LETTERS.index(ORDER[i]) + LETTERS.index(ORDER[i + 1]) for i in range(0, len(ORDER), 2)]
+        _ORDER["order"] = [(x // 2, "av"[x % 2] if len(nodes[x // 2]["alt"]) > 1 else list(nodes[x // 2]["alt"])[0]) for x in code_]
+        _ORDER["nodes"] = nodes
+    if "order" not in _ORDER:
+        _ORDER["order"] = _schedule(nodes, COST, _tune(nodes))[0]
+        _ORDER["nodes"] = nodes
+    cnt = {"v": 0, "a": 0, "p": 0, "g": 0}
+    know = {e: {} for e in Qs}
+    token, clock, queue, owed = {}, {}, {}, {}
+
+    def wait(e, tok):
+        if know[e].get(tok[0], 0) < tok[1]:
+            Qs[e].wait_ge(T.sem[tok[0]], tok[1])
+            for k, n in clock[tok].items():
+                know[e][k] = max(know[e].get(k, 0), n)
+
+    for i, e in _ORDER["order"]:
+        nd = nodes[i]
+        queue[i] = e
+        if nd["kind"] == "land":
+            tok = (nd["sem"], arrive[(core, nd["sem"])])
+            clock[tok] = {tok[0]: tok[1]}
+        else:
+            need = {}
+            for d in nd["deps"]:
+                if d in token and not (e == queue[d] and (e == "p" or d not in nd["hard"])):
+                    need[token[d][0]] = max(need.get(token[d][0], 0), token[d][1])
+            for tok in sorted(need.items(), key=lambda x: -sum(clock[x].values())):
+                wait(e, tok)
+            if nd["kind"] == "send":
+                nd["alt"][e]()
+                continue
+            if nd["kind"] == "dma":
+                nd["alt"][e]().then_inc(T.sem[nd["sem"]], 16)
+                tok = (nd["sem"], 16)
+            else:
+                for x in nd["alt"][e]:
+                    x[0]().then_inc(T.sem["c" + e], 1)
+                    cnt[e] += 1
+                tok = ("c" + e, cnt[e])
+            clock[tok] = dict(know[e])
+            clock[tok][tok[0]] = tok[1]
+        token[i] = tok
+        owed[tok[0]] = tok[1]
+    g.wait_ge(T.sem.ls, sent[0])
+    for tok in owed.items():
+        wait("g", tok)

@@ -3,69 +3,73 @@ from concourse.mybir import AluOpType as AL, AxisListType as AX, ActivationFunct
 
 N, V, R, L, ST, Q = 8, 2304, 1024, 224, 4, 3
 W = 16 * L
-CH = 4
 CUT = [0, 64, 128, 176, L]
-RELU = []
-WACT = []
-SPLIT = []
-SOFT = [False]
+CH = len(CUT) - 1
 KW = 320
-MW = 160
+MW = 196
+MS = 100
+BIG = 4096.0
+SHIFT = 2.0 ** 17
+LN32 = 3.4657359027997265
+MAGIC = 1.5 * 2 ** 28
 BF, F32, I32, U16, F16 = "bfloat16", "float32", "int32", "uint16", "float16"
 
 _S = {
-    "X": (V + 64, BF), "rpt": (R, I32), "xg": (W, BF), "yg": (W + 768, BF), "dg": (W, BF), "a2": (W, BF),
+    "X": (V + 64, BF), "rpt": (R, I32), "rpm": (R, F32), "xg": (W, BF), "yg": (W + 768, BF), "dg": (W, BF), "dr": (W, BF), "a2": (W, BF),
     "avi": (16, I32), "bvi": (16, I32), "kci": (L, I32), "thi": (8, I32),
     "KB": (ST * 2 * KW, BF), "M": (ST * MW, BF), "MP": (ST * 112, BF), "MQ": (ST * 112, BF), "At": (ST * 32, F32),
-    "zs_": (ST * L, BF), "zl": (ST * L, BF), "as_": (ST * L, U16), "al": (ST * L, U16),
-    "ra": (L, U16), "rb": (L, U16), "rbf": (KW, F32), "offf": (KW, F32), "off": (L, U16), "bl": (16, U16),
-    "bl2": (4, U16), "rb2": (48, U16), "rb2f": (48, F32), "kpc": (48, F32), "dlf": (48, F32),
-    "negn": (4, F32), "tL": (4, F32), "Lx": (4, U16), "ko": (48, BF), "gm": (768, BF), "sc": (768, F32), "tk": (48, F32),
-    "dl": (48, F32), "dl2": (48, BF),
-    "ks": (256, F32), "ki": (16, I32), "kt": (32, I32), "ek": (256, BF), "eK": (256, BF), "l1": (16, U16),
-    "prod": (L, F16), "cl": (16, U16), "cf": (16, F32), "kb": (16, F32), "xk": (L, BF), "zz": (2 * L, BF),
-    "hz": (2 * L, I32), "zo": (16, F32), "zp": (16, F32), "zq": (16, U16), "dr": (W, BF), "Zn": (144, BF), "Z2": (144, BF), "af": (16, F32), "a5": (16, F32), "ui": (16, I32), "am": (16, I32), "dm": (16, F32),
-    "mis": (240, BF), "div": (L, BF), "cum": (L, BF), "sg": (3 * L, BF), "S": (4, F32), "Du": (4, U16),
-    "dvl": (16, F32), "t1": (16, F32), "an": (16, F32), "tz": (L, BF), "thf": (4, F32), "thr": (4, F32), "Ai": (4, I32), "Aj": (4, I32),
-    "ab": (896, BF), "ms": (896, BF), "b1": (16, F32), "b2": (16, F32), "b3": (16, F32), "b4": (16, F32), "so": (16, U16), "ybf": (16, F32),
-    "pi": (4, I32), "pj": (8, I32), "col": (8, F32), "ci": (L, F32), "cb": (128, F32), "mc": (768, BF), "r64": (896, BF),
-    "Z": (144, BF), "Zw": (144, BF), "Zh": (144, F16), "BO": (128, BF), "BOh": (128, F16), "B8": (8, BF),
-    "I": (128, BF), "In": (128, BF), "Ih": (128, BF), "Ib": (128, BF), "RM": (16, F32), "E": (16 * 128, BF), "kr": (128, BF),
-    "l16": (L, BF), "lq": (L, BF), "ex": (48, U16), "mT": (256, BF), "r16": (128, BF), "one": (L, BF), "cj": (48, F32),
-    "lc": (16, F32), "l16l": (16, BF), "sb": (4, F32), "jc": (4, F32), "jd": (4, BF), "dmp": (16, F32), "kc0": (16, F32),
-    "bh": (32, I32), "bhb": (32, BF), "bt": (2 * L, BF),
+    "zs_": (ST * L, BF), "zl": (ST * L, BF), "fa": (56 + L, F32), "al": (ST * 112, F32), "ub": (56 + L, U16), "bll": (ST * L, U16),
+    "au": (16, U16), "ra": (L, U16), "rb": (L, U16), "offf": (KW, F32), "off": (L, U16),
+    "bl2": (4, U16), "rb2": (48, U16), "negn": (4, F32), "tL": (4, F32), "Lx": (4, U16),
+    "G": (48, BF), "sW": (192, F32), "tW": (48, I32), "aW": (48, I32), "kn": (48, F32),
+    "ks": (256, F32), "ki": (16, I32), "kt": (32, I32), "ktb": (16, BF), "ek": (256, BF), "eK": (256, BF), "l1": (16, U16),
+    "eq": (L, BF), "prod": (L, F16), "cl": (16, U16), "kb": (16, F32), "xk": (L, BF), "zz": (L, BF), "tz": (L, BF),
+    "hz": (L, I32), "h0": (L, I32), "ui": (16, I32), "am": (16, I32), "dm": (16, F32), "dvl": (16, F32), "t1": (16, F32),
+    "fit": (240, BF), "div": (L, BF), "cum": (L, BF), "sg": (3 * L, BF), "S": (4, F32), "Du": (4, U16),
+    "thf": (4, F32), "thr": (4, F32), "q": (4, F32), "nm": (4, F32),
+    "ab": (896, BF), "ms": (896, F32), "Ib": (128, BF), "Zq": (144, BF), "b3": (16, F32), "b4": (16, F32), "so": (16, U16), "ybf": (16, F32),
+    "pi": (4, I32), "pj": (4, I32), "col": (8, F32), "cb": (128, F32), "mc": (256, BF), "r64": (448, BF),
+    "Z": (144, BF), "Zn": (144, BF), "Zw": (144, BF), "Zh": (144, F16), "BO": (128, BF), "BOh": (128, F16), "B8": (24, BF), "rbf": (KW, F32), "rb2f": (48, F32), "c16": (16, F16), "Ig": (128, F16), "lose": (16, F32), "msb": (896, BF), "r6b": (896, BF),
+    "I": (128, BF), "In": (128, BF), "Ih": (128, BF), "I5": (128, F32), "Sw": (128, BF), "kr": (128, BF),
+    "l16": (L, BF), "lq": (L, BF), "mT": (256, BF), "r16": (128, BF), "one": (L, BF), "cj": (48, F32),
+    "lc": (16, F32), "l16l": (16, BF), "sb": (4, F32), "jc": (4, F32), "jd": (4, BF), "dmp": (32, F32), "kc0": (16, F32),
+    "c11": (32, BF), "zr": (8, BF), "p32": (4, BF), "wq": (4, F32), "Wq": (512, BF), "Dq": (512, BF), "cq": (192, BF), "rq": (192, BF),
+    "bh": (32, I32), "bt": (2 * L, BF),
 }
-SCRATCH = {k: ("sbuf", [128, w], d) for k, (w, d) in _S.items()
-           if (RELU or k not in ("Zn", "Z2")) and (RELU or WACT or k != "dr")}
-_P = ["XA", "XB", "T0", "T1", "DD", "M0", "M1", "M2"]
+for _b in ("ktb", "eq", "bll", "nm", "thf", "negn"):
+    del _S[_b]
+SCRATCH = {k: ("sbuf", [128, w], d) for k, (w, d) in _S.items()}
+_P = ["A0", "A1", "A2", "T0", "T1", "DD", "H", "M2"]
 for _b in _P:
     SCRATCH[_b] = ("psum", [128, 512], F32)
 _MSG = ["A", "MP", "MQ", "a", "z", "KB"]
 SEMAPHORES = (["cv", "ca", "cp", "cg", "ls"] + ["%s%d" % (m, t) for m in _MSG for t in range(ST)]
               + ["ld%d" % i for i in range(8)] + ["st%d" % i for i in range(6)])
 
-COST = {"cy": 0.83e-3, "phi": 1.25, "gam": 1.56, "sca": 3.5, "pe": 0.6e-3, "fix": 0.06, "lat": 0.23, "issue": 0.6, "far": 5.5, "dma": 2.0}
-LETTERS = "abcdefghijklmnopqrstuvwxyzABCDEFGHIJKLMNOPQRSTUVWXYZ"
-SHIFT = "HAGwyvLyEEOEGPNACwDHPCHvxFMIDTPLBFBKADDIuDECBBzEAxAArqoMDwCDzAABABBEACODDACEBLCIDDEGFACAOzzGACAABIzKAAIHEGAPAAJDzJGJECrFzAEEBJACGwxxoIuOzyuGLDFGAFSvsTRszGBAvuHFYYYxzGpvDHFJKyovwZZvBCZFuzECPXIvwYEQzFZZCDCzCzKADwrZxHwvyzsEzzMSDBxKEJwxxJDCBEznpxEwItwMwDFFQryvxvGwyCvuAsyykFSBKGFwxDvxAtEBBMLTGCOmXGSyTYvAsLytrvCYKwKCBwsFyGPJQjCLFFQDvtGCFYFFYuQAACIGNzAyFwCLxAIGxABoxJtxCuAyPGCAKZkMXAAvBsCCADEzIEvYJEvzADACCyAEAzADFsAAAALzJICFLBzBAnBzACVAyF"
-ENGINE = "axxaxaaxavxvxaxx"
-ORDER = "acaaaeagaiakaoaqamasaucnaBaHchazaTaRbZaFbTbfcjcrdlbbawdndjclbddpcddVaZeodIbEbAbwbobudZdKdFefdNebdtdPdWeSeqewecesbseyeCeIeUeEbqfaeKeWfcbybKbgfxfDeufgfifmfoeAeYeGeMfefkfqeOfseRfvaDdrfVdHfZfXcLgbfybidQfAfEdSbIbkbCbmbGgefGfJgjbNaJglgqaPendvfPaLcbgtcRdbfKdwfQfMgdggdAdyfSgzcPaVbRgAgngodDgVgGegeigYcZelaXgLbVgPhvhpgTgCgWgEluhxhbbPhrgJhdhzhegNgxhtcthghAhChHhIhKhMdfddcfcxgvcTiIiEiKiOiQiGiAiwikiyiCiWiMiUiSdhiZcpgRiskQhEhihkhmhQjbhPcvjdaNjfinjhhUhWhSiuipjjjljnhYiaicjpbXcVifjqjzjZjDjAjukSkYkUjIjtkbjHknjUjWjElajwkijLcXkpkkjNkrlkkhkdktjTkfkBjOlenelwirkDczkvkHlmlgkxkNmflZlIlCkWlclylOlAlilolqlKlEmglGlQlMlSlUmamcmimlltmmlXmrmxmsmojRcBmBmzcNmDkFmFmGmLmumIkzmNihijmPnxmSmVmQkIkKkPnbnynDnAngncmZnFninKnMnInOnGpupapypepipopkpcmXnlnXnnnZnrnRrWnvnpnTobornVodpgoYpwpqpmpsojntozoeokomoopBrsowosouogcDoMpDoHpFoAoCoEcFpHoPoUoJpJoRpLpNoWoLpPpRpWoTpVqBpSqbqDrrqfqkqPqnqvqwqyqcqMqKrurAqpqgqqrwqTqRqjrGrCrMryqVqtqHqFrdqJrpqXrfrhqZrjrbsBsHrYrEtGrIpYserOsksasqrKrkrmrQrSscsgsmsisssosusCswsIsEsNszrVsOsKcJsZsTtdsUtbtfthsQtitnsWtktptrtstZcHtuuavwvyuctxuftDtItEtBuhuzuttNtKuoukuqumuitPuBtTuTtXyuvWvUvCvEvIvSvMvGvAtRuvuDvKuWwavOuxuFvQvYvauLtzuZuUvjuGuMuOuQwdvouItVxQwfvlwhvrvcvevgwjvtwlvnwnwpwrwtvvwxxdwuwywDwMwEwIwYxPxfwHxSxYxmxowLwPxrxaxUwAyaxlxhxtwRwSyeykxvxjwXxxxDxFwVxzywygyCxWxHymxByIyyyOycxLxJyZyEyKyAAeyGyQzayMzfySyiyoyqzlzcyUzgzmzizryXytzszoxNzxzzzBzFzDzuzGAxzIzLAyzPADAAzQAFzNARAXAOAMAKzSAZAIBbAGBnBoBeBgzZBsBqzVBvzXBwByBSBWBEBIBABKBUBYBMCaBOBQBGAbBCCRAgAlAtAcCdApCAAiCfAnChArBcCjAvBkClATCnCpCrAVCtCDCyCFBiCLCJCHCMCODdCTCVCXCwCuDeCZDbDhDkDi"
-
-
-CHAIN = {
-    "f": {"a": "xg.1 xg.3 a2.1 a2.2 a2.3 a2.4 a2.5 a2.6 a2.7 a2.8 yg.4 dg.2 dg.4 dg.6 dg.8",
-          "v": "ra.1 xg.2 xg.4 yg.1 yg.2 yg.3 dg.1 dg.3 dg.5 dg.7"},
-    "m": {"a": "yg.1 xg.1 a2.1 a2.2 a2.3 a2.4 a2.5 a2.6 a2.7 a2.8 dg.2 dg.4 dg.6 dg.8",
-          "v": "ra.1 xg.2 gm.1 sc.1 sc.2 dg.1 dg.3 dg.5 dg.7"},
-}
-
-
-def _tune(nodes):
-    keys = sorted({n["key"] for n in nodes})
-    flex = dict(zip(sorted({n["key"] for n in nodes if len(n["alt"]) > 1}), ENGINE.replace("x", " ")))
-    return {k: ((LETTERS.index(s) - 26) / 2, flex.get(k, "").strip()) for k, s in zip(keys, SHIFT)}
-
-
-_ORDER = {}
+ROUND = (0, 1, 1, 2)
+RELU = [[], [], []]
+WACT = [[], [], []]
+VMAX = [[], [], []]
+LATE = [1, 1, 1]
+OPT = {"E1": 1, "WK": 0, "C16": 1}
+SENDS = ["KB", "A", "M", "a"]
+ORDER = [{'v': 'ex pj2 pj1 SW pj0 col pj3 WT cq0 Sw I rq au bh af cq1 kr bo bl BO r64 Z mT bt0 r16 bt1 ra rb BOh K0 RQ x1 x0 off y1 d0 Zh y2 d1 thr d2 cq2 ks0 d3 ks1 rpm ki sb kt1 r65 wq eK fit0 jc fit1 thf prod div0 div1 Ig kt0 cum ek c16 cl kb tz Ih Wq0 Du At l1 cq3 Zw Wq3 Dq2 keep +bl Km h0 +rb ms1 ui ms0 am zn dm Dq0 dvl b3 t1 b4 an so hz X4 X3 X2 nm rq0 X1', 'a': 'ld5 ld3 lc ld4 p32 lq B9 B8 b0 In y0 y3 x2 x3 a1 a2 a0 a4 a5 kc0 a3 a7 r0 a6 r1 r2 r3 Zn l16l Wq1 rbf r6b I5 Zq sg1 sg2 sg0 ab8 ab6 ab11 ab3 ab10 zz ab4 Dm Kp ab1 ab9 ab12 ab2 ab5 ab7 ab13 ab0 bm xk Ib Dq1 B10 lose Dq3 dmp +rbf Wq2 +offf q thn jd', 'p': 'pb0 poff ps2 ps1 ps0 ps4 ps5 ps3 ps7 ps6 pT4 pT0 pT1 pT2 pT3 pK0 pT5 pD0 pT6 pT7 pK1 pD1 pD2 pD3 pk pn0 pn1 pc pcr +pbl pl pc2 pH pu pP pdl ph +poff', 'g': 'ci pi S0 PP KB0 cb one mc cj c12 l16 zr ld6 fitz sendKB c11 X0 dm0 sendA sendM senda'}, {'v': 'y1 negn sW tL tW Lx1 aW Lx0 bl2 kn Lx2 rb2 sO au ra x0 ym x3 off rb2f d3 sK d0 d1 d2 ks1 ks0 ki sR sB kt1 kt0 fit1 eK ek fit0 prod div1 div0 cum c16 cl l1 kb tz Du At Kp Dm q keep bm Km dvl ms1 ms0 h0 b3 ui b4 am so dm hz t1 zn an X4 nm X3 +bl X2 +rb X1', 'a': 'y3 G y2 y0 x1 x2 a0 a1 a2 a3 a4 r3 a6 a5 a7 r0 r1 r2 sg0 sg2 sg1 ab0 ab8 ab10 ab12 ab11 ab9 zz ab5 ab2 ab13 ab7 ab6 ab4 ab1 ab3 xk lose +rbf thn +offf', 'p': 'pW0 pW1 pb2 ps0 ps1 ps2 ps3 ps4 pT0 ps6 ps5 ps7 pT4 pT1 pT2 pT5 pT6 pT3 pT7 pK0 pK1 pD3 pD0 pD1 pD2 pk pn1 pn0 pl pc pcr pc2 pdl pH pu ph pP +pbl +poff', 'g': 'sendKB sendA sendM senda'}, {'v': 'y1 y3 bl2 negn rb2 sW tL Lx0 Lx2 au tW ra aW x0 kn Lx1 sO x2 off d0 d1 d3 d2 sK rb2f ks0 sR fit1 fit0 div1 ks1 div0 ki cum kt1 eK h0 sB prod Du Kp keep Dm Km kb cl kt0 ek c16 tz l1 ms1 ms0 dvl lose b3 b4 hz so X4 zn X3 +negn ui +tL am X2 +Lx2 +Lx0 +Lx1 X1 +sB dm +sW t1 +tW an +aW +kn +sK', 'a': 'y0 y2 G ym x1 x3 a0 a2 a1 a3 a5 r0 a4 r1 r3 r2 a6 a7 At sg2 sg1 sg0 bm ab9 ab7 ab12 ab3 ab4 ab5 ab11 ab13 ab10 ab1 ab6 ab8 ab2 ab0 xk zz +G st4 +ybf +st5', 'p': 'pW0 pb2 pW1 ps0 ps2 ps1 ps3 ps5 ps4 pT0 ps6 pT1 pT2 pD0 pT3 ps7 pT4 pT5 pD1 pK0 pD3 pD2 pT6 pn1 pT7 pK1 pn0 pH pk pc pcr +pW0 pl pc2 pdl ph pP pu +pW1 +pbl', 'g': 'sendA sendM'}]
+_old2 = [{'v': 'pj2 rq pj3 r64 SW pj0 Sw I Dq2 pj1 col bh ex bo mT bt0 bt1 r16 BO bl au Z WT kr ra K0 rb x1 x0 off y3 Zh y2 d0 d1 Dq0 d3 dmp ks0 r3 d2 rq0 ks1 thr ki cq0 kt1 kt0 fit1 ktb ek rpm eq fit0 prod div0 div1 BOh cum thf RQ Zq r65 cl l1 wq kb cq1 tz Du Wq2 af At +rb Kp bm cq2 Km dvl Ib Wq1 ui am Dm dm h0 t1 keep an ms1 zn ms0 hz b3 b4 cq3 so X4 X3 X2 X1 nm thn', 'a': 'ld5 ld3 In lc ld4 l16l Dq1 Zn jd B8 b0 y1 x2 y0 x3 a1 a0 a2 a4 a3 lq a5 r0 sb a7 a6 r1 r2 jc eK I5 Ih Dq3 p32 sg2 kc0 sg1 sg0 Zw zz Wq3 ab10 ab13 ab8 ab2 ab11 Wq0 ab9 ab3 ab5 ab7 ab12 ab1 ab0 ab4 ab6 xk q +offf', 'p': 'pb0 poff ps1 ps2 ps0 ps4 ps3 ps5 pT4 pT0 pT1 pT2 pT3 ps6 ps7 pK0 pT5 pE3 pD0 pT6 pT7 pK1 pD3 pD1 pD2 pk pn0 pn1 pl pc pcr pc2 pdl pu pH pa1 pv1 pP pa0 pv0 ph +poff', 'g': 'pi PP ci mc KB0 cb ld6 l16 one X0 zr dm0 c11 fitz c12 cj S0 sendKB sendA senda sendM'}, {'v': 'negn y1 au tL ra Lx0 x0 Lx1 bl2 sW tW Lx2 aW sB kn rb2 sO ym off bl sK d0 d2 d1 ks0 ks1 ki kt1 ktb kt0 eK ek eq prod d3 l1 kb cl r3 fit0 tz fit1 div0 div1 cum +rb ui am h0 dm Du nm zn dvl Km t1 keep an ms0 ms1 b3 hz b4 so X4 thn X3 X2 X1', 'a': 'y0 y2 G x1 x3 x2 a1 a0 a2 a4 a3 a5 a7 a6 r0 r1 y3 r2 ab12 ab5 ab10 ab4 zz ab0 ab6 ab8 ab3 ab9 ab2 ab13 ab7 ab1 ab11 At sg2 sg1 sg0 q Kp xk bm Dm +offf', 'p': 'pW0 pW1 pb2 ps1 ps0 ps2 pbl ps4 ps3 pT0 ps5 ps7 ps6 pT1 pT2 pT3 pK0 pT4 pT5 pT6 pT7 pK1 pD0 pk pl pD1 pcr pc pD2 pE3 pD3 pn0 pc2 pn1 pu pH pP pdl pa0 pv0 pa1 pv1 ph +poff', 'g': 'sendKB sendA senda sendM'}, {'v': 'y1 au negn ra tL x1 sW bl2 Lx0 rb2 Lx2 tW Lx1 aW x2 kn sB sO ym off sK d1 d0 d3 ks0 ks1 ki kt1 ktb d2 r3 kt0 eq bl prod fit1 ek fit0 div1 l1 div0 cum At cl kb tz Du Kp bm keep h0 hz ms1 dvl ms0 Km b3 b4 ui so X4 am X3 dm X2 +negn +tL X1 +Lx1 +Lx2 +Lx0 t1 +sB +sW an +tW +aW +kn zn +sK', 'a': 'y3 y0 G x0 x3 a1 a0 a2 a4 a3 a5 y2 a7 a6 r0 r1 eK r2 xk sg1 sg0 sg2 ab9 ab6 ab12 ab11 ab7 ab0 ab8 ab10 ab13 ab5 ab3 ab1 ab4 ab2 Dm zz +G st4 +ybf +st5', 'p': 'pb2 pW0 pW1 ps0 ps1 ps2 ps4 ps3 ps5 pT0 pT1 ps7 pT2 pT4 pT5 ps6 pT3 pbl pK0 pT6 pT7 pK1 pD0 pE3 pD1 pk pD3 pD2 pn1 pcr pl pn0 pc pH pc2 pdl ph pa1 pv1 pa0 pv0 pu +pW0 pP +pW1 +pbl', 'g': 'sendA sendM'}]
+_old1 = [
+    {"v": "cq0 cq1 pj2 pj1 pj0 col BO r64 BOh Z I au ex bl SW mT WT bh bo rq bt1 Sw K0 bt0 ra rpm rb Ih x1 y1 off kr kc0 y3 r16 cq2 d1 thr af d0 d3 r65 r3 cq3 Dq0 d2 ks0 ks1 ki rq0 Zh kt0 kt1 sb ktb fit1 jd eK ek eq jc prod pj3 fit0 l1 thf xk cl Dq1 tz div1 kb div0 cum At RQ wq +rb ui Wq3 q am dm dvl nm t1 h0 an zn Du ms0 ms1 Km b3 keep b4 hz so X4 X3 X2 Wq1 X1 Wq2",
+     "a": "ld4 ld3 lq B8 lc l16l Zn In ld5 b0 x0 y0 x2 a1 x3 a2 a0 y2 a4 a3 a5 a7 a6 r0 r1 Dq2 r2 I5 Ib p32 Dq3 Zq Zw zz ab7 ab2 ab13 ab9 ab10 ab3 ab8 ab4 ab0 ab6 ab1 ab12 dmp ab11 ab5 sg0 sg1 sg2 bm Dm Kp Wq0 +offf thn",
+     "p": "pb0 ps1 poff ps0 ps2 ps5 ps4 pT0 ps3 ps7 ps6 pT1 pT2 pT3 pT4 pT5 pK0 pT6 pT7 pK1 pE3 pD3 pD0 pD1 pk pn1 pD2 pl pc pn0 pcr pu pdl pH pP pa0 pv0 pa1 pv1 ph +poff",
+     "g": "pi PP cb fitz ci mc l16 KB0 X0 sendKB ld6 S0 one c11 zr c12 dm0 sendA cj senda sendM"},
+    {"v": "negn y2 au tL ra x0 sW Lx1 tW Lx2 aW Lx0 bl2 kn rb2 sO y1 sB off ym sK d0 d1 ks1 ks0 ki kt1 bl kt0 ktb d2 eq prod d3 kb cl r3 fit0 ek tz fit1 l1 div0 div1 cum At +rb ui am dm dvl t1 Du h0 an zn Km keep ms1 ms0 b3 nm hz b4 so X4 X3 X2 X1",
+     "a": "y0 x1 G x2 x3 a1 a0 a2 a4 a3 a5 a7 a6 r0 r1 eK y3 r2 ab6 ab1 ab10 ab5 ab9 ab4 ab13 ab8 ab7 ab2 zz ab11 sg2 ab12 sg1 sg0 ab0 ab3 Kp xk Dm bm q thn +offf",
+     "p": "pW0 pW1 pb2 ps1 ps2 ps0 ps4 ps3 pT0 ps5 ps7 ps6 pT4 pT1 pT2 pT5 pT6 pT7 pT3 pK1 pK0 pbl pD0 pk pD1 pc pcr pD2 pE3 pD3 pl pn0 pn1 pu pdl pH pP pa1 pv1 pa0 pv0 ph +poff",
+     "g": "sendKB sendA senda sendM"},
+    {"v": "negn y3 au tL ra Lx1 y0 bl2 Lx0 Lx2 sW tW rb2 aW x3 sB kn ym sO off sK d0 d3 bl r3 d1 d2 ks0 fit1 ks1 ki kt1 ktb fit0 div1 eq div0 prod cum At kt0 ek kb cl Du Kp bm keep Km tz l1 h0 dvl ms1 ms0 b3 b4 hz so X4 X3 ui X2 +negn X1 +tL am +Lx0 +Lx1 +Lx2 dm +sB +sW t1 +tW an +aW zn +kn +sK",
+     "a": "y1 G x0 x1 x2 a2 a0 a1 y2 a3 a4 a5 r0 a7 a6 r1 r2 eK sg1 sg2 sg0 ab13 ab12 ab7 ab3 ab9 ab11 ab6 ab10 ab8 ab2 ab4 ab1 ab0 +G ab5 xk zz Dm st4 +ybf +st5",
+     "p": "pb2 pW0 pW1 ps2 ps0 ps1 ps3 ps4 ps5 pT0 pbl ps6 pT1 ps7 pE3 pD3 pT4 pT2 pT3 pK0 pD0 pT5 pT6 pT7 pK1 pn1 pD1 pD2 pk pn0 pc pcr pH pdl pl pa1 pv1 pa0 pv0 ph pu pP +pW0 +pW1 +pbl",
+     "g": "sendA sendM"},
+]
+_C = {}
 
 
 def _mask(es):
@@ -129,116 +133,33 @@ def _traffic(T, topo):
         nx = T.cores[(r + 1) % N]
         for t in range(ST):
             last = t == ST - 1
-            if not last:
-                o, p = 2 * KW * t, 2 * KW * (t + 1)
-                pair(c, "KB", t, [(("KB", o, o + L), ("KB", p, p + L), nx, "KB%d" % t, ports[2]),
-                                  (("KB", o + KW, o + KW + L), ("KB", p + KW, p + KW + L), nx, "KB%d" % t, ports[3])])
-            av = ("At", 32 * t + 4 * r, 32 * t + 4 * r + 1)
-            call(c, "A", t, [(av, av, x, "A%d" % t) for x in ports])
-            for x in ports:
-                call(x, "A", t, [(av, av, d, "A%d" % t) for d in fan[x]])
-            if not last:
-                pair(c, "a", t, [(("as_", L * t, L * t + L), ("al", L * t + L, L * t + 2 * L), nx, "a%d" % t, ports[2]),
-                                 (("zs_", L * t, L * t + L), ("zl", L * t + L, L * t + 2 * L), nx, "z%d" % t, ports[3])])
-            mate = T.cores[(r - Q + (0 if last else 1)) % N]
-            items = [(("M", MW * t + 48, MW * t + 160), ("MQ", 112 * t, 112 * t + 112), mate, "MQ%d" % t, ports[1])]
-            if not last:
-                items.append((("M", MW * t, MW * t + 112), ("MP", 112 * t, 112 * t + 112), nx, "MP%d" % t, ports[0]))
-            pair(c, "M", t, items)
+            for msg in SENDS:
+                if msg == "KB" and not last:
+                    o, p, u = 2 * KW * t, 2 * KW * (t + 1), 14 * (ST - 1 - t)
+                    pair(c, "KB", t, [(("KB", o, o + L), ("KB", p, p + L), nx, "KB%d" % t, ports[2]),
+                                      (("KB", o + KW, o + KW + L), ("KB", p + KW, p + KW + L), nx, "KB%d" % t, ports[3])])
+                if msg == "A":
+                    av = ("At", 32 * t + 4 * r, 32 * t + 4 * r + 1)
+                    call(c, "A", t, [(av, av, x, "A%d" % t) for x in ports])
+                    for x in ports:
+                        call(x, "A", t, [(av, av, d, "A%d" % t) for d in fan[x]])
+                if msg == "a" and not last:
+                    u = 14 * (ST - 1 - t)
+                    pair(c, "a", t, [(("fa", u, u + 112), ("al", 112 * t + 112, 112 * t + 224), nx, "a%d" % t, ports[2]),
+                                     (("zs_", L * t, L * t + L), ("zl", L * t + L, L * t + 2 * L), nx, "z%d" % t, ports[3])])
+                if msg == "M":
+                    mate = T.cores[(r - Q + (0 if last else 1)) % N]
+                    items = [(("M", MW * t + 96, MW * t + 96 + MS), ("MQ", 112 * t, 112 * t + MS), mate, "MQ%d" % t, ports[1])]
+                    if not last:
+                        items.append((("M", MW * t, MW * t + MS), ("MP", 112 * t, 112 * t + MS), nx, "MP%d" % t, ports[0]))
+                    pair(c, "M", t, items)
     return calls, arrive
 
 
-def _cost(kind, out, ins, c):
-    def n(v):
-        if v[0] == "ind":
-            return 16 * (v[2][2] - v[2][1])
-        return len(range(v[1], v[2], v[3] if len(v) > 3 else 1))
-
-    def two(v):
-        return v[0] in _S and _S[v[0]][1] in (BF, U16, F16)
-    if kind == "pe":
-        return max(64, n(ins[1])) * c["pe"]
-    if kind == "iota":
-        return 0.13 + 2 * n(out) * c["cy"] * c["phi"]
-    m = max([n(v) for v in ins] + [n(out) if not ins else 0])
-    if out[0] == "ind":
-        return c["fix"] + n(out) * c["sca"] * c["cy"]
-    if any(v[0] == "ind" for v in ins):
-        return c["fix"] + m * c["gam"] * c["cy"]
-    k = 1.0
-    if kind == "half" and all(two(v) for v in [out] + ins):
-        k = 0.5
-    if kind == "tt" and all(v[0] in _S for v in ins):
-        k = 2.0
-    return c["fix"] + max(64, m * k) * c["cy"] * c["phi"]
-
-
-def _times(nd, e, c):
-    k = nd["kind"]
-    if k == "land":
-        return 0.0, c["far"] + {"A": 1.0, "M": 0.8, "K": 1.0}.get(nd["sem"][0], 0.0)
-    if k == "send":
-        return c["issue"], 0.0
-    if k == "dma":
-        return 0.1, c["dma"] + nd["bytes"] / 2.5e3
-    d = sum(_cost(x[1], x[2], x[3], c) for x in nd["alt"][e])
-    return d, d + c["lat"]
-
-
-def _schedule(nodes, c, tune):
-    n = len(nodes)
-    tm = c.get("tm") or [{e: _times(nd, e, c) for e in nd["alt"]} for nd in nodes]
-    kids = [[] for i in range(n)]
-    for i, nd in enumerate(nodes):
-        for d in nd["deps"]:
-            kids[d].append(i)
-    pr = [0.0] * n
-    left = [len(nd["deps"]) for nd in nodes]
-    topo_ = [i for i in range(n) if left[i] == 0]
-    for i in topo_:
-        for k in kids[i]:
-            left[k] -= 1
-            if left[k] == 0:
-                topo_.append(k)
-    for i in topo_[::-1]:
-        pr[i] = min(x[1] for x in tm[i].values()) + max([pr[k] for k in kids[i]] + [0.0])
-    pr = [p + tune.get(nd["key"], (0.0, ""))[0] for p, nd in zip(pr, nodes)]
-    left = [len(nd["deps"]) for nd in nodes]
-    ready = [i for i in range(n) if left[i] == 0]
-    at = [0.0] * n
-    busy, order, end = {}, [], 0.0
-    while ready:
-        i = max(ready, key=lambda j: pr[j])
-        ready.remove(i)
-        best = None
-        for e in (len(tm[i]) > 1 and tune.get(nodes[i]["key"], (0.0, ""))[1] or tm[i]):
-            s, d, b = at[i], tm[i][e][0], busy.setdefault(e, [])
-            k = len(b)
-            while k > 0 and b[k - 1][1] > s:
-                k -= 1
-            while k < len(b) and b[k][0] < s + d:
-                s = max(s, b[k][1])
-                k += 1
-            if best is None or s < best[0]:
-                best = (s, e, k)
-        s, e, k = best
-        if e != "r":
-            busy[e].insert(k, (s, s + tm[i][e][0]))
-        order.append((s, len(order), i, e))
-        end = max(end, s + tm[i][e][1])
-        for k in kids[i]:
-            both = list(tm[k]) == [e] and (e == "p" or i not in nodes[k]["hard"])
-            at[k] = max(at[k], s + (tm[i][e][0] if both else tm[i][e][1]))
-            left[k] -= 1
-            if left[k] == 0:
-                ready.append(k)
-    return [x[2:] for x in sorted(order)], end
-
-
 def rank_program(g, core, T, topo):
-    if "traffic" not in _ORDER:
-        _ORDER["traffic"] = _traffic(T, topo)
-    calls, arrive = _ORDER["traffic"]
+    if "traffic" not in _C:
+        _C["traffic"] = _traffic(T, topo)
+    calls, arrive = _C["traffic"]
     if core not in calls:
         return
     mine = calls[core]
@@ -272,9 +193,9 @@ def rank_program(g, core, T, topo):
         return
 
     Qs = {"v": g.vector, "a": g.scalar, "p": g.tensor, "g": g, "s": g.sync}
-    nodes, acc, lastsend, seen = [], {}, [], {}
+    nodes, acc, rnd = [], {}, [0]
 
-    def node(kind, alt, outs, ins, more=(), **kw):
+    def node(name, kind, alt, outs, ins, more=(), **kw):
         rd, wr = [], []
         for v in ins:
             rd += [v[1], v[2]] if v[0] == "ind" else [v]
@@ -284,24 +205,20 @@ def rank_program(g, core, T, topo):
                 rd.append(v[2])
             else:
                 wr.append(v)
-        e = sorted(alt)[0]
-        deps, hard = set(more), set(more)
+        e = list(alt)[0]
+        deps = set(more)
         for vs, w in ((rd, False), (wr, True)):
             for v in vs:
                 for lo, hi, w0, e0, j in acc.get(v[0], []):
                     if ((w or w0) and lo < v[2] and v[1] < hi) or (v[0] in _P and (e0 != e or e == "p")):
                         deps.add(j)
-                        if not SOFT[0] or (w0 and not w) or kind != "c" or nodes[j]["kind"] != "c":
-                            hard.add(j)
         i = len(nodes)
         for v in wr:
             acc[v[0]] = [] if v[0] in _P and e == "p" else [a for a in acc.get(v[0], []) if not (len(v) == 3 and v[1] <= a[0] and a[1] <= v[2])]
         for vs, w in ((rd, False), (wr, True)):
             for v in vs:
                 acc.setdefault(v[0], []).append((v[1], v[2], w, e, i))
-        name = (wr[0][0] if wr else kind) + "."
-        seen[name] = seen.get(name, 0) + 1
-        nodes.append(dict(kind=kind, alt=alt, deps=sorted(deps), hard=hard, step=seen.get("t", -1), key=seen.get("", "s") + name + str(seen[name]), **kw))
+        nodes.append(dict(kind=kind, alt=alt, deps=sorted(deps), key=(rnd[0], name), **kw))
         return i
 
     def aps(*xs):
@@ -310,84 +227,90 @@ def rank_program(g, core, T, topo):
     def val(x):
         return ap(x) if isinstance(x, tuple) else x
 
-    def vec(fn, kind, out, big, small=()):
-        node("c", {"v": [(fn, kind, out, big)]}, [out], big + aps(*small))
+    def vec(name, fn, out, big, small=()):
+        node(name, "c", {"v": [fn]}, [out], big + aps(*small))
 
-    def cp(out, in_):
-        vec(lambda: g.vector.tensor_copy(ap(out), ap(in_)), "half", out, [in_])
+    def cp(name, out, in_):
+        vec(name, lambda: g.vector.tensor_copy(ap(out), ap(in_)), out, [in_])
 
-    def tt(out, a, b, o):
-        vec(lambda: g.vector.tensor_tensor(ap(out), ap(a), ap(b), o), "tt", out, [a, b])
+    def tt(name, out, a, b, o):
+        vec(name, lambda: g.vector.tensor_tensor(ap(out), ap(a), ap(b), o), out, [a, b])
 
-    def ts(out, a, s1, o0, s2=None, o1=None):
+    def ts(name, out, a, s1, o0, s2=None, o1=None):
         if o1 is None:
-            vec(lambda: g.vector.tensor_scalar(ap(out), ap(a), val(s1), None, o0), "half", out, [a], [s1])
+            vec(name, lambda: g.vector.tensor_scalar(ap(out), ap(a), val(s1), None, o0), out, [a], [s1])
         else:
-            vec(lambda: g.vector.tensor_scalar(ap(out), ap(a), val(s1), val(s2), o0, o1), "half", out, [a], [s1, s2])
+            vec(name, lambda: g.vector.tensor_scalar(ap(out), ap(a), val(s1), val(s2), o0, o1), out, [a], [s1, s2])
 
-    def scan(out, d0, d1, o0, o1):
-        vec(lambda: g.vector.tensor_tensor_scan(ap(out), ap(d0), ap(d1), 0.0, o0, o1), "half", out, [d0, d1])
+    def scan(name, out, d0, d1, o0, o1):
+        vec(name, lambda: g.vector.tensor_tensor_scan(ap(out), ap(d0), ap(d1), 0.0, o0, o1), out, [d0, d1])
 
-    def mset(out, c):
-        vec(lambda: g.vector.memset(ap(out), c), "half", out, [])
+    def mset(name, out, c):
+        vec(name, lambda: g.vector.memset(ap(out), c), out, [])
 
-    def act(out, in_, f, bias=0.0, scale=1.0, accum=None):
+    def act(name, out, in_, f, bias=0.0, scale=1.0, accum=None):
         if accum is None:
             fn = lambda: g.scalar.activation(ap(out), ap(in_), f, bias=val(bias), scale=val(scale))
         else:
             fn = lambda: g.scalar.activation(ap(out), ap(in_), f, bias=val(bias), scale=val(scale), accum_out=ap(accum))
-        node("c", {"a": [(fn, "one", out, [in_])]}, [out] + aps(accum), [in_] + aps(bias, scale))
+        node(name, "c", {"a": [fn]}, [out] + aps(accum), [in_] + aps(bias, scale))
 
-    def mov(out, in_):
-        node("c", {"a": [(lambda: g.scalar.activation(ap(out), ap(in_), AF.Copy), "one", out, [in_])],
-                   "v": [(lambda: g.vector.tensor_copy(ap(out), ap(in_)), "half", out, [in_])]}, [out], [in_])
+    def mov(name, out, in_):
+        node(name, "c", {"a": [lambda: g.scalar.activation(ap(out), ap(in_), AF.Copy)],
+                         "v": [lambda: g.vector.tensor_copy(ap(out), ap(in_))]}, [out], [in_])
 
-    def mms(ms):
+    def lin(name, out, in_, scale, bias):
+        node(name, "c", {"a": [lambda: g.scalar.activation(ap(out), ap(in_), AF.Identity, bias=val(bias), scale=val(scale))],
+                         "v": [lambda: g.vector.tensor_scalar(ap(out), ap(in_), val(scale), val(bias), AL.mult, AL.add)]},
+             [out], [in_] + aps(bias, scale))
+
+    def mms(name, ms):
         def one(m):
-            return (lambda: g.tensor.matmul(ap(m[0]), ap(m[1]), ap(m[2]), m[3], m[4]), "pe", m[0], [m[1], m[2]])
-        node("c", {"p": [one(m) for m in ms]}, [m[0] for m in ms], [m[1] for m in ms] + [m[2] for m in ms])
+            return lambda: g.tensor.matmul(ap(m[0]), ap(m[1]), ap(m[2]), m[3], m[4])
+        node(name, "c", {"p": [one(m) for m in ms]}, [m[0] for m in ms], [m[1] for m in ms] + [m[2] for m in ms])
 
-    def total(out, terms):
-        mms([(out, a, b, i == 0, i == len(terms) - 1) for i, (a, b) in enumerate(terms)])
+    def total(name, out, terms, start=True, stop=True):
+        mms(name, [(out, a, b, start and i == 0, stop and i == len(terms) - 1) for i, (a, b) in enumerate(terms)])
 
-    def iota(out, pattern, base, cm):
+    def iota(name, out, pattern, base, cm):
         if _S[out[0]][1] == I32:
             fn = lambda: g.iota(ap(out), pattern, base, cm)
         else:
             fn = lambda: g.iota(ap(out), pattern, base, cm, allow_small_or_imprecise_dtypes=True)
-        node("c", {"g": [(fn, "iota", out, [])]}, [out], [])
-
-    def size(v):
-        return (v[2] - v[1]) * (4 if _S[v[0]][1] in (F32, I32) else 2)
+        node(name, "c", {"g": [fn]}, [out], [])
 
     def load(e, sem, dst, src, slow=False):
         if slow:
             fn = lambda: Qs[e].dma_start(ap(dst), src, allow_slow_non_contiguous=True)
         else:
             fn = lambda: Qs[e].dma_start(ap(dst), src)
-        node("dma", {e: fn}, [dst], [], sem=sem, bytes=size(dst))
+        node(sem, "dma", {e: fn}, [dst], [], sem=sem)
 
     def store(e, sem, dst, src):
-        node("dma", {e: lambda: Qs[e].dma_start(dst, ap(src))}, [], [src], sem=sem, bytes=size(src))
+        node(sem, "dma", {e: lambda: Qs[e].dma_start(dst, ap(src))}, [], [src], sem=sem)
 
     def send(msg, t, lands):
         items = [i for m, u, i in mine if m == msg and u == t][0]
-        i = node("send", {"g": lambda: fused(items)}, [], [x[0] for x in items], more=lastsend[-1:])
-        lastsend.append(i)
+        i = node("send" + msg, "send", {"g": lambda: fused(items)}, [], [x[0] for x in items])
         for sem, views in lands:
-            node("land", {"r": None}, views, [], more=[i], sem=sem)
+            node("land" + sem[:-1], "land", {"r": None}, views, [], more=[i], sem=sem)
 
     def ind(win, offs):
         return ("ind", win, offs)
 
-    def to_list(out, zmat, src, o, n=L):
-        total(out, [((zmat, 15 - r, 143 - r), (src, o + r, o + n, 16)) for r in range(16)])
+    def rows(zmat, src, o, n=L):
+        return [((zmat, 15 - r, 143 - r), (src, o + r, o + n, 16)) for r in range(16)]
 
-    C = lambda name, i: (name, i, i + 1)
+    share = {"nm": ("q", 1, 2), "thf": ("thr", 1, 2), "negn": ("tL", 3, 4)}
+    C = lambda name, i: share.get(name, (name, i, i + 1))
     I_, In, Ih, Ib, BO = ("I", 0, 128), ("In", 0, 128), ("Ih", 0, 128), ("Ib", 0, 128), ("BO", 0, 128)
-    GP, RR, O15, PP, EV, OD, WT = [C("col", i) for i in range(7)]
+    GP, RR, SW, PP, WT = [C("col", i) for i in range(5)]
+    RQ = C("p32", 1)
     Xw, RP = ("X", 0, V), ("rpt", 0, R)
-    Em = lambda m: ("E", 128 * m, 128 * m + 128)
+    ci = lambda a, b: ("fa", 56 + a, 56 + b)
+    ex = lambda a, b: ("ub", 56 + a, 56 + b)
+    an = lambda t: ("fa", 14 * (ST - 1 - t), 14 * (ST - t))
+    bl = lambda t: ("ub", 14 * (ST - 1 - t), 14 * (ST - t))
 
     load("s", "ld0", ("avi", 0, 14), T.av[:])
     load("s", "ld1", RP, T.rp[:])
@@ -396,271 +319,308 @@ def rank_program(g, core, T, topo):
     load("a", "ld4", ("kci", 0, L), T.kc[:])
     load("a", "ld5", ("zl", 0, L), T.zs[:])
     load("g", "ld6", ("thi", 0, 1), T.th[:], True)
-    iota(("pi", 0, 1), [[0, 1]], 0, 1)
-    iota(("ci", 0, L), [[1, L]], 0, 0)
-    iota(("cb", 0, 128), [[16, 8], [0, 16]], 0, 0)
-    iota(("mc", 0, 768), [[0, 48], [1, 16]], 0, 0)
-    iota(("r64", 0, 896), [[0, 14], [1, 64]], 0, 0)
-    ts(C("pj", 0), C("pi", 0), 112, AL.bitwise_and)
-    ts(C("pj", 1), C("pi", 0), 15, AL.bitwise_and)
-    ts(C("pj", 2), C("pi", 0), 1, AL.bitwise_and)
-    cp(("col", 0, 2), ("pj", 0, 2))
-    cp(PP, C("pi", 0))
-    cp(OD, C("pj", 2))
-    ts(EV, C("pj", 2), -1.0, AL.mult, 1.0, AL.add)
-    ts(O15, C("pj", 1), -16.0, AL.mult, 240.0, AL.add)
-    ts(WT, C("pj", 1), 2.0, AL.mult, 1.0, AL.add)
-    ts(I_, ("ci", 0, 128), PP, AL.is_equal)
-    ts(In, ("ci", 0, 128), PP, AL.is_equal, -1.0, AL.mult)
-    ts(Ih, ("ci", 0, 128), PP, AL.is_equal, 0.5, AL.mult)
-    ts(Ib, ("ci", 0, 128), PP, AL.is_equal, 8192.0, AL.mult)
-    ts(("Z", 0, 144), ("ci", 0, 144), GP, AL.subtract, 15.0, AL.is_equal)
-    ts(BO, ("cb", 0, 128), GP, AL.is_equal)
-    ts(("B8", 0, 8), ("cb", 0, 128, 16), GP, AL.is_equal, 256.0, AL.mult)
-    ts(("RM", 0, 16), ("ci", 0, 16), RR, AL.is_equal)
-    for m in range(16):
-        act(Em(m), BO, AF.Identity, scale=C("RM", m))
-    cp(("Zh", 0, 144), ("Z", 0, 144))
-    cp(("BOh", 0, 128), BO)
-    ts(("Zw", 0, 144), ("Z", 0, 144), WT, AL.mult)
-    ts(("l16", 0, L), ("ci", 0, L), 16.0, AL.mult)
-    ts(("lq", 0, L), ("ci", 0, L), 1.0 / 512, AL.mult)
-    ts(("cj", 0, 48), ("ci", 0, 48), 16.0, AL.mult)
-    cp(("ex", 0, 48), ("ci", 0, 48))
-    ts(("mT", 0, 256), ("mc", 0, 256), RR, AL.is_equal)
-    ts(("r16", 0, 128), ("mc", 0, 128), 0.0, AL.is_equal, float(2 ** 24), AL.mult)
-    ts(("r64", 0, 896), ("r64", 0, 896), 0.0, AL.is_equal, 65536.0, AL.mult)
-    mset(("one", 0, L), 1.0)
-    ts(("kr", 0, 128), ("one", 0, 128), RR, AL.mult, 16.0, AL.mult)
-    mset(("X", V, V + 64), 0.0)
-    mset(("yg", 0, 768), 0.0)
-    mset(("mis", L, 240), 0.0)
-    mset(("M", 0, ST * MW), 0.0)
-    mset(("as_", 0, (ST - 1) * L), 0)
-    for t in range(ST):
-        mset(("KB", 2 * KW * t + L, 2 * KW * t + L + 16), 0.0)
-        mset(("KB", 2 * KW * t + KW + L, 2 * KW * t + KW + L + 16), 0.0)
-    ts(("lc", 0, 14), ("ci", 0, 14), 16.0, AL.mult, RR, AL.add)
-    cp(C("thf", 0), C("thi", 0))
-    cp(C("thr", 0), C("thi", 0))
-    ts(("l16l", 0, 14), ("lc", 0, 14), 16.0, AL.mult)
-    ts(("sb", 0, 3), ("lc", 0, 3), 0.5, AL.add)
-    ts(("jc", 0, 3), ("lc", 0, 3), 1.0, AL.add, 1000.0, AL.mult)
-    ts(("jd", 0, 3), ("lc", 0, 3), 2.0, AL.mult, float(L), AL.add)
-    ts(("kc0", 0, 14), ("lc", 0, 14), -1.0 / 512, AL.mult, 0.25, AL.add)
-    for s in range(0, 14, 4):
-        e = min(s + 4, 14)
-        ts(("dmp", s, e), ("lc", 0, e - s), float(V), AL.add)
-    cp(("al", 0, 14), ("avi", 0, 14))
-    cp(("bl", 0, 14), ("bvi", 0, 14))
-    cp(("KB", 0, L), ("kci", 0, L))
-    ts(("bh", 0, 14), ("bvi", 0, 14), 992, AL.bitwise_and)
-    ts(("bh", 16, 30), ("bvi", 0, 14), 31, AL.bitwise_and)
-    cp(("bhb", 0, 14), ("bh", 0, 14))
-    cp(("bhb", 16, 30), ("bh", 16, 30))
-    mms([(("M0", h * L + r, h * L + L, 16), Em(r), ("bhb", 16 * h, 16 * h + 14), True, True) for h in range(2) for r in range(16)])
-    act(("bt", 0, L), ("M0", 0, L), AF.Identity, scale=EV)
-    act(("bt", L, 2 * L), ("M0", L, 2 * L), AF.Identity, scale=OD)
-    tt(("KB", KW, KW + L), ("bt", 0, L), ("bt", L, 2 * L), AL.add)
+    iota("pi", ("pi", 0, 1), [[0, 1]], 0, 1)
+    iota("PP", PP, [[0, 1]], 0, 1)
+    iota("ci", ci(0, L), [[1, L]], 0, 0)
+    iota("cb", ("cb", 0, 128), [[16, 8], [0, 16]], 0, 0)
+    iota("mc", ("mc", 0, 256), [[0, 16], [1, 16]], 0, 0)
+    iota("l16", ("l16", 0, L), [[16, L]], 0, 0)
+    iota("cj", ("cj", 0, 48), [[16, 48]], 0, 0)
+    iota("one", ("one", 0, L), [[0, L]], 1, 0)
+    iota("zr", ("zr", 0, 8), [[0, 8]], 0, 0)
+    iota("c11", ("c11", 0, 14), [[0, 14]], V // 2, 0)
+    iota("S0", C("S", 3), [[0, 1]], 0, 0)
+    iota("fitz", C("fit", L), [[0, 1]], 0, 0)
+    iota("KB0", ("KB", L, ST * 2 * KW, KW), [[0, 2 * ST]], 0, 0)
+    iota("X0", ("X", V, V + 64), [[0, 64]], 0, 0)
+    iota("c12", ("c11", 16, 30), [[0, 14]], int(SHIFT), 0)
+    mset("r64", ("r64", 0, 448), 2.0 ** 30)
+    mset("r65", ("r64", 0, 448, 64), -2.0 ** 30)
+    lin("r6b", ("r6b", 0, 448), ("r64", 0, 448), -1.0, 0.0)
+    ts("pj0", C("pj", 0), C("pi", 0), 112, AL.bitwise_and)
+    ts("pj1", C("pj", 1), C("pi", 0), 15, AL.bitwise_and)
+    ts("pj2", C("pj", 2), C("pi", 0), 1, AL.bitwise_and)
+    ts("pj3", C("pj", 3), C("pi", 0), 12, AL.bitwise_and)
+    cp("col", ("col", 0, 2), ("pj", 0, 2))
+    ts("SW", SW, C("pj", 2), -2.0, AL.mult, 1.0, AL.add)
+    ts("WT", WT, C("pj", 1), 2.0, AL.mult, 1.0, AL.add)
+    ts("RQ", RQ, C("pj", 3), 0.25, AL.mult)
+    ts("I", I_, ci(0, 128), PP, AL.is_equal)
+    lin("In", In, I_, -1.0, 0.0)
+    lin("Ih", Ih, I_, 0.5, 0.0)
+    lin("I5", ("I5", 0, 128), I_, 5.0, 0.0)
+    ts("Sw", ("Sw", 0, 128), ci(0, 128), PP, AL.subtract, SW, AL.is_equal)
+    ts("Z", ("Z", 0, 144), ci(0, 144), GP, AL.subtract, 15.0, AL.is_equal)
+    ts("BO", BO, ("cb", 0, 128), GP, AL.is_equal)
+    lin("B8", ("B8", 0, 8), ("BO", 0, 128, 16), 256.0, 0.0)
+    lin("B9", ("B8", 8, 16), ("BO", 0, 128, 16), -256.0, 0.0)
+    lin("B10", ("B8", 16, 24), ("BO", 0, 128, 16), 512.0, 0.0)
+    lin("Zn", ("Zn", 0, 144), ("Z", 0, 144), -1.0, 0.0)
+    lin("Ib", Ib, I_, -4 * SHIFT, 0.0)
+    lin("Zq", ("Zq", 0, 144), ("Z", 0, 144), 1.0 / 16, 0.0)
+    cp("Zh", ("Zh", 0, 144), ("Z", 0, 144))
+    cp("BOh", ("BOh", 0, 128), BO)
+    cp("Ig", ("Ig", 0, 128), I_)
+    lin("Zw", ("Zw", 0, 144), ("Z", 0, 144), WT, 0.0)
+    lin("lq", ("lq", 0, L), ci(0, L), 1.0 / 128, 0.0)
+    cp("ex", ex(0, L), ci(0, L))
+    ts("mT", ("mT", 0, 256), ("mc", 0, 256), RR, AL.is_equal)
+    ts("r16", ("r16", 0, 128), ("mc", 0, 128), 0.0, AL.is_equal, float(2 ** 24), AL.mult)
+    ts("kr", ("kr", 0, 128), ("one", 0, 128), RR, AL.mult, 16.0, AL.mult)
+    lin("lc", ("lc", 0, 14), ci(0, 14), 16.0, RR)
+    cp("thr", C("thr", 0), C("thi", 0))
+    ts("thf", C("thf", 0), C("thi", 0), 15.5, AL.add)
+    lin("l16l", ("l16l", 0, 14), ("lc", 0, 14), 16.0, 0.0)
+    lin("sb", ("sb", 0, 3), ("lc", 0, 3), BIG, BIG / 2)
+    lin("jc", ("jc", 0, 3), ("lc", 0, 3), 1.0, -14.5)
+    lin("jd", ("jd", 0, 3), ("lc", 0, 3), 2.0, float(L))
+    lin("kc0", ("kc0", 0, 14), ("lc", 0, 14), -1.0 / 128, V // 2 - SHIFT + 0.25)
+    iota("dm0", ("dmp", 16, 32), [[0, 4], [16, 4]], V - int(SHIFT), 0)
+    lin("dmp", ("dmp", 0, 16), ("dmp", 16, 32), 1.0, RR)
+    act("p32", C("p32", 0), RR, AF.Exp, scale=LN32)
+    ts("wq", ("wq", 0, 4), ci(0, 4), RQ, AL.is_equal, C("p32", 0), AL.mult)
+    mset("rq", ("rq", 0, 192), 1.0)
+    mset("rq0", ("rq", 0, 192, 4), 0.0)
+    for q in range(4):
+        lin("Wq%d" % q, ("Wq", 128 * q, 128 * q + 128), BO, C("wq", q), 0.0)
+        lin("Dq%d" % q, ("Dq", 128 * q, 128 * q + 128), I_, 2.0 ** (20 + 20 * q), 0.0)
+        mset("cq%d" % q, ("cq", q, 192, 4), (0.5 - 4 * q) * 2.0 ** (20 + 20 * q))
+    cp("au", ("au", 0, 14), ("avi", 0, 14))
+    cp("af", ("al", 0, 14), ("avi", 0, 14))
+    cp("bl", bl(0), ("bvi", 0, 14))
+    cp("K0", ("KB", 0, L), ("kci", 0, L))
+    ts("rpm", ("rpm", 0, R), RP, -float(V // 2), AL.add)
+    ts("bh", ("bh", 0, 14), ("bvi", 0, 14), 992, AL.bitwise_and)
+    ts("bo", ("bh", 16, 30), ("bvi", 0, 14), 31, AL.bitwise_and)
+    tt("bt0", ("bt", 0, L), ind(("bh", 0, 14), ex(0, 14)), ("mT", 0, L), AL.mult)
+    tt("bt1", ("bt", L, 2 * L), ind(("bh", 16, 30), ex(0, 14)), ("mT", 0, L), AL.mult)
+    total("pb0", ("H", 0, L), [(I_, ("bt", 0, L)), (("Sw", 0, 128), ("bt", L, 2 * L))])
+    act("b0", ("KB", KW, KW + L), ("H", 0, L), AF.Copy)
 
     ch = lambda name, c: (name, 16 * CUT[c], 16 * CUT[c + 1])
     lc = lambda name, c: (name, CUT[c], CUT[c + 1])
-    if RELU:
-        ts(("Zn", 0, 144), ("Z", 0, 144), -1.0, AL.mult)
-        ts(("Z2", 0, 144), ("Z", 0, 144), 2.0, AL.mult)
     Lx = ("Lx", 0, 3)
 
     def early(t):
         ko = 2 * KW * t
         if t > 0:
-            to_list(("M2", 0, 14), "Z", "KB", ko + KW)
-            ts(("bl", 0, 14), ("M2", 0, 14), 0.125, AL.mult)
-        cp(("rb", 0, L), ind(RP, ("bl", 0, 14)))
-        ts(("rbf", 0, L), ("rb", 0, L), -1152.0, AL.add)
-        total(("M1", 0, L), [(I_, ("l16", 0, L)), (I_, ("KB", ko, ko + L))])
-        act(("offf", 0, L), ("M1", 0, L), AF.Identity, bias=768.0)
+            total("pbl", ("H", 256, 270), rows("Z", "KB", ko + KW))
+            cp("bl", bl(t), ("H", 256, 270))
+        cp("rb", ("rb", 0, L), ind(RP, bl(t)))
+        mov("rbf", ("rbf", 0, L), ind(("rpm", 0, R), bl(t)))
+        total("poff", ("H", 0, L), [(I_, ("l16", 0, L)), (I_, ("KB", ko, ko + L))])
+        if t == 0:
+            cp("off", ("off", 0, L), ("H", 0, L))
+        else:
+            act("offf", ("offf", 0, L), ("H", 0, L), AF.Identity, bias=768.0)
 
     def merge(t, ko, mp, mo, final):
         qo = 112 * t
-        Kp, mis_ = (mp, mo + 64, mo + 112), (mp, mo + 16, mo + 64)
+        Km, keep, Kq, bq = (mp, mo + 4, mo + 52), (mp, mo + 52, mo + 100), ("MQ", qo + 4, qo + 52), ("MQ", qo + 52, qo + 100)
         if not final:
-            to_list(("M2", 0, 3), "Z", "MQ", qo + 64, 48)
-            ts(("bl2", 0, 3), ("M2", 0, 3), 0.125, AL.mult)
-            cp(("rb2", 0, 48), ind(RP, ("bl2", 0, 3)))
-            mov(("yg", 0, 768), ind(Xw, ("rb2", 0, 48)))
-            ts(("rb2f", 0, 48), ("rb2", 0, 48), -1152.0, AL.add)
-            tt(("kpc", 0, 48), Kp, ("cj", 0, 48), AL.add)
-        act(("ko", 0, 48), ("MQ", qo + 16, qo + 64), AF.Identity, bias=O15)
-        act(("tk", 0, 48), Kp, AF.Identity, bias=-240.0, scale=15.0)
-        node("c", {"v": [(lambda: g.vector.tensor_reduce(ap(C("negn", 0)), ap(("At", 32 * t, 32 * t + 32, 4)), AX.X, AL.min, negate=True),
-                          "one", C("negn", 0), [C("negn", 0)])]}, [C("negn", 0)], [("At", 32 * t, 32 * t + 32)])
-        ts(("tL", 0, 3), ("jc", 0, 3), C("negn", 0), AL.add)
+            total("pb2", ("M2", 32, 35), rows("Z", "MQ", qo + 52, 48))
+            cp("bl2", ("bl2", 0, 3), ("M2", 32, 35))
+            cp("rb2", ("rb2", 0, 48), ind(RP, ("bl2", 0, 3)))
+            mov("ym", ("yg", 0, 768), ind(Xw, ("rb2", 0, 48)))
+        node("negn", "c", {"v": [lambda: g.vector.tensor_reduce(ap(C("negn", 0)), ap(("At", 32 * t, 32 * t + 32, 4)), AX.X, AL.min, negate=True)]},
+             [C("negn", 0)], [("At", 32 * t, 32 * t + 32)])
+        ts("tL", ("tL", 0, 3), ("jc", 0, 3), C("negn", 0), AL.add, 1000.0, AL.mult)
         for s in range(3):
-            ts(C("Lx", s), C("tL", s), C("jd", s), AL.min, C(mp, mo + s), AL.max)
-        mms([(("DD", m, 512, 16), Em(m), ("ko", 0, 32), True, True) for m in range(16)])
-        mms([(("M0", m, 256, 16), Em(m), ("ko", 32, 48), True, True) for m in range(16)])
-        tt(("gm", 0, 768), ind(Kp, ("ex", 0, 48)), ("mc", 0, 768), AL.is_lt)
-        scan(("sc", 0, 512), ("gm", 0, 512), ("DD", 0, 512), AL.mult, AL.max)
-        scan(("sc", 512, 768), ("gm", 512, 768), ("M0", 0, 256), AL.mult, AL.max)
-        tt(("dl", 0, 48), ("sc", 15, 768, 16), ("tk", 0, 48), AL.add)
-        tt(("dl2", 0, 48), ("dl", 0, 48), mis_, AL.mult)
-        tt(ind(("KB", ko, ko + KW), Lx), Kp, ("dl2", 0, 48), AL.add)
-        cp(ind(("KB", ko + KW, ko + 2 * KW), Lx), ("MQ", qo + 64, qo + 112))
+            ts("Lx%d" % s, C("Lx", s), C("tL", s), C("jd", s), AL.min, C(mp, mo + s), AL.max)
+        act("G", ("G", 0, 48), Km, AF.Exp, scale=-LN32)
+        mms("pW0", [(("H", 0, 192), I_, ("cq", 0, 192), True, False)]
+            + [(("H", q, 192, 4), ("Dq", 128 * q, 128 * q + 128), Km, False, False) for q in range(4)])
+        mms("pW1", [(("H", q, 192, 4), ("Wq", 128 * q, 128 * q + 128), Kq, False, q == 3) for q in range(4)])
+        scan("sW", ("sW", 0, 192), ("rq", 0, 192), ("H", 0, 192), AL.mult, AL.max)
+        tt("tW", ("tW", 0, 48), ("sW", 3, 192, 4), ("G", 0, 48), AL.mult)
+        ts("aW", ("aW", 0, 48), ("tW", 0, 48), 15, AL.bitwise_and)
+        tt("kn", ("kn", 0, 48), ("aW", 0, 48), keep, AL.add)
+        if not final:
+            tt("sO", ind(("offf", 0, KW), Lx), ("kn", 0, 48), ("cj", 0, 48), AL.add)
+            cp("off", ("off", 0, L), ("offf", 0, L))
+        cp("sK", ind(("KB", ko, ko + KW), Lx), ("kn", 0, 48))
+        cp("sB", ind(("KB", ko + KW, ko + 2 * KW), Lx), bq)
         if final:
-            to_list(("M2", 0, 14), "Z", "KB", ko + KW)
-            ts(("ybf", 0, 14), ("M2", 0, 14), 0.125, AL.mult)
+            total("pbl", ("M2", 16, 30), rows("Z", "KB", ko + KW))
+            act("ybf", ("ybf", 0, 14), ("M2", 16, 30), AF.Copy)
             store("s", "st0", T.yb[:], ("ybf", 0, 14))
             store("a", "st5", T.yk[:], ("KB", ko, ko + L))
         else:
-            tt(("dlf", 0, 48), ("dl", 0, 48), mis_, AL.mult)
-            tt(ind(("offf", 0, KW), Lx), ("dlf", 0, 48), ("kpc", 0, 48), AL.add)
-            cp(ind(("rbf", 0, KW), Lx), ("rb2f", 0, 48))
+            mov("rb2f", ("rb2f", 0, 48), ind(("rpm", 0, R), ("bl2", 0, 3)))
+            cp("sR", ind(("rbf", 0, KW), Lx), ("rb2f", 0, 48))
 
     early(0)
     for t in range(ST):
         last = t == ST - 1
-        seen.clear()
-        seen[""], seen["t"] = "f" if t == 0 else "m", t
+        rnd[0] = t
         ko, mo, p = 2 * KW * t, MW * t, 2 * KW * (t + 1)
-        K_, z_, a_ = ("KB", ko, ko + L), ("zl", L * t, L * t + L), ("al", L * t, L * t + 14)
+        K_, z_, a_ = ("KB", ko, ko + L), ("zl", L * t, L * t + L), ("al", 112 * t, 112 * t + 14)
         for c in range(CH):
-            mov(("yg", 768 + 16 * CUT[c], 768 + 16 * CUT[c + 1]), ind(Xw, lc("rb", c)))
-        cp(("ra", 0, L), ind(RP, a_))
+            mov("y%d" % c, ("yg", 768 + 16 * CUT[c], 768 + 16 * CUT[c + 1]), ind(Xw, lc("rb", c)))
+        if t > 0:
+            cp("au", ("au", 0, 14), a_)
+        cp("ra", ("ra", 0, L), ind(RP, ("au", 0, 14)))
         for c in range(CH):
-            mov(ch("xg", c), ind(Xw, lc("ra", c)))
+            mov("x%d" % c, ch("xg", c), ind(Xw, lc("ra", c)))
         if t > 0:
             merge(t - 1, ko, "MP", 112 * (t - 1), False)
-        cp(("off", 0, L), ("offf", 0, L))
         if not last:
             send("KB", t, [("KB%d" % t, [("KB", p, p + L), ("KB", p + KW, p + KW + L)])])
-        cp(("af", 0, 14), a_)
-        ts(("a5", 0, 14), a_, 5.0, AL.mult)
 
         for h, (l0, n) in enumerate(((0, 128), (128, L - 128))):
             Th = "T%d" % h
-            mms([((Th, 0, 128), ("kr", 0, 128), I_, True, False)])
             for i in range(4):
-                bank, o = ("XA", "XB", "M1")[(4 * h + i) % 3], 16 * l0 + 4 * n * i
-                mms([((bank, n * j, n * j + n), a, b, s, not s) for j in range(4)
-                     for a, b, s in ((I_, ("xg", 16 * l0 + 4 * i + j, 16 * (l0 + n), 16), True), (In, ("zl", L * t + l0, L * t + l0 + n), False))])
-                act(("a2", o, o + 4 * n), (bank, 0, 4 * n), AF.Abs)
-                if i == 3:
-                    mms([((Th, 0, 128, 1, n), ("KB", ko + l0, ko + l0 + n), I_, False, False)])
-                mms([((Th, 4 * i + j, 128, 16, n), ("a2", o + n * j, o + n * j + n), ("B8", 0, 8), False, i == 3 and j == 3 and n == 128)
-                     for j in range(4)] + ([((Th, 0, 128, 16), I_, ("M", 4, 12), False, True)] if i == 3 and n < 128 else []))
-            scan(("ks", 128 * h, 128 * h + 128), ("r16", 0, 128), (Th, 0, 128), AL.max, AL.min)
+                bank, o, m = "A%d" % ((4 * h + i) % 3), 16 * l0 + 4 * n * i, 4 * h + i
+                if h in VMAX[ROUND[t]]:
+                    xk_ = [("xg", 16 * l0 + 4 * i + j, 16 * (l0 + n), 16) for j in range(4)]
+                    if i == 0:
+                        total("pz%d" % h, ("DD", 256, 256 + n), [(I_, ("zl", L * t + l0, L * t + l0 + n))])
+                    node("a%d" % m, "c", {"v": [(lambda j=j, o=o, n=n, x=xk_[j]: g.vector.tensor_tensor(
+                        ap(("a2", o + n * j, o + n * j + n)), ap(x), ap(("DD", 256, 256 + n)), AL.max)) for j in range(4)]},
+                        [("a2", o, o + 4 * n)], xk_ + [("DD", 256, 256 + n)])
+                    mms("ps%d" % m, ([((Th, 0, 128), ("kr", 0, 128), I_, True, False)] if i == 0 else [])
+                        + [((Th, 4 * i + j, 128, 16, n), xk_[j], ("B8", 8, 16), False, False) for j in range(4)])
+                    mms("pT%d" % m, [((Th, 4 * i + j, 128, 16, n), ("a2", o + n * j, o + n * j + n), ("B8", 16, 24), False, False) for j in range(4)])
+                    continue
+                bank = "A%d" % (m % 3)
+                mms("ps%d" % m, [((bank, n * j, n * j + n), a, b, s, not s) for j in range(4)
+                                 for a, b, s in ((I_, ("xg", 16 * l0 + 4 * i + j, 16 * (l0 + n), 16), True), (In, ("zl", L * t + l0, L * t + l0 + n), False))])
+                act("a%d" % m, ("a2", o, o + 4 * n), (bank, 0, 4 * n), AF.Abs)
+                mms("pT%d" % m, ([((Th, 0, 128), ("kr", 0, 128), I_, True, False)] if i == 0 else [])
+                    + [((Th, 4 * i + j, 128, 16, n), ("a2", o + n * j, o + n * j + n), ("B8", 0, 8), False, False) for j in range(4)])
+            mms("pK%d" % h, [((Th, 0, 128, 1, n), ("KB", ko + l0, ko + l0 + n), I_, False, n == 128)]
+                + ([((Th, 0, 128, 16), I_, ("zr", 0, 8), False, True)] if n < 128 else []))
+            scan("ks%d" % h, ("ks", 128 * h, 128 * h + 128), ("r16", 0, 128), (Th, 0, 128), AL.max, AL.min)
         for c in range(CH):
-            rows = lambda z, b: [((z, 15 - k, 143 - k), (b, 16 * CUT[c] + k, 16 * CUT[c + 1], 16)) for k in range(16)]
-            yw, mid = ("yg", 0, 768 + 16 * CUT[c + 1]), (CUT[c] + CUT[c + 1]) // 2
-            if c in WACT:
-                act(ch("dr", c), ind(yw, lc("off", c)), AF.Copy)
-                for bank, p0, p1 in (("XA", CUT[c], mid), ("XB", mid, CUT[c + 1])):
-                    total((bank, 0, 16 * (p1 - p0)), [(I_, ("dr", 16 * p0, 16 * p1)), (In, ("xg", 16 * p0, 16 * p1))])
-                    act(("dg", 16 * p0, 16 * p1), (bank, 0, 16 * (p1 - p0)), AF.Abs)
-                total(lc("DD", c), rows("Z", "dg"))
-                continue
-            for p0, p1 in ((CUT[c], mid), (mid, CUT[c + 1])) if c in SPLIT else ((CUT[c], CUT[c + 1]),):
-                tt(("dg", 16 * p0, 16 * p1), ind(yw, ("off", p0, p1)), ("xg", 16 * p0, 16 * p1), AL.subtract)
-            if c in RELU:
-                ts(ch("dr", c), ch("dg", c), 0.0, AL.max)
-                total(lc("DD", c), rows("Zn", "dg") + rows("Z2", "dr"))
+            yw = ("yg", 768 if t == 0 else 0, 768 + 16 * CUT[c + 1])
+            bank, relu = "H" if c == CH - 1 else "DD", c in RELU[ROUND[t]]
+            if c in WACT[ROUND[t]]:
+                act("d%d" % c, ch("dg", c), ind(yw, lc("off", c)), AF.Copy)
+                mid = 8 * (CUT[c] + CUT[c + 1])
+                for h, (p0, p1) in enumerate(((16 * CUT[c], mid), (mid, 16 * CUT[c + 1]))):
+                    total("pw%d%d" % (c, h), ("A%d" % h, 0, p1 - p0), [(I_, ("dg", p0, p1)), (In, ("xg", p0, p1))])
+                    act("r%d%d" % (c, h), ("dr", p0, p1), ("A%d" % h, 0, p1 - p0), AF.Abs)
             else:
-                act(ch("dg", c), ch("dg", c), AF.Abs)
-                total(lc("DD", c), rows("Z", "dg"))
-        cp(("ki", 0, 16), ("ks", 15, 256, 16))
-        ts(("kt", 0, 16), ("ki", 0, 16), 4, AL.logical_shift_right, 15, AL.bitwise_and)
-        ts(("kt", 16, 32), ("ki", 0, 16), 15, AL.bitwise_and)
-        cp(("eK", 0, 256), ind(("kt", 16, 32), ("ex", 0, 16)))
-        tt(("ek", 0, 256), ind(("kt", 0, 16), ("ex", 0, 16)), ("mT", 0, 256), AL.mult)
-        mms([(("T0", 0, 128), ("eK", 0, 128), I_, True, True), (("T0", 128, L), ("eK", 128, 256), ("I", 0, 96), True, True)])
-        mms([(("T1", 0, 14), I_, ("l16l", 0, 14), True, False), (("T1", 0, 8), ("ek", 0, 128), ("BO", 0, 128, 16), False, False),
-             (("T1", 8, 14), ("ek", 128, 256), ("BO", 0, 96, 16), False, True)])
-        ts(("T0", 256, 256 + L), ("T0", 0, L), RR, AL.is_equal)
-        tt(("prod", 0, L), ("T0", 256, 256 + L), ("rbf", 0, L), AL.mult)
-        cp(("l1", 0, 14), ("T1", 0, 14))
-        mov(("xk", 0, L), ind(("xg", 0, W), ("l1", 0, 14)))
-        to_list(("M2", 0, 14), "Zh", "prod", 0)
-        ts(("cl", 0, 14), ("M2", 0, 14), 1152.0, AL.add)
-        ts(("cf", 0, 14), ("M2", 0, 14), 1152.0, AL.add)
-        tt(("kb", 0, 14), ("kc0", 0, 14), ("M2", 0, 14), AL.subtract)
-        tt(("tz", 0, L), ind(Xw, ("cl", 0, 14)), z_, AL.subtract)
-        act(("zz", 0, L), ("tz", 0, L), AF.Abs)
-        total(("M0", L, 2 * L), [(Ih, z_), (Ih, ("xg", 0, W, 16))])
-        total(("M0", 0, L), [(Ih, ("xk", 0, L)), (Ih, ("tz", 0, L)), (Ih, z_)])
-        to_list(("T1", 0, 14), "Zw", "zz", 0)
-        ts(("hz", 0, 2 * L), ("M0", 0, 2 * L), -0.25, AL.add)
-        tt(("ui", 0, 14), ("T1", 0, 14), ("a5", 0, 14), AL.add)
-        cp(("zz", L, 2 * L), ("hz", L, 2 * L))
-        ts(("am", 0, 14), ("ui", 0, 14), R - 1, AL.bitwise_and)
-        tt(("b2", 0, 14), ("dmp", 0, 14), ("cf", 0, 14), AL.subtract)
-        tt(("dm", 0, 14), ("af", 0, 14), ("am", 0, 14), AL.subtract)
+                tt("d%d" % c, ch("dg", c), ind(yw, lc("off", c)), ch("xg", c), AL.subtract)
+            if c in WACT[ROUND[t]]:
+                pass
+            elif relu:
+                total("pE%d" % c, lc(bank, c), rows("Zn", "dg", 16 * CUT[c], 16 * (CUT[c + 1] - CUT[c])), stop=False)
+                ts("r%d" % c, ch("dr", c), ch("dg", c), 0.0, AL.max, 2.0, AL.mult)
+            else:
+                act("r%d" % c, ch("dr", c), ch("dg", c), AF.Abs)
+            total("pD%d" % c, lc(bank, c), rows("Z", "dr", 16 * CUT[c], 16 * (CUT[c + 1] - CUT[c])), start=not relu)
+        for h, (bank, l0, l1) in enumerate((("DD", 0, CUT[-2]), ("H", CUT[-2], L))):
+            ts("fit%d" % h, ("fit", l0, l1), (bank, l0, l1), C("thr", 0), AL.is_le, 32.0, AL.mult)
+            total("pn%d" % h, (bank, 256 + l0, 256 + l1), [(BO, ("fit", l0, l1))])
+            ts("div%d" % h, ("div", l0, l1), (bank, 256 + l0, 256 + l1), 272.0, AL.is_lt, BIG, AL.mult)
+        scan("cum", ("cum", 0, L), ("one", 0, L), ("div", 0, L), AL.mult, AL.add)
+        cp("ki", ("ki", 0, 16), ("ks", 15, 256, 16))
+        ts("kt1", ("kt", 16, 32), ("ki", 0, 16), 15, AL.bitwise_and)
+        ts("kt0", ("kt", 0, 16), ("ki", 0, 16), 4, AL.logical_shift_right, 15, AL.bitwise_and)
+        tt("eK", ("eK", 0, 256), ind(("kt", 16, 32), ex(0, 16)), ("mc", 0, 256), AL.is_equal)
+        tt("ek", ("ek", 0, 256), ind(("kt", 0, 16), ex(0, 16)), ("mT", 0, 256), AL.mult)
+        mms("pk", [(("T0", 0, 128), ("eK", 0, 128), I_, True, True), (("T0", 128, L), ("eK", 128, 256), ("I", 0, 96), True, True)])
+        mms("pl", [(("T1", 0, 14), I_, ("l16l", 0, 14), True, False), (("T1", 0, 8), ("ek", 0, 128), ("BO", 0, 128, 16), False, False),
+                   (("T1", 8, 14), ("ek", 128, 256), ("BO", 0, 96, 16), False, True)])
+        tt("prod", ("prod", 0, L), ("T0", 0, L), ("rbf", 0, L), AL.mult)
+        cp("l1", ("l1", 0, 14), ("T1", 0, 14))
+        mov("xk", ("xk", 0, L), ind(("xg", 0, W), ("l1", 0, 14)))
+        clist = [(I_, ("c11", 0, 14)), (In, ("c11", 16, 30))] + rows("Zh", "prod", 0)
+        total("pc", ("M2", 0, 14), clist)
+        ts("cl", ("cl", 0, 14), ("M2", 0, 14), SHIFT, AL.add)
+        tt("kb", ("kb", 0, 14), ("kc0", 0, 14), ("M2", 0, 14), AL.subtract)
+        if OPT["C16"]:
+            ts("c16", ("c16", 0, 14), ("M2", 0, 14), SHIFT - V // 2, AL.add)
+            clist = clist[:2] + [(("Ig", 0, 128), ("c16", 0, 14))]
+        if OPT["WK"]:
+            mov("tz", ("tz", 0, L), ind(Xw, ("cl", 0, 14)))
+            total("ptz", ("T1", 64, 64 + L), [(I_, ("tz", 0, L)), (In, z_)])
+            act("zz", ("zz", 0, L), ("T1", 64, 64 + L), AF.Abs)
+        else:
+            tt("tz", ("tz", 0, L), ind(Xw, ("cl", 0, 14)), z_, AL.subtract)
+            act("zz", ("zz", 0, L), ("tz", 0, L), AF.Abs)
+        total("pu", ("T1", 0, 14), [(("I5", 0, 128), a_)] + rows("Zw", "zz", 0))
+        total("ph", ("M2", 64, 64 + L), [(Ih, ("xk", 0, L)), (Ih, ("tz", 0, L))] + ([] if OPT["WK"] else [(Ih, z_)]))
+        ts("hz", ("hz", 0, L), ("M2", 64, 64 + L), -0.25, AL.add)
+        cp("ui", ("ui", 0, 14), ("T1", 0, 14))
+        ts("am", ("am", 0, 14), ("ui", 0, 14), R - 1, AL.bitwise_and)
+        tt("dm", ("dm", 0, 14), a_, ("am", 0, 14), AL.subtract)
 
-        ts(("mis", 0, L), ("DD", 0, L), C("thr", 0), AL.is_gt)
-        total(("XA", 0, L), [(BO, ("mis", 0, L))])
-        to_list(("XB", 0, 14), "Z", "mis", 0)
-        ts(("div", 0, L), ("XA", 0, L), 7.5, AL.is_gt)
-        scan(("cum", 0, L), ("one", 0, L), ("div", 0, L), AL.mult, AL.add)
-        total(("T0", 0, L), [(("BOh", 0, 128), ("prod", 0, L)), (I_, ("lq", 0, L)), (Ib, ("div", 0, L))])
-        act(C("At", 32 * t + 4 * rank), C("cum", L - 1), AF.Identity, scale=1000.0)
+        late = LATE[ROUND[t]]
+        total("pcr", ("T0", 0, L), [(("BOh", 0, 128), ("prod", 0, L)), (I_, ("lq", 0, L))] + ([(I_, ("div", 0, L))] if late else []))
+        wins = [min(64 * (s // 4), L - 64) for s in range(14)]
+        for s in range(14):
+            act("ab%d" % s, ("ab", 64 * s, 64 * s + 64), ("T0", wins[s], wins[s] + 64), AF.Abs, bias=C("kb", s))
+        for h in range(0 if late else 2):
+            bank = "A%d" % (h + 1)
+            total("pa%d" % h, (bank, 0, 448), [(Ib, ("ab", 448 * h, 448 * h + 448))], stop=False)
+            mms("pv%d" % h, [((bank, 64 * s, 64 * s + 64), Ib, ("div", wins[7 * h + s], wins[7 * h + s] + 64), False, s == 6) for s in range(7)])
+        total("pc2", ("A0", 0, 14), clist, stop=False)
+        total("pdl", ("A0", 0, 14), rows("Zq", "div", 0), start=False)
+
+        total("pH", ("DD", 0, L), [(Ih, z_), (Ih, ("xg", 0, W, 16)), (I_, ("div", 0, L))])
+        total("pP", ("T0", 0, L), [(I_, ("zz", 0, L)), (In, ("div", 0, L))])
+        ts("h0", ("h0", 0, L), ("DD", 0, L), -BIG - 0.25, AL.add)
+        tt("zn", ("zs_", L * t, L * t + L), ("T0", 0, L), ("h0", 0, L), AL.max)
+        At = C("At", 32 * t + 4 * rank)
+        lin("At", At, C("cum", L - 1), 1.0 / BIG, -15.5)
         for s in range(3):
-            act(("sg", L * s, L * s + L), ("cum", 0, L), AF.Sign, bias=C("sb", s), scale=-1.0, accum=C("S", s))
-        ts(("dvl", 0, 14), ("XB", 0, 14), 7.5, AL.is_gt)
-        tt(("t1", 0, 14), ("dvl", 0, 14), ("dm", 0, 14), AL.mult)
-        tt(("an", 0, 14), ("t1", 0, 14), ("am", 0, 14), AL.add)
-        ts(("zo", 0, 14), ("XB", 0, 14), 7.5, AL.is_gt, float(L), AL.mult)
-        tt(("zp", 0, 14), ("zo", 0, 14), ("lc", 0, 14), AL.add)
-        cp(("zq", 0, 14), ("zp", 0, 14))
-        mov(("zs_", L * t, L * t + L), ind(("zz", 0, 2 * L), ("zq", 0, 14)))
+            act("sg%d" % s, ("sg", L * s, L * s + L), ("cum", 0, L), AF.Sign, bias=C("sb", s), scale=-1.0, accum=C("S", s))
+        ts("dvl", ("dvl", 0, 14), ("A0", 0, 14), BIG - SHIFT, AL.is_ge)
+        tt("t1", ("t1", 0, 14), ("dvl", 0, 14), ("dm", 0, 14), AL.mult)
+        tt("an", an(t), ("t1", 0, 14), ("am", 0, 14), AL.add)
         send("A", t, [("A%d" % t, [C("At", 32 * t + 4 * r) for r in range(N) if r != rank])])
         if last:
-            store("s", "st1", T.ya[:], ("an", 0, 14))
+            store("s", "st1", T.ya[:], an(t))
             store("s", "st2", T.yz[:], ("zs_", L * t, L * t + L))
         else:
-            cp(("as_", L * t, L * t + 14), ("an", 0, 14))
-            send("a", t, [("a%d" % t, [("al", L * t + L, L * t + 2 * L)]), ("z%d" % t, [("zl", L * t + L, L * t + 2 * L)])])
-        ts(("Du", 0, 3), ("S", 0, 3), 0.5, AL.mult, 112.0, AL.add)
-        act(("M", mo, mo + 3), ("S", 0, 3), AF.Identity, bias=112.0, scale=0.5)
-        mov(("M", mo + 64, mo + 112), ind(("KB", ko, ko + 240), ("Du", 0, 3)))
-        mov(("M", mo + 16, mo + 64), ind(("mis", 0, 240), ("Du", 0, 3)))
-        mov(("M", mo + 112, mo + 160), ind(("KB", ko + KW, ko + KW + 240), ("Du", 0, 3)))
-        send("M", t, [("MQ%d" % t, [("MQ", 112 * t, 112 * t + 112)])] + ([] if last else [("MP%d" % t, [("MP", 112 * t, 112 * t + 112)])]))
+            send("a", t, [("a%d" % t, [("al", 112 * t + 112, 112 * t + 224)]), ("z%d" % t, [("zl", L * t + L, L * t + 2 * L)])])
+        Du = ("Du", 0, 3)
+        ts("Du", Du, ("S", 0, 3), 0.5, AL.mult, 112.0, AL.add)
+        lin("Dm", ("M", mo, mo + 4), ("S", 0, 4), 0.5, 112.0)
+        mov("Kp", ("M", mo + 100, mo + 148), ind(("KB", ko, ko + L + 1), Du))
+        mov("bm", ("M", mo + 148, mo + 196), ind(("KB", ko + KW, ko + KW + L + 1), Du))
+        tt("Km", ("M", mo + 4, mo + 52), ind(("fit", 0, L + 1), Du), ("M", mo + 100, mo + 148), AL.add)
+        tt("keep", ("M", mo + 52, mo + 100), ind(("fit", 0, L + 1), Du), ("M", mo + 100, mo + 148), AL.min)
+        send("M", t, [("MQ%d" % t, [("MQ", 112 * t, 112 * t + MS)])] + ([] if last else [("MP%d" % t, [("MP", 112 * t, 112 * t + MS)])]))
         if not last:
-            cp(C("Ai", 0), C("cum", L - 1))
-            ts(C("Aj", 0), C("Ai", 0), 31, AL.bitwise_and)
-            tt(C("thr", 0), C("Aj", 0), C("thf", 0), AL.add)
+            lin("q", C("q", 0), At, 1.0, MAGIC)
+            ts("nm", C("nm", 0), C("q", 0), MAGIC, AL.subtract, At, AL.subtract)
+            lin("thn", C("thr", 0), C("nm", 0), -1.0, C("thf", 0))
+            rnd[0] = t + 1
             early(t + 1)
+            rnd[0] = t
 
-        for s in range(14):
-            w0 = min(64 * (s // 4), L - 64)
-            act(("ab", 64 * s, 64 * s + 64), ("T0", w0, w0 + 64), AF.Abs, bias=C("kb", s))
-        scan(("ms", 0, 896), ("r64", 0, 896), ("ab", 0, 896), AL.max, AL.min)
-        ts(("b1", 0, 14), ("ms", 63, 896, 64), 0.25, AL.not_equal)
-        tt(("b3", 0, 14), ("b1", 0, 14), ("b2", 0, 14), AL.mult)
-        tt(("b4", 0, 14), ("b3", 0, 14), ("cf", 0, 14), AL.add)
-        cp(("so", 0, 14), ("b4", 0, 14))
+        if late:
+            for h in range(2):
+                scan("ms%d" % h, ("msb", 448 * h, 448 * h + 448), ("r6b", 0, 448), ("ab", 448 * h, 448 * h + 448), AL.max, AL.min)
+            lin("lose", ("lose", 0, 14), ("msb", 63, 896, 64), -4 * SHIFT, 0.0)
+            tt("b3", ("b3", 0, 14), ("lose", 0, 14), ("A0", 0, 14), AL.max)
+        else:
+            for h in range(2):
+                scan("ms%d" % h, ("ms", 448 * h, 448 * h + 448), ("r64", 0, 448), ("A%d" % (h + 1), 0, 448), AL.min, AL.max)
+            tt("b3", ("b3", 0, 14), ("ms", 63, 896, 64), ("A0", 0, 14), AL.max)
+        tt("b4", ("b4", 0, 14), ("b3", 0, 14), ("dmp", 0, 14), AL.min)
+        ts("so", ("so", 0, 14), ("b4", 0, 14), SHIFT, AL.add)
         for s in (12, 8, 4, 0):
             e = min(s + 4, 14)
-            cp(ind(("X", 0, V + 64), ("so", s, e)), ("hz", 16 * s, 16 * e))
+            cp("X%d" % (s // 4 + 1), ind(("X", 0, V + 64), ("so", s, e)), ("hz", 16 * s, 16 * e))
         if last:
             store("s", "st3", T.yx[:, 0:V // 2], ("X", 0, V // 2))
             store("a", "st4", T.yx[:, V // 2:V], ("X", V // 2, V))
+            rnd[0] = ST
             merge(t, ko, "M", mo, True)
 
-    for t in range(0 if ORDER else ST):
-        byk = {nd["key"][1:]: i for i, nd in enumerate(nodes) if nd["step"] == t}
-        for e, names in CHAIN["f" if t == 0 else "m"].items():
-            row = [byk[x] for x in names.split()]
-            for i, j in zip([None] + row, row):
-                nodes[j]["alt"] = {e: nodes[j]["alt"][e]}
-                if i is not None:
-                    nodes[j]["deps"] = sorted(set(nodes[j]["deps"]) | {i})
-    if ORDER and "order" not in _ORDER:
-        code_ = [52 * LETTERS.index(ORDER[i]) + LETTERS.index(ORDER[i + 1]) for i in range(0, len(ORDER), 2)]
-        _ORDER["order"] = [(x // 2, "av"[x % 2] if len(nodes[x // 2]["alt"]) > 1 else list(nodes[x // 2]["alt"])[0]) for x in code_]
-        _ORDER["nodes"] = nodes
-    if "order" not in _ORDER:
-        _ORDER["order"] = _schedule(nodes, COST, _tune(nodes))[0]
-        _ORDER["nodes"] = nodes
+    index = {nd["key"]: i for i, nd in enumerate(nodes)}
+    lists = {e: [] for e in list(Qs) + ["r"]}
+    for i, nd in enumerate(nodes):
+        if ORDER is None or nd["kind"] == "land" or list(nd["alt"]) == ["s"]:
+            lists[list(nd["alt"])[0]].append(i)
+    for t in range(ST if ORDER else 0):
+        for e, names in ORDER[ROUND[t]].items():
+            lists[e] += [index[(t + 1, x[1:]) if x[0] == "+" else (t, x)] for x in names.split()]
+    _C["nodes"], _C["lists"] = nodes, lists
     cnt = {"v": 0, "a": 0, "p": 0, "g": 0}
     know = {e: {} for e in Qs}
     token, clock, queue, owed = {}, {}, {}, {}
@@ -671,7 +631,7 @@ def rank_program(g, core, T, topo):
             for k, n in clock[tok].items():
                 know[e][k] = max(know[e].get(k, 0), n)
 
-    for i, e in _ORDER["order"]:
+    def issue(i, e):
         nd = nodes[i]
         queue[i] = e
         if nd["kind"] == "land":
@@ -680,25 +640,32 @@ def rank_program(g, core, T, topo):
         else:
             need = {}
             for d in nd["deps"]:
-                if d in token and not (e == queue[d] and (e == "p" or d not in nd["hard"])):
+                if d in token and not (e == queue[d] == "p"):
                     need[token[d][0]] = max(need.get(token[d][0], 0), token[d][1])
             for tok in sorted(need.items(), key=lambda x: -sum(clock[x].values())):
                 wait(e, tok)
             if nd["kind"] == "send":
                 nd["alt"][e]()
-                continue
+                return
             if nd["kind"] == "dma":
                 nd["alt"][e]().then_inc(T.sem[nd["sem"]], 16)
                 tok = (nd["sem"], 16)
             else:
-                for x in nd["alt"][e]:
-                    x[0]().then_inc(T.sem["c" + e], 1)
-                    cnt[e] += 1
+                for x in nd["alt"][e][:-1]:
+                    x()
+                nd["alt"][e][-1]().then_inc(T.sem["c" + e], 1)
+                cnt[e] += 1
                 tok = ("c" + e, cnt[e])
             clock[tok] = dict(know[e])
             clock[tok][tok[0]] = tok[1]
         token[i] = tok
         owed[tok[0]] = tok[1]
+
+    head = {e: 0 for e in lists}
+    while len(queue) < len(nodes):
+        go = [e for e in lists if head[e] < len(lists[e]) and all(d in queue for d in nodes[lists[e][head[e]]]["deps"])]
+        issue(lists[go[0]][head[go[0]]], go[0])
+        head[go[0]] += 1
     g.wait_ge(T.sem.ls, sent[0])
     for tok in owed.items():
         wait("g", tok)

from concourse.bass import DstId, RemoteDMATransfer
from concourse.mybir import AluOpType as AL, AxisListType as AX, ActivationFunctionType as AF

N, V, R, L, ST, Q = 8, 2304, 1024, 224, 4, 3
W = 16 * L
CUT = [0, 64, 128, 176, L]
CH = len(CUT) - 1
KW = 320
MW = 196
MS = 100
BIG = 4096.0
SHIFT = 2.0 ** 17
LN32 = 3.4657359027997265
MAGIC = 1.5 * 2 ** 28
BF, F32, I32, U16, F16 = "bfloat16", "float32", "int32", "uint16", "float16"

_S = {
    "X": (V + 64, BF), "rpt": (R, I32), "rpm": (R, F32), "xg": (W, BF), "yg": (W + 768, BF), "dg": (W, BF), "dr": (W, BF), "a2": (W, BF),
    "avi": (16, I32), "bvi": (16, I32), "kci": (L, I32), "thi": (8, I32),
    "KB": (ST * 2 * KW, BF), "M": (ST * MW, BF), "MP": (ST * 112, BF), "MQ": (ST * 112, BF), "At": (ST * 32, F32),
    "zs_": (ST * L, BF), "zl": (ST * L, BF), "fa": (56 + L, F32), "al": (ST * 112, F32), "ub": (56 + L, U16), "bll": (ST * L, U16),
    "au": (16, U16), "ra": (L, U16), "rb": (L, U16), "offf": (KW, F32), "off": (L, U16),
    "bl2": (4, U16), "rb2": (48, U16), "negn": (4, F32), "tL": (4, F32), "Lx": (4, U16),
    "G": (48, BF), "sW": (192, F32), "tW": (48, I32), "aW": (48, I32), "kn": (48, F32),
    "ks": (256, F32), "ki": (16, I32), "kt": (32, I32), "ktb": (16, BF), "ek": (256, BF), "eK": (256, BF), "l1": (16, U16),
    "eq": (L, BF), "prod": (L, F16), "cl": (16, U16), "kb": (16, F32), "xk": (L, BF), "zz": (L, BF), "tz": (L, BF),
    "hz": (L, I32), "h0": (L, I32), "ui": (16, I32), "am": (16, I32), "dm": (16, F32), "dvl": (16, F32), "t1": (16, F32),
    "fit": (240, BF), "div": (L, BF), "cum": (L, BF), "sg": (3 * L, BF), "S": (4, F32), "Du": (4, U16),
    "thf": (4, F32), "thr": (4, F32), "q": (4, F32), "nm": (4, F32),
    "ab": (896, BF), "ms": (896, F32), "Ib": (128, BF), "Zq": (144, BF), "b3": (16, F32), "b4": (16, F32), "so": (16, U16), "ybf": (16, F32),
    "pi": (4, I32), "pj": (4, I32), "col": (8, F32), "cb": (128, F32), "mc": (256, BF), "r64": (448, BF),
    "Z": (144, BF), "Zn": (144, BF), "Zw": (144, BF), "Zh": (144, F16), "BO": (128, BF), "BOh": (128, F16), "B8": (24, BF), "rbf": (KW, F32), "rb2f": (48, F32), "c16": (16, F16), "Ig": (128, F16), "lose": (16, F32), "msb": (896, BF), "r6b": (896, BF),
    "I": (128, BF), "In": (128, BF), "Ih": (128, BF), "I5": (128, F32), "Sw": (128, BF), "kr": (128, BF),
    "l16": (L, BF), "lq": (L, BF), "mT": (256, BF), "r16": (128, BF), "one": (L, BF), "cj": (48, F32),
    "lc": (16, F32), "l16l": (16, BF), "sb": (4, F32), "jc": (4, F32), "jd": (4, BF), "dmp": (32, F32), "kc0": (16, F32),
    "c11": (32, BF), "zr": (8, BF), "p32": (4, BF), "wq": (4, F32), "Wq": (512, BF), "Dq": (512, BF), "cq": (192, BF), "rq": (192, BF),
    "bh": (32, I32), "bt": (2 * L, BF),
}
for _b in ("ktb", "eq", "bll", "nm", "thf", "negn"):
    del _S[_b]
SCRATCH = {k: ("sbuf", [128, w], d) for k, (w, d) in _S.items()}
_P = ["A0", "A1", "A2", "T0", "T1", "DD", "H", "M2"]
for _b in _P:
    SCRATCH[_b] = ("psum", [128, 512], F32)
_MSG = ["A", "MP", "MQ", "a", "z", "KB"]
SEMAPHORES = (["cv", "ca", "cp", "cg", "ls"] + ["%s%d" % (m, t) for m in _MSG for t in range(ST)]
              + ["ld%d" % i for i in range(8)] + ["st%d" % i for i in range(6)])

ROUND = (0, 1, 1, 2)
RELU = [[], [], []]
WACT = [[], [], []]
VMAX = [[], [], []]
LATE = [1, 1, 1]
OPT = {"E1": 1, "WK": 0, "C16": 1}
SENDS = ["KB", "A", "M", "a"]
ORDER = [{'v': 'ex pj2 pj1 SW pj0 col pj3 WT cq0 Sw I rq au bh af cq1 kr bo bl BO r64 Z mT bt0 r16 bt1 ra rb BOh K0 RQ x1 x0 off y1 d0 Zh y2 d1 thr d2 cq2 ks0 d3 ks1 rpm ki sb kt1 r65 wq eK fit0 jc fit1 thf prod div0 div1 Ig kt0 cum ek c16 cl kb tz Ih Wq0 Du At l1 cq3 Zw Wq3 Dq2 keep +bl Km h0 +rb ms1 ui ms0 am zn dm Dq0 dvl b3 t1 b4 an so hz X4 X3 X2 nm rq0 X1', 'a': 'ld5 ld3 lc ld4 p32 lq B9 B8 b0 In y0 y3 x2 x3 a1 a2 a0 a4 a5 kc0 a3 a7 r0 a6 r1 r2 r3 Zn l16l Wq1 rbf r6b I5 Zq sg1 sg2 sg0 ab8 ab6 ab11 ab3 ab10 zz ab4 Dm Kp ab1 ab9 ab12 ab2 ab5 ab7 ab13 ab0 bm xk Ib Dq1 B10 lose Dq3 dmp +rbf Wq2 +offf q thn jd', 'p': 'pb0 poff ps2 ps1 ps0 ps4 ps5 ps3 ps7 ps6 pT4 pT0 pT1 pT2 pT3 pK0 pT5 pD0 pT6 pT7 pK1 pD1 pD2 pD3 pk pn0 pn1 pc pcr +pbl pl pc2 pH pu pP pdl ph +poff', 'g': 'ci pi S0 PP KB0 cb one mc cj c12 l16 zr ld6 fitz sendKB c11 X0 dm0 sendA sendM senda'}, {'v': 'y1 negn sW tL tW Lx1 aW Lx0 bl2 kn Lx2 rb2 sO au ra x0 ym x3 off rb2f d3 sK d0 d1 d2 ks1 ks0 ki sR sB kt1 kt0 fit1 eK ek fit0 prod div1 div0 cum c16 cl l1 kb tz Du At Kp Dm q keep bm Km dvl ms1 ms0 h0 b3 ui b4 am so dm hz t1 zn an X4 nm X3 +bl X2 +rb X1', 'a': 'y3 G y2 y0 x1 x2 a0 a1 a2 a3 a4 r3 a6 a5 a7 r0 r1 r2 sg0 sg2 sg1 ab0 ab8 ab10 ab12 ab11 ab9 zz ab5 ab2 ab13 ab7 ab6 ab4 ab1 ab3 xk lose +rbf thn +offf', 'p': 'pW0 pW1 pb2 ps0 ps1 ps2 ps3 ps4 pT0 ps6 ps5 ps7 pT4 pT1 pT2 pT5 pT6 pT3 pT7 pK0 pK1 pD3 pD0 pD1 pD2 pk pn1 pn0 pl pc pcr pc2 pdl pH pu ph pP +pbl +poff', 'g': 'sendKB sendA sendM senda'}, {'v': 'y1 y3 bl2 negn rb2 sW tL Lx0 Lx2 au tW ra aW x0 kn Lx1 sO x2 off d0 d1 d3 d2 sK rb2f ks0 sR fit1 fit0 div1 ks1 div0 ki cum kt1 eK h0 sB prod Du Kp keep Dm Km kb cl kt0 ek c16 tz l1 ms1 ms0 dvl lose b3 b4 hz so X4 zn X3 +negn ui +tL am X2 +Lx2 +Lx0 +Lx1 X1 +sB dm +sW t1 +tW an +aW +kn +sK', 'a': 'y0 y2 G ym x1 x3 a0 a2 a1 a3 a5 r0 a4 r1 r3 r2 a6 a7 At sg2 sg1 sg0 bm ab9 ab7 ab12 ab3 ab4 ab5 ab11 ab13 ab10 ab1 ab6 ab8 ab2 ab0 xk zz +G st4 +ybf +st5', 'p': 'pW0 pb2 pW1 ps0 ps2 ps1 ps3 ps5 ps4 pT0 ps6 pT1 pT2 pD0 pT3 ps7 pT4 pT5 pD1 pK0 pD3 pD2 pT6 pn1 pT7 pK1 pn0 pH pk pc pcr +pW0 pl pc2 pdl ph pP pu +pW1 +pbl', 'g': 'sendA sendM'}]
_old2 = [{'v': 'pj2 rq pj3 r64 SW pj0 Sw I Dq2 pj1 col bh ex bo mT bt0 bt1 r16 BO bl au Z WT kr ra K0 rb x1 x0 off y3 Zh y2 d0 d1 Dq0 d3 dmp ks0 r3 d2 rq0 ks1 thr ki cq0 kt1 kt0 fit1 ktb ek rpm eq fit0 prod div0 div1 BOh cum thf RQ Zq r65 cl l1 wq kb cq1 tz Du Wq2 af At +rb Kp bm cq2 Km dvl Ib Wq1 ui am Dm dm h0 t1 keep an ms1 zn ms0 hz b3 b4 cq3 so X4 X3 X2 X1 nm thn', 'a': 'ld5 ld3 In lc ld4 l16l Dq1 Zn jd B8 b0 y1 x2 y0 x3 a1 a0 a2 a4 a3 lq a5 r0 sb a7 a6 r1 r2 jc eK I5 Ih Dq3 p32 sg2 kc0 sg1 sg0 Zw zz Wq3 ab10 ab13 ab8 ab2 ab11 Wq0 ab9 ab3 ab5 ab7 ab12 ab1 ab0 ab4 ab6 xk q +offf', 'p': 'pb0 poff ps1 ps2 ps0 ps4 ps3 ps5 pT4 pT0 pT1 pT2 pT3 ps6 ps7 pK0 pT5 pE3 pD0 pT6 pT7 pK1 pD3 pD1 pD2 pk pn0 pn1 pl pc pcr pc2 pdl pu pH pa1 pv1 pP pa0 pv0 ph +poff', 'g': 'pi PP ci mc KB0 cb ld6 l16 one X0 zr dm0 c11 fitz c12 cj S0 sendKB sendA senda sendM'}, {'v': 'negn y1 au tL ra Lx0 x0 Lx1 bl2 sW tW Lx2 aW sB kn rb2 sO ym off bl sK d0 d2 d1 ks0 ks1 ki kt1 ktb kt0 eK ek eq prod d3 l1 kb cl r3 fit0 tz fit1 div0 div1 cum +rb ui am h0 dm Du nm zn dvl Km t1 keep an ms0 ms1 b3 hz b4 so X4 thn X3 X2 X1', 'a': 'y0 y2 G x1 x3 x2 a1 a0 a2 a4 a3 a5 a7 a6 r0 r1 y3 r2 ab12 ab5 ab10 ab4 zz ab0 ab6 ab8 ab3 ab9 ab2 ab13 ab7 ab1 ab11 At sg2 sg1 sg0 q Kp xk bm Dm +offf', 'p': 'pW0 pW1 pb2 ps1 ps0 ps2 pbl ps4 ps3 pT0 ps5 ps7 ps6 pT1 pT2 pT3 pK0 pT4 pT5 pT6 pT7 pK1 pD0 pk pl pD1 pcr pc pD2 pE3 pD3 pn0 pc2 pn1 pu pH pP pdl pa0 pv0 pa1 pv1 ph +poff', 'g': 'sendKB sendA senda sendM'}, {'v': 'y1 au negn ra tL x1 sW bl2 Lx0 rb2 Lx2 tW Lx1 aW x2 kn sB sO ym off sK d1 d0 d3 ks0 ks1 ki kt1 ktb d2 r3 kt0 eq bl prod fit1 ek fit0 div1 l1 div0 cum At cl kb tz Du Kp bm keep h0 hz ms1 dvl ms0 Km b3 b4 ui so X4 am X3 dm X2 +negn +tL X1 +Lx1 +Lx2 +Lx0 t1 +sB +sW an +tW +aW +kn zn +sK', 'a': 'y3 y0 G x0 x3 a1 a0 a2 a4 a3 a5 y2 a7 a6 r0 r1 eK r2 xk sg1 sg0 sg2 ab9 ab6 ab12 ab11 ab7 ab0 ab8 ab10 ab13 ab5 ab3 ab1 ab4 ab2 Dm zz +G st4 +ybf +st5', 'p': 'pb2 pW0 pW1 ps0 ps1 ps2 ps4 ps3 ps5 pT0 pT1 ps7 pT2 pT4 pT5 ps6 pT3 pbl pK0 pT6 pT7 pK1 pD0 pE3 pD1 pk pD3 pD2 pn1 pcr pl pn0 pc pH pc2 pdl ph pa1 pv1 pa0 pv0 pu +pW0 pP +pW1 +pbl', 'g': 'sendA sendM'}]
_old1 = [
    {"v": "cq0 cq1 pj2 pj1 pj0 col BO r64 BOh Z I au ex bl SW mT WT bh bo rq bt1 Sw K0 bt0 ra rpm rb Ih x1 y1 off kr kc0 y3 r16 cq2 d1 thr af d0 d3 r65 r3 cq3 Dq0 d2 ks0 ks1 ki rq0 Zh kt0 kt1 sb ktb fit1 jd eK ek eq jc prod pj3 fit0 l1 thf xk cl Dq1 tz div1 kb div0 cum At RQ wq +rb ui Wq3 q am dm dvl nm t1 h0 an zn Du ms0 ms1 Km b3 keep b4 hz so X4 X3 X2 Wq1 X1 Wq2",
     "a": "ld4 ld3 lq B8 lc l16l Zn In ld5 b0 x0 y0 x2 a1 x3 a2 a0 y2 a4 a3 a5 a7 a6 r0 r1 Dq2 r2 I5 Ib p32 Dq3 Zq Zw zz ab7 ab2 ab13 ab9 ab10 ab3 ab8 ab4 ab0 ab6 ab1 ab12 dmp ab11 ab5 sg0 sg1 sg2 bm Dm Kp Wq0 +offf thn",
     "p": "pb0 ps1 poff ps0 ps2 ps5 ps4 pT0 ps3 ps7 ps6 pT1 pT2 pT3 pT4 pT5 pK0 pT6 pT7 pK1 pE3 pD3 pD0 pD1 pk pn1 pD2 pl pc pn0 pcr pu pdl pH pP pa0 pv0 pa1 pv1 ph +poff",
     "g": "pi PP cb fitz ci mc l16 KB0 X0 sendKB ld6 S0 one c11 zr c12 dm0 sendA cj senda sendM"},
    {"v": "negn y2 au tL ra x0 sW Lx1 tW Lx2 aW Lx0 bl2 kn rb2 sO y1 sB off ym sK d0 d1 ks1 ks0 ki kt1 bl kt0 ktb d2 eq prod d3 kb cl r3 fit0 ek tz fit1 l1 div0 div1 cum At +rb ui am dm dvl t1 Du h0 an zn Km keep ms1 ms0 b3 nm hz b4 so X4 X3 X2 X1",
     "a": "y0 x1 G x2 x3 a1 a0 a2 a4 a3 a5 a7 a6 r0 r1 eK y3 r2 ab6 ab1 ab10 ab5 ab9 ab4 ab13 ab8 ab7 ab2 zz ab11 sg2 ab12 sg1 sg0 ab0 ab3 Kp xk Dm bm q thn +offf",
     "p": "pW0 pW1 pb2 ps1 ps2 ps0 ps4 ps3 pT0 ps5 ps7 ps6 pT4 pT1 pT2 pT5 pT6 pT7 pT3 pK1 pK0 pbl pD0 pk pD1 pc pcr pD2 pE3 pD3 pl pn0 pn1 pu pdl pH pP pa1 pv1 pa0 pv0 ph +poff",
     "g": "sendKB sendA senda sendM"},
    {"v": "negn y3 au tL ra Lx1 y0 bl2 Lx0 Lx2 sW tW rb2 aW x3 sB kn ym sO off sK d0 d3 bl r3 d1 d2 ks0 fit1 ks1 ki kt1 ktb fit0 div1 eq div0 prod cum At kt0 ek kb cl Du Kp bm keep Km tz l1 h0 dvl ms1 ms0 b3 b4 hz so X4 X3 ui X2 +negn X1 +tL am +Lx0 +Lx1 +Lx2 dm +sB +sW t1 +tW an +aW zn +kn +sK",
     "a": "y1 G x0 x1 x2 a2 a0 a1 y2 a3 a4 a5 r0 a7 a6 r1 r2 eK sg1 sg2 sg0 ab13 ab12 ab7 ab3 ab9 ab11 ab6 ab10 ab8 ab2 ab4 ab1 ab0 +G ab5 xk zz Dm st4 +ybf +st5",
     "p": "pb2 pW0 pW1 ps2 ps0 ps1 ps3 ps4 ps5 pT0 pbl ps6 pT1 ps7 pE3 pD3 pT4 pT2 pT3 pK0 pD0 pT5 pT6 pT7 pK1 pn1 pD1 pD2 pk pn0 pc pcr pH pdl pl pa1 pv1 pa0 pv0 ph pu pP +pW0 +pW1 +pbl",
     "g": "sendA sendM"},
]
_C = {}


def _mask(es):
    m = 0
    for e in es:
        m |= 1 << e
    return m


def _pow2(n):
    k = 1
    while 2 * k <= n:
        k *= 2
    return k


def _deal(topo, src, dsts):
    on = [d for d in dsts if d in topo.cores_of(src)]
    out_ = [d for d in dsts if d not in on]
    used = topo.engines(src, out_[0]) if out_ else []
    free = [e for e in topo.engines(src, on[0]) if e not in used] if on else []
    res, i, j = [], 0, 0
    for d in dsts:
        if d in on:
            k = _pow2(len(free) // len(on))
            res.append(free[i:i + k])
            i += k
        else:
            k = _pow2(len(used) // len(out_))
            res.append(used[j:j + k])
            j += k
    return res


def _traffic(T, topo):
    calls, arrive = {}, {}

    def call(src, msg, t, items):
        es = _deal(topo, src, [i[2] for i in items])
        items = [i + (e,) for i, e in zip(items, es)]
        calls.setdefault(src, []).append((msg, t, items))
        for i in items:
            arrive[(i[2], i[3])] = arrive.get((i[2], i[3]), 0) + len(i[4])

    def pair(c, msg, t, items):
        call(c, msg, t, [(s, d, to if topo.may_write(c, to) else port, sem) for s, d, to, sem, port in items])
        for s, d, to, sem, port in items:
            if not topo.may_write(c, to):
                call(port, msg, t, [(d, d, to, sem)])

    for r, c in enumerate(T.cores):
        far = [d for d in T.cores if not topo.may_write(c, d)]
        ports = [x for x in topo.cores_of(c) if x != c and all(topo.may_write(x, d) for d in far)]
        ports.sort(key=lambda x: topo.die(x) != topo.die(c))
        near = [d for d in T.cores if d != c and d not in far]
        fan = {x: [] for x in ports}
        for i, d in enumerate(far):
            fan[ports[i % len(ports)]].append(d)
        for i, d in enumerate(near):
            fan[ports[-1 - i % len(ports)]].append(d)
        nx = T.cores[(r + 1) % N]
        for t in range(ST):
            last = t == ST - 1
            for msg in SENDS:
                if msg == "KB" and not last:
                    o, p, u = 2 * KW * t, 2 * KW * (t + 1), 14 * (ST - 1 - t)
                    pair(c, "KB", t, [(("KB", o, o + L), ("KB", p, p + L), nx, "KB%d" % t, ports[2]),
                                      (("KB", o + KW, o + KW + L), ("KB", p + KW, p + KW + L), nx, "KB%d" % t, ports[3])])
                if msg == "A":
                    av = ("At", 32 * t + 4 * r, 32 * t + 4 * r + 1)
                    call(c, "A", t, [(av, av, x, "A%d" % t) for x in ports])
                    for x in ports:
                        call(x, "A", t, [(av, av, d, "A%d" % t) for d in fan[x]])
                if msg == "a" and not last:
                    u = 14 * (ST - 1 - t)
                    pair(c, "a", t, [(("fa", u, u + 112), ("al", 112 * t + 112, 112 * t + 224), nx, "a%d" % t, ports[2]),
                                     (("zs_", L * t, L * t + L), ("zl", L * t + L, L * t + 2 * L), nx, "z%d" % t, ports[3])])
                if msg == "M":
                    mate = T.cores[(r - Q + (0 if last else 1)) % N]
                    items = [(("M", MW * t + 96, MW * t + 96 + MS), ("MQ", 112 * t, 112 * t + MS), mate, "MQ%d" % t, ports[1])]
                    if not last:
                        items.append((("M", MW * t, MW * t + MS), ("MP", 112 * t, 112 * t + MS), nx, "MP%d" % t, ports[0]))
                    pair(c, "M", t, items)
    return calls, arrive


def rank_program(g, core, T, topo):
    if "traffic" not in _C:
        _C["traffic"] = _traffic(T, topo)
    calls, arrive = _C["traffic"]
    if core not in calls:
        return
    mine = calls[core]
    rank = T.rank_of(core)

    def ap(v):
        if v[0] == "ind":
            return ap(v[1]).indirect(ap(v[2]))
        if len(v) == 5:
            return T[v[0]][0:v[4], v[1]:v[2]:v[3]]
        if len(v) == 4:
            return T[v[0]][:, v[1]:v[2]:v[3]]
        return T[v[0]][:, v[1]:v[2]]

    sent = [0]

    def fused(items):
        trs = []
        for s, d, to, sem, es in items:
            rid, pid = topo.addr(to, core)
            trs.append(RemoteDMATransfer(dst_ids=[DstId(rid=rid, pnc=pid)], dma_engine_mask=_mask(es), remote_sem=T.sem[sem],
                                         src=ap(s), dst=ap(d)))
            sent[0] += len(es)
        g.remote_dma_fused(trs, local_sem=T.sem.ls)

    if rank is None:
        for msg, t, items in mine:
            g.wait_ge(T.sem[items[0][3]], arrive[(core, items[0][3])])
            fused(items)
        g.wait_ge(T.sem.ls, sent[0])
        return

    Qs = {"v": g.vector, "a": g.scalar, "p": g.tensor, "g": g, "s": g.sync}
    nodes, acc, rnd = [], {}, [0]

    def node(name, kind, alt, outs, ins, more=(), **kw):
        rd, wr = [], []
        for v in ins:
            rd += [v[1], v[2]] if v[0] == "ind" else [v]
        for v in outs:
            if v[0] == "ind":
                wr.append(v[1])
                rd.append(v[2])
            else:
                wr.append(v)
        e = list(alt)[0]
        deps = set(more)
        for vs, w in ((rd, False), (wr, True)):
            for v in vs:
                for lo, hi, w0, e0, j in acc.get(v[0], []):
                    if ((w or w0) and lo < v[2] and v[1] < hi) or (v[0] in _P and (e0 != e or e == "p")):
                        deps.add(j)
        i = len(nodes)
        for v in wr:
            acc[v[0]] = [] if v[0] in _P and e == "p" else [a for a in acc.get(v[0], []) if not (len(v) == 3 and v[1] <= a[0] and a[1] <= v[2])]
        for vs, w in ((rd, False), (wr, True)):
            for v in vs:
                acc.setdefault(v[0], []).append((v[1], v[2], w, e, i))
        nodes.append(dict(kind=kind, alt=alt, deps=sorted(deps), key=(rnd[0], name), **kw))
        return i

    def aps(*xs):
        return [x for x in xs if isinstance(x, tuple)]

    def val(x):
        return ap(x) if isinstance(x, tuple) else x

    def vec(name, fn, out, big, small=()):
        node(name, "c", {"v": [fn]}, [out], big + aps(*small))

    def cp(name, out, in_):
        vec(name, lambda: g.vector.tensor_copy(ap(out), ap(in_)), out, [in_])

    def tt(name, out, a, b, o):
        vec(name, lambda: g.vector.tensor_tensor(ap(out), ap(a), ap(b), o), out, [a, b])

    def ts(name, out, a, s1, o0, s2=None, o1=None):
        if o1 is None:
            vec(name, lambda: g.vector.tensor_scalar(ap(out), ap(a), val(s1), None, o0), out, [a], [s1])
        else:
            vec(name, lambda: g.vector.tensor_scalar(ap(out), ap(a), val(s1), val(s2), o0, o1), out, [a], [s1, s2])

    def scan(name, out, d0, d1, o0, o1):
        vec(name, lambda: g.vector.tensor_tensor_scan(ap(out), ap(d0), ap(d1), 0.0, o0, o1), out, [d0, d1])

    def mset(name, out, c):
        vec(name, lambda: g.vector.memset(ap(out), c), out, [])

    def act(name, out, in_, f, bias=0.0, scale=1.0, accum=None):
        if accum is None:
            fn = lambda: g.scalar.activation(ap(out), ap(in_), f, bias=val(bias), scale=val(scale))
        else:
            fn = lambda: g.scalar.activation(ap(out), ap(in_), f, bias=val(bias), scale=val(scale), accum_out=ap(accum))
        node(name, "c", {"a": [fn]}, [out] + aps(accum), [in_] + aps(bias, scale))

    def mov(name, out, in_):
        node(name, "c", {"a": [lambda: g.scalar.activation(ap(out), ap(in_), AF.Copy)],
                         "v": [lambda: g.vector.tensor_copy(ap(out), ap(in_))]}, [out], [in_])

    def lin(name, out, in_, scale, bias):
        node(name, "c", {"a": [lambda: g.scalar.activation(ap(out), ap(in_), AF.Identity, bias=val(bias), scale=val(scale))],
                         "v": [lambda: g.vector.tensor_scalar(ap(out), ap(in_), val(scale), val(bias), AL.mult, AL.add)]},
             [out], [in_] + aps(bias, scale))

    def mms(name, ms):
        def one(m):
            return lambda: g.tensor.matmul(ap(m[0]), ap(m[1]), ap(m[2]), m[3], m[4])
        node(name, "c", {"p": [one(m) for m in ms]}, [m[0] for m in ms], [m[1] for m in ms] + [m[2] for m in ms])

    def total(name, out, terms, start=True, stop=True):
        mms(name, [(out, a, b, start and i == 0, stop and i == len(terms) - 1) for i, (a, b) in enumerate(terms)])

    def iota(name, out, pattern, base, cm):
        if _S[out[0]][1] == I32:
            fn = lambda: g.iota(ap(out), pattern, base, cm)
        else:
            fn = lambda: g.iota(ap(out), pattern, base, cm, allow_small_or_imprecise_dtypes=True)
        node(name, "c", {"g": [fn]}, [out], [])

    def load(e, sem, dst, src, slow=False):
        if slow:
            fn = lambda: Qs[e].dma_start(ap(dst), src, allow_slow_non_contiguous=True)
        else:
            fn = lambda: Qs[e].dma_start(ap(dst), src)
        node(sem, "dma", {e: fn}, [dst], [], sem=sem)

    def store(e, sem, dst, src):
        node(sem, "dma", {e: lambda: Qs[e].dma_start(dst, ap(src))}, [], [src], sem=sem)

    def send(msg, t, lands):
        items = [i for m, u, i in mine if m == msg and u == t][0]
        i = node("send" + msg, "send", {"g": lambda: fused(items)}, [], [x[0] for x in items])
        for sem, views in lands:
            node("land" + sem[:-1], "land", {"r": None}, views, [], more=[i], sem=sem)

    def ind(win, offs):
        return ("ind", win, offs)

    def rows(zmat, src, o, n=L):
        return [((zmat, 15 - r, 143 - r), (src, o + r, o + n, 16)) for r in range(16)]

    share = {"nm": ("q", 1, 2), "thf": ("thr", 1, 2), "negn": ("tL", 3, 4)}
    C = lambda name, i: share.get(name, (name, i, i + 1))
    I_, In, Ih, Ib, BO = ("I", 0, 128), ("In", 0, 128), ("Ih", 0, 128), ("Ib", 0, 128), ("BO", 0, 128)
    GP, RR, SW, PP, WT = [C("col", i) for i in range(5)]
    RQ = C("p32", 1)
    Xw, RP = ("X", 0, V), ("rpt", 0, R)
    ci = lambda a, b: ("fa", 56 + a, 56 + b)
    ex = lambda a, b: ("ub", 56 + a, 56 + b)
    an = lambda t: ("fa", 14 * (ST - 1 - t), 14 * (ST - t))
    bl = lambda t: ("ub", 14 * (ST - 1 - t), 14 * (ST - t))

    load("s", "ld0", ("avi", 0, 14), T.av[:])
    load("s", "ld1", RP, T.rp[:])
    load("s", "ld2", Xw, T.ph[:])
    load("a", "ld3", ("bvi", 0, 14), T.bv[:])
    load("a", "ld4", ("kci", 0, L), T.kc[:])
    load("a", "ld5", ("zl", 0, L), T.zs[:])
    load("g", "ld6", ("thi", 0, 1), T.th[:], True)
    iota("pi", ("pi", 0, 1), [[0, 1]], 0, 1)
    iota("PP", PP, [[0, 1]], 0, 1)
    iota("ci", ci(0, L), [[1, L]], 0, 0)
    iota("cb", ("cb", 0, 128), [[16, 8], [0, 16]], 0, 0)
    iota("mc", ("mc", 0, 256), [[0, 16], [1, 16]], 0, 0)
    iota("l16", ("l16", 0, L), [[16, L]], 0, 0)
    iota("cj", ("cj", 0, 48), [[16, 48]], 0, 0)
    iota("one", ("one", 0, L), [[0, L]], 1, 0)
    iota("zr", ("zr", 0, 8), [[0, 8]], 0, 0)
    iota("c11", ("c11", 0, 14), [[0, 14]], V // 2, 0)
    iota("S0", C("S", 3), [[0, 1]], 0, 0)
    iota("fitz", C("fit", L), [[0, 1]], 0, 0)
    iota("KB0", ("KB", L, ST * 2 * KW, KW), [[0, 2 * ST]], 0, 0)
    iota("X0", ("X", V, V + 64), [[0, 64]], 0, 0)
    iota("c12", ("c11", 16, 30), [[0, 14]], int(SHIFT), 0)
    mset("r64", ("r64", 0, 448), 2.0 ** 30)
    mset("r65", ("r64", 0, 448, 64), -2.0 ** 30)
    lin("r6b", ("r6b", 0, 448), ("r64", 0, 448), -1.0, 0.0)
    ts("pj0", C("pj", 0), C("pi", 0), 112, AL.bitwise_and)
    ts("pj1", C("pj", 1), C("pi", 0), 15, AL.bitwise_and)
    ts("pj2", C("pj", 2), C("pi", 0), 1, AL.bitwise_and)
    ts("pj3", C("pj", 3), C("pi", 0), 12, AL.bitwise_and)
    cp("col", ("col", 0, 2), ("pj", 0, 2))
    ts("SW", SW, C("pj", 2), -2.0, AL.mult, 1.0, AL.add)
    ts("WT", WT, C("pj", 1), 2.0, AL.mult, 1.0, AL.add)
    ts("RQ", RQ, C("pj", 3), 0.25, AL.mult)
    ts("I", I_, ci(0, 128), PP, AL.is_equal)
    lin("In", In, I_, -1.0, 0.0)
    lin("Ih", Ih, I_, 0.5, 0.0)
    lin("I5", ("I5", 0, 128), I_, 5.0, 0.0)
    ts("Sw", ("Sw", 0, 128), ci(0, 128), PP, AL.subtract, SW, AL.is_equal)
    ts("Z", ("Z", 0, 144), ci(0, 144), GP, AL.subtract, 15.0, AL.is_equal)
    ts("BO", BO, ("cb", 0, 128), GP, AL.is_equal)
    lin("B8", ("B8", 0, 8), ("BO", 0, 128, 16), 256.0, 0.0)
    lin("B9", ("B8", 8, 16), ("BO", 0, 128, 16), -256.0, 0.0)
    lin("B10", ("B8", 16, 24), ("BO", 0, 128, 16), 512.0, 0.0)
    lin("Zn", ("Zn", 0, 144), ("Z", 0, 144), -1.0, 0.0)
    lin("Ib", Ib, I_, -4 * SHIFT, 0.0)
    lin("Zq", ("Zq", 0, 144), ("Z", 0, 144), 1.0 / 16, 0.0)
    cp("Zh", ("Zh", 0, 144), ("Z", 0, 144))
    cp("BOh", ("BOh", 0, 128), BO)
    cp("Ig", ("Ig", 0, 128), I_)
    lin("Zw", ("Zw", 0, 144), ("Z", 0, 144), WT, 0.0)
    lin("lq", ("lq", 0, L), ci(0, L), 1.0 / 128, 0.0)
    cp("ex", ex(0, L), ci(0, L))
    ts("mT", ("mT", 0, 256), ("mc", 0, 256), RR, AL.is_equal)
    ts("r16", ("r16", 0, 128), ("mc", 0, 128), 0.0, AL.is_equal, float(2 ** 24), AL.mult)
    ts("kr", ("kr", 0, 128), ("one", 0, 128), RR, AL.mult, 16.0, AL.mult)
    lin("lc", ("lc", 0, 14), ci(0, 14), 16.0, RR)
    cp("thr", C("thr", 0), C("thi", 0))
    ts("thf", C("thf", 0), C("thi", 0), 15.5, AL.add)
    lin("l16l", ("l16l", 0, 14), ("lc", 0, 14), 16.0, 0.0)
    lin("sb", ("sb", 0, 3), ("lc", 0, 3), BIG, BIG / 2)
    lin("jc", ("jc", 0, 3), ("lc", 0, 3), 1.0, -14.5)
    lin("jd", ("jd", 0, 3), ("lc", 0, 3), 2.0, float(L))
    lin("kc0", ("kc0", 0, 14), ("lc", 0, 14), -1.0 / 128, V // 2 - SHIFT + 0.25)
    iota("dm0", ("dmp", 16, 32), [[0, 4], [16, 4]], V - int(SHIFT), 0)
    lin("dmp", ("dmp", 0, 16), ("dmp", 16, 32), 1.0, RR)
    act("p32", C("p32", 0), RR, AF.Exp, scale=LN32)
    ts("wq", ("wq", 0, 4), ci(0, 4), RQ, AL.is_equal, C("p32", 0), AL.mult)
    mset("rq", ("rq", 0, 192), 1.0)
    mset("rq0", ("rq", 0, 192, 4), 0.0)
    for q in range(4):
        lin("Wq%d" % q, ("Wq", 128 * q, 128 * q + 128), BO, C("wq", q), 0.0)
        lin("Dq%d" % q, ("Dq", 128 * q, 128 * q + 128), I_, 2.0 ** (20 + 20 * q), 0.0)
        mset("cq%d" % q, ("cq", q, 192, 4), (0.5 - 4 * q) * 2.0 ** (20 + 20 * q))
    cp("au", ("au", 0, 14), ("avi", 0, 14))
    cp("af", ("al", 0, 14), ("avi", 0, 14))
    cp("bl", bl(0), ("bvi", 0, 14))
    cp("K0", ("KB", 0, L), ("kci", 0, L))
    ts("rpm", ("rpm", 0, R), RP, -float(V // 2), AL.add)
    ts("bh", ("bh", 0, 14), ("bvi", 0, 14), 992, AL.bitwise_and)
    ts("bo", ("bh", 16, 30), ("bvi", 0, 14), 31, AL.bitwise_and)
    tt("bt0", ("bt", 0, L), ind(("bh", 0, 14), ex(0, 14)), ("mT", 0, L), AL.mult)
    tt("bt1", ("bt", L, 2 * L), ind(("bh", 16, 30), ex(0, 14)), ("mT", 0, L), AL.mult)
    total("pb0", ("H", 0, L), [(I_, ("bt", 0, L)), (("Sw", 0, 128), ("bt", L, 2 * L))])
    act("b0", ("KB", KW, KW + L), ("H", 0, L), AF.Copy)

    ch = lambda name, c: (name, 16 * CUT[c], 16 * CUT[c + 1])
    lc = lambda name, c: (name, CUT[c], CUT[c + 1])
    Lx = ("Lx", 0, 3)

    def early(t):
        ko = 2 * KW * t
        if t > 0:
            total("pbl", ("H", 256, 270), rows("Z", "KB", ko + KW))
            cp("bl", bl(t), ("H", 256, 270))
        cp("rb", ("rb", 0, L), ind(RP, bl(t)))
        mov("rbf", ("rbf", 0, L), ind(("rpm", 0, R), bl(t)))
        total("poff", ("H", 0, L), [(I_, ("l16", 0, L)), (I_, ("KB", ko, ko + L))])
        if t == 0:
            cp("off", ("off", 0, L), ("H", 0, L))
        else:
            act("offf", ("offf", 0, L), ("H", 0, L), AF.Identity, bias=768.0)

    def merge(t, ko, mp, mo, final):
        qo = 112 * t
        Km, keep, Kq, bq = (mp, mo + 4, mo + 52), (mp, mo + 52, mo + 100), ("MQ", qo + 4, qo + 52), ("MQ", qo + 52, qo + 100)
        if not final:
            total("pb2", ("M2", 32, 35), rows("Z", "MQ", qo + 52, 48))
            cp("bl2", ("bl2", 0, 3), ("M2", 32, 35))
            cp("rb2", ("rb2", 0, 48), ind(RP, ("bl2", 0, 3)))
            mov("ym", ("yg", 0, 768), ind(Xw, ("rb2", 0, 48)))
        node("negn", "c", {"v": [lambda: g.vector.tensor_reduce(ap(C("negn", 0)), ap(("At", 32 * t, 32 * t + 32, 4)), AX.X, AL.min, negate=True)]},
             [C("negn", 0)], [("At", 32 * t, 32 * t + 32)])
        ts("tL", ("tL", 0, 3), ("jc", 0, 3), C("negn", 0), AL.add, 1000.0, AL.mult)
        for s in range(3):
            ts("Lx%d" % s, C("Lx", s), C("tL", s), C("jd", s), AL.min, C(mp, mo + s), AL.max)
        act("G", ("G", 0, 48), Km, AF.Exp, scale=-LN32)
        mms("pW0", [(("H", 0, 192), I_, ("cq", 0, 192), True, False)]
            + [(("H", q, 192, 4), ("Dq", 128 * q, 128 * q + 128), Km, False, False) for q in range(4)])
        mms("pW1", [(("H", q, 192, 4), ("Wq", 128 * q, 128 * q + 128), Kq, False, q == 3) for q in range(4)])
        scan("sW", ("sW", 0, 192), ("rq", 0, 192), ("H", 0, 192), AL.mult, AL.max)
        tt("tW", ("tW", 0, 48), ("sW", 3, 192, 4), ("G", 0, 48), AL.mult)
        ts("aW", ("aW", 0, 48), ("tW", 0, 48), 15, AL.bitwise_and)
        tt("kn", ("kn", 0, 48), ("aW", 0, 48), keep, AL.add)
        if not final:
            tt("sO", ind(("offf", 0, KW), Lx), ("kn", 0, 48), ("cj", 0, 48), AL.add)
            cp("off", ("off", 0, L), ("offf", 0, L))
        cp("sK", ind(("KB", ko, ko + KW), Lx), ("kn", 0, 48))
        cp("sB", ind(("KB", ko + KW, ko + 2 * KW), Lx), bq)
        if final:
            total("pbl", ("M2", 16, 30), rows("Z", "KB", ko + KW))
            act("ybf", ("ybf", 0, 14), ("M2", 16, 30), AF.Copy)
            store("s", "st0", T.yb[:], ("ybf", 0, 14))
            store("a", "st5", T.yk[:], ("KB", ko, ko + L))
        else:
            mov("rb2f", ("rb2f", 0, 48), ind(("rpm", 0, R), ("bl2", 0, 3)))
            cp("sR", ind(("rbf", 0, KW), Lx), ("rb2f", 0, 48))

    early(0)
    for t in range(ST):
        last = t == ST - 1
        rnd[0] = t
        ko, mo, p = 2 * KW * t, MW * t, 2 * KW * (t + 1)
        K_, z_, a_ = ("KB", ko, ko + L), ("zl", L * t, L * t + L), ("al", 112 * t, 112 * t + 14)
        for c in range(CH):
            mov("y%d" % c, ("yg", 768 + 16 * CUT[c], 768 + 16 * CUT[c + 1]), ind(Xw, lc("rb", c)))
        if t > 0:
            cp("au", ("au", 0, 14), a_)
        cp("ra", ("ra", 0, L), ind(RP, ("au", 0, 14)))
        for c in range(CH):
            mov("x%d" % c, ch("xg", c), ind(Xw, lc("ra", c)))
        if t > 0:
            merge(t - 1, ko, "MP", 112 * (t - 1), False)
        if not last:
            send("KB", t, [("KB%d" % t, [("KB", p, p + L), ("KB", p + KW, p + KW + L)])])

        for h, (l0, n) in enumerate(((0, 128), (128, L - 128))):
            Th = "T%d" % h
            for i in range(4):
                bank, o, m = "A%d" % ((4 * h + i) % 3), 16 * l0 + 4 * n * i, 4 * h + i
                if h in VMAX[ROUND[t]]:
                    xk_ = [("xg", 16 * l0 + 4 * i + j, 16 * (l0 + n), 16) for j in range(4)]
                    if i == 0:
                        total("pz%d" % h, ("DD", 256, 256 + n), [(I_, ("zl", L * t + l0, L * t + l0 + n))])
                    node("a%d" % m, "c", {"v": [(lambda j=j, o=o, n=n, x=xk_[j]: g.vector.tensor_tensor(
                        ap(("a2", o + n * j, o + n * j + n)), ap(x), ap(("DD", 256, 256 + n)), AL.max)) for j in range(4)]},
                        [("a2", o, o + 4 * n)], xk_ + [("DD", 256, 256 + n)])
                    mms("ps%d" % m, ([((Th, 0, 128), ("kr", 0, 128), I_, True, False)] if i == 0 else [])
                        + [((Th, 4 * i + j, 128, 16, n), xk_[j], ("B8", 8, 16), False, False) for j in range(4)])
                    mms("pT%d" % m, [((Th, 4 * i + j, 128, 16, n), ("a2", o + n * j, o + n * j + n), ("B8", 16, 24), False, False) for j in range(4)])
                    continue
                bank = "A%d" % (m % 3)
                mms("ps%d" % m, [((bank, n * j, n * j + n), a, b, s, not s) for j in range(4)
                                 for a, b, s in ((I_, ("xg", 16 * l0 + 4 * i + j, 16 * (l0 + n), 16), True), (In, ("zl", L * t + l0, L * t + l0 + n), False))])
                act("a%d" % m, ("a2", o, o + 4 * n), (bank, 0, 4 * n), AF.Abs)
                mms("pT%d" % m, ([((Th, 0, 128), ("kr", 0, 128), I_, True, False)] if i == 0 else [])
                    + [((Th, 4 * i + j, 128, 16, n), ("a2", o + n * j, o + n * j + n), ("B8", 0, 8), False, False) for j in range(4)])
            mms("pK%d" % h, [((Th, 0, 128, 1, n), ("KB", ko + l0, ko + l0 + n), I_, False, n == 128)]
                + ([((Th, 0, 128, 16), I_, ("zr", 0, 8), False, True)] if n < 128 else []))
            scan("ks%d" % h, ("ks", 128 * h, 128 * h + 128), ("r16", 0, 128), (Th, 0, 128), AL.max, AL.min)
        for c in range(CH):
            yw = ("yg", 768 if t == 0 else 0, 768 + 16 * CUT[c + 1])
            bank, relu = "H" if c == CH - 1 else "DD", c in RELU[ROUND[t]]
            if c in WACT[ROUND[t]]:
                act("d%d" % c, ch("dg", c), ind(yw, lc("off", c)), AF.Copy)
                mid = 8 * (CUT[c] + CUT[c + 1])
                for h, (p0, p1) in enumerate(((16 * CUT[c], mid), (mid, 16 * CUT[c + 1]))):
                    total("pw%d%d" % (c, h), ("A%d" % h, 0, p1 - p0), [(I_, ("dg", p0, p1)), (In, ("xg", p0, p1))])
                    act("r%d%d" % (c, h), ("dr", p0, p1), ("A%d" % h, 0, p1 - p0), AF.Abs)
            else:
                tt("d%d" % c, ch("dg", c), ind(yw, lc("off", c)), ch("xg", c), AL.subtract)
            if c in WACT[ROUND[t]]:
                pass
            elif relu:
                total("pE%d" % c, lc(bank, c), rows("Zn", "dg", 16 * CUT[c], 16 * (CUT[c + 1] - CUT[c])), stop=False)
                ts("r%d" % c, ch("dr", c), ch("dg", c), 0.0, AL.max, 2.0, AL.mult)
            else:
                act("r%d" % c, ch("dr", c), ch("dg", c), AF.Abs)
            total("pD%d" % c, lc(bank, c), rows("Z", "dr", 16 * CUT[c], 16 * (CUT[c + 1] - CUT[c])), start=not relu)
        for h, (bank, l0, l1) in enumerate((("DD", 0, CUT[-2]), ("H", CUT[-2], L))):
            ts("fit%d" % h, ("fit", l0, l1), (bank, l0, l1), C("thr", 0), AL.is_le, 32.0, AL.mult)
            total("pn%d" % h, (bank, 256 + l0, 256 + l1), [(BO, ("fit", l0, l1))])
            ts("div%d" % h, ("div", l0, l1), (bank, 256 + l0, 256 + l1), 272.0, AL.is_lt, BIG, AL.mult)
        scan("cum", ("cum", 0, L), ("one", 0, L), ("div", 0, L), AL.mult, AL.add)
        cp("ki", ("ki", 0, 16), ("ks", 15, 256, 16))
        ts("kt1", ("kt", 16, 32), ("ki", 0, 16), 15, AL.bitwise_and)
        ts("kt0", ("kt", 0, 16), ("ki", 0, 16), 4, AL.logical_shift_right, 15, AL.bitwise_and)
        tt("eK", ("eK", 0, 256), ind(("kt", 16, 32), ex(0, 16)), ("mc", 0, 256), AL.is_equal)
        tt("ek", ("ek", 0, 256), ind(("kt", 0, 16), ex(0, 16)), ("mT", 0, 256), AL.mult)
        mms("pk", [(("T0", 0, 128), ("eK", 0, 128), I_, True, True), (("T0", 128, L), ("eK", 128, 256), ("I", 0, 96), True, True)])
        mms("pl", [(("T1", 0, 14), I_, ("l16l", 0, 14), True, False), (("T1", 0, 8), ("ek", 0, 128), ("BO", 0, 128, 16), False, False),
                   (("T1", 8, 14), ("ek", 128, 256), ("BO", 0, 96, 16), False, True)])
        tt("prod", ("prod", 0, L), ("T0", 0, L), ("rbf", 0, L), AL.mult)
        cp("l1", ("l1", 0, 14), ("T1", 0, 14))
        mov("xk", ("xk", 0, L), ind(("xg", 0, W), ("l1", 0, 14)))
        clist = [(I_, ("c11", 0, 14)), (In, ("c11", 16, 30))] + rows("Zh", "prod", 0)
        total("pc", ("M2", 0, 14), clist)
        ts("cl", ("cl", 0, 14), ("M2", 0, 14), SHIFT, AL.add)
        tt("kb", ("kb", 0, 14), ("kc0", 0, 14), ("M2", 0, 14), AL.subtract)
        if OPT["C16"]:
            ts("c16", ("c16", 0, 14), ("M2", 0, 14), SHIFT - V // 2, AL.add)
            clist = clist[:2] + [(("Ig", 0, 128), ("c16", 0, 14))]
        if OPT["WK"]:
            mov("tz", ("tz", 0, L), ind(Xw, ("cl", 0, 14)))
            total("ptz", ("T1", 64, 64 + L), [(I_, ("tz", 0, L)), (In, z_)])
            act("zz", ("zz", 0, L), ("T1", 64, 64 + L), AF.Abs)
        else:
            tt("tz", ("tz", 0, L), ind(Xw, ("cl", 0, 14)), z_, AL.subtract)
            act("zz", ("zz", 0, L), ("tz", 0, L), AF.Abs)
        total("pu", ("T1", 0, 14), [(("I5", 0, 128), a_)] + rows("Zw", "zz", 0))
        total("ph", ("M2", 64, 64 + L), [(Ih, ("xk", 0, L)), (Ih, ("tz", 0, L))] + ([] if OPT["WK"] else [(Ih, z_)]))
        ts("hz", ("hz", 0, L), ("M2", 64, 64 + L), -0.25, AL.add)
        cp("ui", ("ui", 0, 14), ("T1", 0, 14))
        ts("am", ("am", 0, 14), ("ui", 0, 14), R - 1, AL.bitwise_and)
        tt("dm", ("dm", 0, 14), a_, ("am", 0, 14), AL.subtract)

        late = LATE[ROUND[t]]
        total("pcr", ("T0", 0, L), [(("BOh", 0, 128), ("prod", 0, L)), (I_, ("lq", 0, L))] + ([(I_, ("div", 0, L))] if late else []))
        wins = [min(64 * (s // 4), L - 64) for s in range(14)]
        for s in range(14):
            act("ab%d" % s, ("ab", 64 * s, 64 * s + 64), ("T0", wins[s], wins[s] + 64), AF.Abs, bias=C("kb", s))
        for h in range(0 if late else 2):
            bank = "A%d" % (h + 1)
            total("pa%d" % h, (bank, 0, 448), [(Ib, ("ab", 448 * h, 448 * h + 448))], stop=False)
            mms("pv%d" % h, [((bank, 64 * s, 64 * s + 64), Ib, ("div", wins[7 * h + s], wins[7 * h + s] + 64), False, s == 6) for s in range(7)])
        total("pc2", ("A0", 0, 14), clist, stop=False)
        total("pdl", ("A0", 0, 14), rows("Zq", "div", 0), start=False)

        total("pH", ("DD", 0, L), [(Ih, z_), (Ih, ("xg", 0, W, 16)), (I_, ("div", 0, L))])
        total("pP", ("T0", 0, L), [(I_, ("zz", 0, L)), (In, ("div", 0, L))])
        ts("h0", ("h0", 0, L), ("DD", 0, L), -BIG - 0.25, AL.add)
        tt("zn", ("zs_", L * t, L * t + L), ("T0", 0, L), ("h0", 0, L), AL.max)
        At = C("At", 32 * t + 4 * rank)
        lin("At", At, C("cum", L - 1), 1.0 / BIG, -15.5)
        for s in range(3):
            act("sg%d" % s, ("sg", L * s, L * s + L), ("cum", 0, L), AF.Sign, bias=C("sb", s), scale=-1.0, accum=C("S", s))
        ts("dvl", ("dvl", 0, 14), ("A0", 0, 14), BIG - SHIFT, AL.is_ge)
        tt("t1", ("t1", 0, 14), ("dvl", 0, 14), ("dm", 0, 14), AL.mult)
        tt("an", an(t), ("t1", 0, 14), ("am", 0, 14), AL.add)
        send("A", t, [("A%d" % t, [C("At", 32 * t + 4 * r) for r in range(N) if r != rank])])
        if last:
            store("s", "st1", T.ya[:], an(t))
            store("s", "st2", T.yz[:], ("zs_", L * t, L * t + L))
        else:
            send("a", t, [("a%d" % t, [("al", 112 * t + 112, 112 * t + 224)]), ("z%d" % t, [("zl", L * t + L, L * t + 2 * L)])])
        Du = ("Du", 0, 3)
        ts("Du", Du, ("S", 0, 3), 0.5, AL.mult, 112.0, AL.add)
        lin("Dm", ("M", mo, mo + 4), ("S", 0, 4), 0.5, 112.0)
        mov("Kp", ("M", mo + 100, mo + 148), ind(("KB", ko, ko + L + 1), Du))
        mov("bm", ("M", mo + 148, mo + 196), ind(("KB", ko + KW, ko + KW + L + 1), Du))
        tt("Km", ("M", mo + 4, mo + 52), ind(("fit", 0, L + 1), Du), ("M", mo + 100, mo + 148), AL.add)
        tt("keep", ("M", mo + 52, mo + 100), ind(("fit", 0, L + 1), Du), ("M", mo + 100, mo + 148), AL.min)
        send("M", t, [("MQ%d" % t, [("MQ", 112 * t, 112 * t + MS)])] + ([] if last else [("MP%d" % t, [("MP", 112 * t, 112 * t + MS)])]))
        if not last:
            lin("q", C("q", 0), At, 1.0, MAGIC)
            ts("nm", C("nm", 0), C("q", 0), MAGIC, AL.subtract, At, AL.subtract)
            lin("thn", C("thr", 0), C("nm", 0), -1.0, C("thf", 0))
            rnd[0] = t + 1
            early(t + 1)
            rnd[0] = t

        if late:
            for h in range(2):
                scan("ms%d" % h, ("msb", 448 * h, 448 * h + 448), ("r6b", 0, 448), ("ab", 448 * h, 448 * h + 448), AL.max, AL.min)
            lin("lose", ("lose", 0, 14), ("msb", 63, 896, 64), -4 * SHIFT, 0.0)
            tt("b3", ("b3", 0, 14), ("lose", 0, 14), ("A0", 0, 14), AL.max)
        else:
            for h in range(2):
                scan("ms%d" % h, ("ms", 448 * h, 448 * h + 448), ("r64", 0, 448), ("A%d" % (h + 1), 0, 448), AL.min, AL.max)
            tt("b3", ("b3", 0, 14), ("ms", 63, 896, 64), ("A0", 0, 14), AL.max)
        tt("b4", ("b4", 0, 14), ("b3", 0, 14), ("dmp", 0, 14), AL.min)
        ts("so", ("so", 0, 14), ("b4", 0, 14), SHIFT, AL.add)
        for s in (12, 8, 4, 0):
            e = min(s + 4, 14)
            cp("X%d" % (s // 4 + 1), ind(("X", 0, V + 64), ("so", s, e)), ("hz", 16 * s, 16 * e))
        if last:
            store("s", "st3", T.yx[:, 0:V // 2], ("X", 0, V // 2))
            store("a", "st4", T.yx[:, V // 2:V], ("X", V // 2, V))
            rnd[0] = ST
            merge(t, ko, "M", mo, True)

    index = {nd["key"]: i for i, nd in enumerate(nodes)}
    lists = {e: [] for e in list(Qs) + ["r"]}
    for i, nd in enumerate(nodes):
        if ORDER is None or nd["kind"] == "land" or list(nd["alt"]) == ["s"]:
            lists[list(nd["alt"])[0]].append(i)
    for t in range(ST if ORDER else 0):
        for e, names in ORDER[ROUND[t]].items():
            lists[e] += [index[(t + 1, x[1:]) if x[0] == "+" else (t, x)] for x in names.split()]
    _C["nodes"], _C["lists"] = nodes, lists
    cnt = {"v": 0, "a": 0, "p": 0, "g": 0}
    know = {e: {} for e in Qs}
    token, clock, queue, owed = {}, {}, {}, {}

    def wait(e, tok):
        if know[e].get(tok[0], 0) < tok[1]:
            Qs[e].wait_ge(T.sem[tok[0]], tok[1])
            for k, n in clock[tok].items():
                know[e][k] = max(know[e].get(k, 0), n)

    def issue(i, e):
        nd = nodes[i]
        queue[i] = e
        if nd["kind"] == "land":
            tok = (nd["sem"], arrive[(core, nd["sem"])])
            clock[tok] = {tok[0]: tok[1]}
        else:
            need = {}
            for d in nd["deps"]:
                if d in token and not (e == queue[d] == "p"):
                    need[token[d][0]] = max(need.get(token[d][0], 0), token[d][1])
            for tok in sorted(need.items(), key=lambda x: -sum(clock[x].values())):
                wait(e, tok)
            if nd["kind"] == "send":
                nd["alt"][e]()
                return
            if nd["kind"] == "dma":
                nd["alt"][e]().then_inc(T.sem[nd["sem"]], 16)
                tok = (nd["sem"], 16)
            else:
                for x in nd["alt"][e][:-1]:
                    x()
                nd["alt"][e][-1]().then_inc(T.sem["c" + e], 1)
                cnt[e] += 1
                tok = ("c" + e, cnt[e])
            clock[tok] = dict(know[e])
            clock[tok][tok[0]] = tok[1]
        token[i] = tok
        owed[tok[0]] = tok[1]

    head = {e: 0 for e in lists}
    while len(queue) < len(nodes):
        go = [e for e in lists if head[e] < len(lists[e]) and all(d in queue for d in nodes[lists[e][head[e]]]["deps"])]
        issue(lists[go[0]][head[go[0]]], go[0])
        head[go[0]] += 1
    g.wait_ge(T.sem.ls, sent[0])
    for tok in owed.items():
        wait("g", tok)
